import numpy as np, ml_dtypes
CORES = [24,25,26,27,28,29,30,31]
N = 8
BF = ml_dtypes.bfloat16
W, R, Q, RO, HOP, E = 3072, 192, 13, 4, 3, 384
def parts(rng):
    v = rng.integers(0, 256, (N, 8, 16, W)); v[..., 1::8] = v[..., 0::8]
    s = 0.15 + 0.85 * rng.random((N, 8, 16, 1)); w = rng.choice(np.array([0.0, 0.1, 0.2]), (N, 8, 1, 1))
    k = np.minimum((W * s * ((1 - w) * rng.random((N, 8, 16, W)) + w * rng.random((N, 8, 1, W))) ** 2).astype(np.int64), W - 1)
    pop = np.argsort(rng.random((8, E)), axis=1)[:, :24] * 8; pop = np.concatenate([pop, pop + 1], axis=1)
    hit = np.take_along_axis(np.broadcast_to(pop, (N, 8, 48)), rng.integers(0, 48, (N, 8, 16 * R)), 2).reshape(N, 8, 16, R)
    p = np.where(rng.random((N, 8, 16, R)) < 0.3, hit, rng.integers(0, W, (N, 8, 16, R)))
    return v, k, p
def look(rng, v, p):
    o = np.take_along_axis(p, rng.integers(0, 16, (N, 8, 1, R)), 2); y = np.take_along_axis(v, o, 3)
    near = np.clip(y + rng.integers(-3, 4, y.shape) * (rng.random(y.shape) < 0.5), 0, 255)
    return np.where(rng.random((N, 8, 1, R)) < 0.75, near, rng.integers(0, 256, y.shape))
def pack(v, k, p, y):
    return {"val": np.ascontiguousarray(v.reshape(N, 128, W)).astype(np.float32).astype(BF), "clk": np.ascontiguousarray(k.reshape(N, 128, W)).astype(np.int32),
            "nam": np.ascontiguousarray(p.reshape(N, 128, R)).astype(np.int32), "seen": np.ascontiguousarray(y.reshape(N, 128, R)).astype(np.float32).astype(BF)}
def setup_inputs(rng):
    v, k, p = parts(rng)
    return pack(v, k, p, look(rng, v, p))
def setup_inputs_count(rng):
    v, k, p = parts(rng); A = W // 4; q = rng.permutation(N)
    v[q[:2]] = rng.integers(0, 256, (2, 8, 16, W)); z = rng.random((N, 8, W))
    for g in (1, 3, 5, 7):
        s = int(rng.integers(0, W - R + 1)); z[q[0], g, s:s + R] -= 1
    b = rng.integers(W // 4, W // 2, (N, 8, 16, 1)); m = np.argsort(z, axis=2); pos = np.argsort(m, axis=2)[:, :, None, :]
    n = np.where(pos < A, 16, np.where(pos < 3 * A, Q - 1, Q)); at = np.argsort(rng.random((N, 8, 16, W)), axis=2) < n
    up = (pos >= A) * rng.choice(np.array([0, 0, 1, 5]), (N, 8, 16, W))
    k = np.where(at, b + up, b - rng.integers(1, W // 8, (N, 8, 16, W)))
    def pick(lo, hi, c): return np.take_along_axis(m, rng.integers(lo, hi, (N, 8, c * R)), 2).reshape(N, 8, c, R)
    o = pick(0, A, 1); o[q[0]] = m[q[0], :, None, :R]; i = np.arange(16)[None, None, :, None]
    k0 = rng.integers(0, 16, (N, 8, 1, R)); k1 = (k0 + rng.integers(1, 16, (N, 8, 1, R))) & 15; k2 = (k0 + rng.integers(1, 16, (N, 8, 1, R))) & 15
    h = rng.integers(0, 3, (N, 8, 1, R)); h[q[0]] = 0; h[q[1]] = rng.integers(1, 3, (8, 1, R))
    p = np.where(i == k0, o, np.where(((i == k1) & (h > 0)) | ((i == k2) & (h > 1)), pick(3 * A, W, 16), pick(A, 3 * A, 16)))
    return pack(v, k, p, np.take_along_axis(v, o, 3))
def setup_inputs_crowd(rng):
    v, k, p = parts(rng); c = np.argsort(rng.random((N, 8, W)), axis=2)[..., :3]; top = np.max(k, axis=3)
    np.put_along_axis(k, np.ascontiguousarray(np.broadcast_to(c[:, :, None, :], (N, 8, 16, 3))), np.stack([top - (top >> 3), top - (top >> 4), top], axis=3), 3)
    r = np.arange(R)[None, None, None, :]; g = np.arange(8)[None, :, None, None]; i = np.arange(16)[None, None, :, None]
    star = np.where((g % 2 == 0) & (r % 2 == 1), c[:, :, None, 1:2], c[:, :, None, 0:1])
    k0 = rng.integers(0, 16, (N, 8, 1, R)); no = (r < 2) | (rng.random((N, 8, 1, R)) < 0.125)
    p = np.where(i == k0, star, np.where((i == ((k0 + 5) & 15)) & no, c[:, :, None, 2:3], p))
    return pack(v, k, p, np.take_along_axis(v, star, 3))
def setup_inputs_ends(rng):
    v, k, p = parts(rng); y = look(rng, v, p)
    p[:, 0] = p[:, 0, :1]
    p[:, 1] = rng.choice(np.array([0, 1, W - 2, W - 1]), (N, 16, R))
    k[:, 2] = (W - 1) * rng.integers(0, 2, (N, 16, W))
    v[:, 3] = 255 * (rng.random((N, 16, W)) < 0.1); y[:, 3] = 255 * (rng.random((N, 16, R)) < 0.9)
    v[:, 3, :, W // 2:] = 0; y[:, 3, :, ::2] = 255
    p[:, 4] = rng.integers(1, W - 1, (N, 16, R)); p[:, 4, 0] = 0; p[:, 4, 15] = W - 1; k[:, 4, :, 0] = 0; k[:, 4, :, W - 1] = 1; y[:, 4] = v[:, 4, :, W - 1:]
    p[:, 5, 0] = 0; k[:, 5, :, 0] = W - 1; y[:, 5] = v[:, 5, :, :1]
    v[:, 6] = 1 * (rng.random((N, 16, W)) < 0.1); y[:, 6] = 255
    h = W - R
    own = np.argsort(rng.random((N, R)), axis=1); rest = np.argsort(rng.random((N, max(h, 15 * R))), axis=1)[:, :15 * R] % h
    p7 = np.concatenate([h + own[:, None, :], rest.reshape(N, 15, R)], axis=1)
    p[:, 7] = np.take_along_axis(p7, np.argsort(rng.random((N, 16, R)), axis=1), 1)
    lead = np.argsort(rng.random((N, 16)), axis=1)[:, :, None] <= 16 - Q
    k[:, 7] = (np.where(lead, h // 2, h) * rng.random((N, 16, W)) ** 4).astype(np.int64)
    k[:, 7, :, h:] = np.where(lead, rng.integers(h // 2, h, (N, 16, R)), rng.integers(0, 9, (N, 16, R)))
    sv = rng.integers(0, 256, (16, R)); v[:, 7, :, h:] = sv; y[:, 7] = sv[:, own].transpose(1, 0, 2)
    return pack(v, k, p, y)
def setup_inputs_ties(rng):
    v, k, p = parts(rng); g = np.arange(8)[None, :, None, None]
    v = rng.integers(0, 2, (N, 8, 16, W)) + 2 * rng.integers(0, 2, (N, 8, 16, W)) * (g % 2); y = rng.integers(0, 4, (N, 8, 16, R))
    k[:, :4] = rng.integers(0, 12, (N, 4, 16, W)); p[:, 3:5] = rng.integers(0, 24, (N, 2, 16, R)) * (W // 32) + 5
    return pack(v, k, p, y)
def setup_inputs_spread(rng):
    lw = np.log2(float(W)); g = np.arange(8)[None, :, None, None]
    c = np.exp2(8 * rng.random((N, 8, 1, W))) * (rng.random((N, 8, 1, W)) > 0.0625)
    v = np.minimum((c * rng.random((N, 8, 16, W))).astype(np.int64), 255)
    z = np.where(g < 4, rng.random((N, 8, 1, W)), rng.random((N, 8, 16, 1)))
    k = np.minimum((np.exp2(lw * z) * rng.random((N, 8, 16, W))).astype(np.int64), W - 1)
    p = np.minimum(np.exp2(lw * rng.random((N, 8, 16, R))).astype(np.int64), W - 1)
    return pack(v, k, p, look(rng, v, p))
def check_inputs(d):
    bad = []
    for k in ("clk", "nam"):
        if np.min(d[k]) < 0 or np.max(d[k]) > W - 1: bad.append("range of " + k)
    for k in ("val", "seen"):
        a = d[k].astype(np.float32)
        if not np.all((a == np.floor(a)) & (a >= 0) & (a <= 255)): bad.append("whole numbers of " + k)
    return bad
def reference(val, clk, nam, seen):
    v = val.astype(np.float32).astype(np.int32).reshape(N, 8, 16, W); y = seen.astype(np.float32).astype(np.int32).reshape(N, 8, 16, R)
    kn = np.array(clk, dtype=np.int32).reshape(N, 8, 16, W); p = np.array(nam, dtype=np.int32).reshape(N, 8, 16, R)
    row = np.arange(16)[None, :, None]
    for t in range(RO):
        for a in range(N):
            b = (a + HOP * t) % N
            pa = p[a]; ix = pa.reshape(8, 1, 16 * R)
            vg = np.take_along_axis(v[b], ix, 2).reshape(8, 16, 16, R)
            kg = np.take_along_axis(kn[b], ix, 2).reshape(8, 16, 16, R)
            d = np.add.reduce(np.abs(vg - y[a][:, :, None, :]), axis=1)
            ks = np.argmin(d, axis=1)
            o = np.take_along_axis(pa, ks[:, None, :], 1)
            ko = np.take_along_axis(kg, ks[:, None, None, :], 2)
            over = (np.add.reduce((kg >= ko).astype(np.int32), axis=1) >= Q) & (pa != o)
            free = ~np.any(over, axis=1); k1 = np.argmax(over, axis=1)
            j = np.maximum.reduce(kg, axis=2)
            p1 = np.take_along_axis(pa, k1[:, None, :], 1); kf = np.take_along_axis(kg, k1[:, None, None, :], 2)[:, :, 0, :]
            back = np.where(row == ks[:, None, :], kf, np.where(row == ((ks + 1) & 15)[:, None, :], p1, pa))
            p[a] = np.where(free[:, None, :], np.maximum(pa, j), back)
            for g in range(8):
                rr = np.flatnonzero(free[g]); names, first = np.unique(o[g, 0, rr], return_index=True)
                kn[b, g][:, names] = j[g][:, rr[first]]
    return {"yp": p.reshape(N, 128, R).astype(np.float32), "yk": np.add.reduce(kn.reshape(N, 128, 8, E), axis=2).astype(np.float32)}

@@ -1,0 +1,536 @@
+import numpy as np
+from concourse.bass import DstId, RemoteDMATransfer
+from concourse.mybir import AluOpType, ActivationFunctionType
+
+W, R, RO, HOP, E = 3072, 192, 4, 3, 384
+C = 64
+NCH = R // C
+EL = 16 * C
+NB = C // 16
+MID = 1536
+K0 = 8
+KW = K0 + W + R
+BIG = 8192.0
+GP = 2
+NKP = 4
+GAM, SCA, HOPX, HOPS, LAT = 1.56, 3.8, 130, 90, 3000
+PERIOD, STAG, SEED, TRIES, POLISH = 15000, 3500, 0, 2000, 400
+
+SCRATCH = {}
+for _d, _l in (
+        ("float32", dict(kw=KW, pl=R, fs=2 * E, fold=E, ccol=144, gcol=128, kcol=128, ncol=16, qcol=64, ocol=64, bcol=128,
+                         pc=16, tma=128, tmb=128, tmc=128, tmd=128, tme=128, swp=128, rdum=R)),
+        ("bfloat16", dict(vw=W, yy=RO * R, ib=128, nib=128, i16n=128, nb=128, pb=128, tri=128, la=128, l2=128, zz=144, sel=16,
+                          kl=128, kr=128, one=128, crow=E, zero=C, rmax=EL // GP, dmask=C, offd=C)),
+        ("float16", dict(po=RO * R, ph=(RO + 1) * R, k16=5 * E, ih=128, boh=128)),
+        ("int32", dict(kraw=W, nraw=R, pi=8)), ("uint16", dict(pu=RO * R))):
+    for _n, _w in _l.items():
+        SCRATCH[_n] = ("sbuf", [128, _w], _d)
+for _j in range(NCH):
+    for _n, _w, _d in (("vg", EL, "bfloat16"), ("mm", EL, "bfloat16"), ("kg", EL, "float16"), ("js", EL, "float16"),
+                       ("ge", EL, "bfloat16"), ("sf", 10 * C + 8, "float32"), ("sh", 3 * C, "float16"),
+                       ("sb", 7 * C, "bfloat16"), ("su", C + 32, "uint16")):
+        SCRATCH["%s%d" % (_n, _j)] = ("sbuf", [128, _w], _d)
+    SCRATCH["oh%d" % _j] = ("sbuf", [128, 18, 8], "bfloat16")
+for _n in ["psy0", "psy1"] + ["ps%s%d" % (_a, _j) for _a in "xz" for _j in range(NCH)]:
+    SCRATCH[_n] = ("psum", [128, 512], "float32")
+SEMAPHORES = (["e_dve", "e_act", "e_pe", "e_pool", "sent", "d_val0", "d_val1", "d_nam", "d_seen", "d_yk"]
+              + ["d_clk%d" % i for i in range(NKP)] + ["d_yp%d" % j for j in range(NCH)]
+              + ["a_y%d" % t for t in range(1, RO)]
+              + ["a_p%d_%d" % (t, j) for t in range(1, RO + 1) for j in range(NCH)])
+A = AluOpType
+F = ActivationFunctionType
+
+
+def build_ops():
+    ops = []
+    cur = [-1, -1]
+
+    def op(eng, cost, fn, rd=(), wr=(), bank=None, sem=None, val=16, lat=0, after=None):
+        ops.append({"eng": eng, "cost": cost, "fn": fn, "rd": list(rd), "wr": list(wr), "bank": bank,
+                    "sem": sem, "val": val, "lat": lat, "after": after, "tag": (cur[0], cur[1])})
+        return len(ops) - 1
+
+    def dve(cost, fn, rd, wr, bank=None):
+        return op("dve", max(64, cost), fn, rd, wr, bank)
+
+    def val(s, T):
+        return s if isinstance(s, (int, float)) else s(T)
+
+    def ts(out, in0, s1, s2, o0, o1, rd, wr, cost=64, bank=None):
+        if o1 is None:
+            return dve(cost, lambda g, T, X: g.vector.tensor_scalar(out(T), in0(T), val(s1, T), None, o0), rd, wr, bank)
+        return dve(cost, lambda g, T, X: g.vector.tensor_scalar(out(T), in0(T), val(s1, T), val(s2, T), o0, o1), rd, wr, bank)
+
+    def tt(out, a, b, o, rd, wr, cost, bank=None):
+        return dve(cost, lambda g, T, X: g.vector.tensor_tensor(out(T), a(T), b(T), o), rd, wr, bank)
+
+    def cp(out, a, rd, wr, cost):
+        return dve(cost, lambda g, T, X: g.vector.tensor_copy(out(T), a(T)), rd, wr)
+
+    def scan(out, d0, d1, init, o0, o1, rd, wr, cost, bank=None):
+        return dve(cost, lambda g, T, X: g.vector.tensor_tensor_scan(out(T), d0(T), d1(T), init, o0, o1), rd, wr, bank)
+
+    def act(out, a, rd, wr, cost, bank=None, bias=0.0, scale=1.0):
+        return op("act", cost, lambda g, T, X: g.scalar.activation(out(T), a(T), F.Identity, bias=bias, scale=scale), rd, wr, bank)
+
+    def mms(lst, rd, wr, bank, mul=1):
+        def fn(g, T, X):
+            ins = None
+            for (o, l, r, st, sp, n) in lst:
+                ins = g.tensor.matmul(o(T), l(T), r(T), st, sp)
+            return ins
+        return op("pe", mul * sum(max(64, m[5]) for m in lst), fn, rd, wr, bank)
+
+    def mset(a, v, wr, cost=64):
+        dve(cost, lambda g, T, X: g.vector.memset(a(T), v), [], wr)
+
+    def ap(name, a=None, b=None, s=None, p=128):
+        return lambda T: T[name][0:p, a:b:s]
+
+    def rev(a):
+        return lambda T: a(T)[:, ::-1]
+
+    def ind(win, a, b, off):
+        return lambda T: T[win][:, a:b].indirect(off(T))
+
+    def dma(q, out, in_, rd, wr, sem, lat):
+        op(q, 60, lambda g, T, X: (g.sync if q == "sp" else g.scalar).dma_start(out(T), in_(T)), rd, wr, sem=sem, lat=lat)
+
+    dma("sp", ap("nraw"), ap("nam"), [], ["nraw"], "d_nam", 2400)
+    dma("sp", ap("vw", 0, W // 2), ap("val", 0, W // 2), [], ["vwa"], "d_val0", 4500)
+    dma("act", ap("vw", W // 2, W), ap("val", W // 2, W), [], ["vwb"], "d_val1", 4500)
+    dma("act", ap("yy", 0, R), ap("seen"), [], ["y0"], "d_seen", 4600)
+    kp = W // NKP
+    for i in range(NKP):
+        dma("sp", ap("kraw", i * kp, (i + 1) * kp), ap("clk", i * kp, (i + 1) * kp), [], ["kraw%d" % i], "d_clk%d" % i, 6000 + 1500 * i)
+
+    def iota(name, n, pat, base=0):
+        op("pool", 160 + 2 * n, lambda g, T, X: g.iota(T[name][:, 0:n], pat, base, 0, allow_small_or_imprecise_dtypes=True), [], [name])
+    op("pool", 162, lambda g, T, X: g.iota(T.pi[:, 0:1], [[0, 1]], 0, 1), [], ["pi"])
+    iota("ccol", 144, [[1, 144]])
+    iota("gcol", 128, [[1, 8], [0, 16]])
+    iota("kcol", 128, [[0, 8], [1, 16]])
+    iota("qcol", 64, [[0, 8], [1, 8]])
+    iota("ocol", 64, [[-1, 8], [0, 8]], 7)
+    iota("bcol", 128, [[0, 64], [8, 2]])
+    iota("ncol", 16, [[16, 16]])
+    M_ = float(MID)
+    cp(ap("pu", 0, R), ap("nraw"), ["nraw"], ["pu0_%d" % j for j in range(NCH)], R)
+    ts(ap("ph", 0, R), ap("nraw"), -M_, None, A.add, None, ["nraw"], ["ph0_%d" % j for j in range(NCH)], R)
+    pi = lambda i: ap("pi", i, i + 1)
+    pc = lambda i: ap("pc", i, i + 1)
+    ts(pi(1), pi(0), 4, None, A.arith_shift_right, None, ["pi"], ["pi1"])
+    ts(pi(2), pi(0), 15, None, A.bitwise_and, None, ["pi"], ["pi2"])
+    ts(pi(5), pi(0), 1.0, None, A.add, None, ["pi"], ["pi5"])
+    ts(pi(3), pi(5), 15, None, A.bitwise_and, None, ["pi5"], ["pi3"])
+    ts(pi(4), pi(0), 1, None, A.bitwise_and, None, ["pi"], ["pi4"])
+    cp(ap("pc", 0, 6), ap("pi", 0, 6), ["pi", "pi1", "pi2", "pi3", "pi4", "pi5"], ["pc"], 64)
+    P_, G_, K_, S_ = pc(0), pc(1), pc(2), pc(3)
+    EQm = (A.is_equal, A.mult)
+    ts(pc(6), G_, 16.0, 15.0, A.mult, A.add, ["pc"], ["pc6"])
+    ts(pc(7), pc(4), -2.0, pc(5), A.mult, A.add, ["pc"], ["pc7"])
+    ts(ap("pc", 8, 11), ap("ccol", 0, 3), P_, None, A.is_equal, None, ["pc", "ccol"], ["pc8"])
+    ts(pc(11), P_, 1.0, None, A.not_equal, None, ["pc"], ["pc11"])
+    c128 = ap("ccol", 0, 128)
+    for name, v in (("ib", 1.0), ("nib", -1.0), ("i16n", -16.0), ("ih", 1.0)):
+        ts(ap(name), c128, P_, v, *EQm, ["ccol", "pc"], [name], 128)
+    ts(ap("swp"), c128, pc(7), None, A.is_equal, None, ["ccol", "pc7"], ["swp"], 128)
+    for i, v in enumerate((32.0, -16.0)):
+        ts(ap("sel", 8 * i, 8 * i + 8), ap("ccol", 0, 8), G_, v, *EQm, ["ccol", "pc"], ["sel%d" % i])
+    ts(ap("kl"), ap("bcol"), pc(9), pc(11), A.mult, A.add, ["bcol", "pc8", "pc11"], ["kl"], 128)
+    ts(ap("tmd", 0, 64), ap("qcol"), pc(8), pc(9), A.mult, A.add, ["qcol", "pc8"], ["tmd0"])
+    ts(ap("tmd", 64, 128), ap("ocol"), pc(10), 131072.0, A.mult, A.mult, ["ocol", "pc8"], ["tmd1"])
+    tt(ap("kr", 0, 64), ap("tmd", 0, 64), ap("tmd", 64, 128), A.add, ["tmd0", "tmd1"], ["kr0"], 128)
+    mset(ap("kr", 64, 128), 0.0, ["kr1"])
+    mset(ap("one", p=1), 1.0, ["one"])
+    mset(ap("crow", p=1), 8 * M_, ["crow"], E // 2)
+    mset(ap("zero"), 0.0, ["zero"])
+    for name, v in (("boh", 1.0), ("nb", -BIG), ("pb", BIG), ("tma", 1.0)):
+        ts(ap(name), ap("gcol"), G_, v, *EQm, ["gcol", "pc"], [name], 128)
+    ts(ap("zz"), ap("ccol"), pc(6), None, A.is_equal, None, ["ccol", "pc6"], ["zz"], 144)
+    mset(ap("rmax"), 0.0, ["rmax"], EL // GP // 2)
+    mset(ap("rmax", 0, EL // GP, 16), -BIG, ["rmax"])
+    mset(ap("kw", 0, K0), -M_, ["kwlo"])
+    mset(ap("kw", K0 + W, KW), 0.0, ["kwhi"], R)
+    kc = ["kcol", "pc"]
+    ts(ap("dmask"), ap("kcol", 0, C), K_, 30720.0, *EQm, kc, ["dmask"])
+    ts(ap("offd"), ap("kcol", 0, C), K_, BIG, A.not_equal, A.mult, kc, ["offd"])
+    ts(ap("tmb"), ap("kcol"), K_, -BIG, A.is_gt, A.mult, kc, ["tmb"], 128)
+    ts(ap("tmc"), ap("kcol"), K_, BIG, *EQm, kc, ["tmc"], 128)
+    tt(ap("tmb"), ap("tmb"), ap("tmc"), A.add, ["tmb", "tmc"], ["tmb"], 256)
+    tt(ap("tri"), ap("tmb"), ap("tma"), A.mult, ["tmb", "tma"], ["tri"], 256)
+    ts(ap("tme"), ap("kcol"), S_, 0.5, *EQm, kc, ["tme"], 128)
+    ts(ap("tmb"), ap("tme"), -1.4375, None, A.add, None, ["tme"], ["tmb"], 128)
+    tt(ap("l2"), ap("tmb"), ap("tma"), A.mult, ["tmb", "tma"], ["l2"], 256)
+    ts(ap("tmc"), ap("tmc"), -8.0 / BIG, -6.25, A.mult, A.add, ["tmc"], ["tmc"], 128)
+    ts(ap("tme"), ap("tme"), -16.0, None, A.mult, None, ["tme"], ["tme"], 128)
+    tt(ap("tme"), ap("tme"), ap("tmc"), A.add, ["tme", "tmc"], ["tme"], 256)
+    tt(ap("la"), ap("tme"), ap("tma"), A.mult, ["tme", "tma"], ["la"], 256)
+    mset(ap("rdum"), -4096.0, ["rdum"], R)
+    ts(ap("rdum", 0, R, 16), ap("ncol", 0, R // 16), K_, float(W - MID), A.add, A.add, ["ncol", "pc"], ["rdum"])
+    for j in range(NCH):
+        mset(ap("sf%d" % j, 9 * C, 9 * C + 8), -4096.0, ["fpad%d" % j])
+        mset(lambda T, j=j: T["oh%d" % j][:], 0.0, ["oh4%d" % j], 72)
+    for i in range(NKP):
+        ts(ap("kw", K0 + i * kp, K0 + (i + 1) * kp), ap("kraw", i * kp, (i + 1) * kp), -M_, None, A.add, None,
+           ["kraw%d" % i], ["kwi%d" % i], kp)
+    KWK = ["kw", "kwlo", "kwhi"] + ["kwi%d" % i for i in range(NKP)]
+
+    def send_y(g, T, X):
+        trs = []
+        for t in range(1, RO):
+            rid, pid, msk = X["dst"](HOP * t, t)
+            trs.append(RemoteDMATransfer(dst_ids=[DstId(rid=rid, pnc=pid)], dma_engine_mask=msk,
+                                         remote_sem=T.sem["a_y%d" % t], src=T.yy[:, 0:R], dst=T.yy[:, t * R:(t + 1) * R]))
+        return g.remote_dma_fused(trs, local_sem=T.sem.sent)
+    s = op("pool", 1200, send_y, ["y0"], [], sem="sent")
+    for t in range(1, RO):
+        op("net", 0, None, [], ["y%d" % t], sem="a_y%d" % t, val=(4, 4, 8)[t - 1], after=s, lat=4000)
+
+    cq = C // GP
+    ep = EL // GP
+    for t in range(RO):
+        for j in range(NCH):
+            cur[0], cur[1] = t, j
+            n0 = R - C * (j + 1)
+            c0 = t * R + n0
+            k = lambda s, j=j: "%s%d" % (s, j)
+            pcs = lambda s: [s + "_%d" % i for i in range(GP)]
+            vg, mm_, kg, js, ge = k("vg"), k("mm"), k("kg"), k("js"), k("ge")
+            sf, sh, sb, su, px, pz = k("sf"), k("sh"), k("sb"), k("su"), k("psx"), k("psz")
+            oh = lambda a, b, s=1, j=j: (lambda T: T["oh%d" % j][:, a:b:s, :])
+            pu, ph, yk = "pu%d_%d" % (t, j), "ph%d_%d" % (t, j), "y%d" % t
+            PC = ap("ph", c0, c0 + C)
+            FF, MB, U1, U2s, U3, T3, S0, S1, S2 = (ap(sf, i * C, (i + 1) * C) for i in range(9))
+            last = lambda i, sf=sf: ap(sf, i * C + 15, (i + 1) * C, 16)
+            f0 = 9 * C + 8
+            FD = ap(sf, f0, f0 + C); FS = ap(sf, f0 - 1, f0 + C - 1)
+            XX, YY, KO = (ap(sh, i * C, (i + 1) * C) for i in range(3))
+            EQO, OVER, HH, EQ = (ap(sb, i * C, (i + 1) * C) for i in range(4))
+            KEY, CC, OHT, O3, UA, UJ, BB = (ap(px, i * C, (i + 1) * C) for i in range(7))
+            CNT, GG, B1, U2, OM, M2 = (ap(pz, i * C, (i + 1) * C) for i in range(6))
+            pc_ = lambda s, i: ap(s, i * ep, (i + 1) * ep)
+            off = lambda i: ap("pu", c0 + i * cq, c0 + (i + 1) * cq)
+
+            if t > 0:
+                ts(ap("pu", c0, c0 + C), PC, M_, None, A.add, None, [ph], [pu])
+            for i in range(GP):
+                act(pc_(vg, i), ind("vw", 0, W, off(i)), [pu, "vwa", "vwb"], [vg + "_%d" % i], 80 + GAM * ep)
+            kk = lambda q: ap(px, q, C, 8)
+            mms([(KEY, ap("kl", p=3), ap("kr", 0, C, p=3), True, False, C)], ["kl", "kr0"], [k("key")], px)
+            mms([(M2, ap("kl", p=3), ap("kr", C, 2 * C, p=3), True, False, C)], ["kl", "kr1"], [k("m2")], pz)
+            b = "psy1"
+            mms([(ap(b, q, 8 * C, 8), ap("ib"), ap("yy", c0, c0 + C), q == 0, q == 7, C) for q in range(8)], [yk, "ib"], [b], b)
+            mms([(kk(q), ap(vg, q, EL, 8), ap("sel", 8, 16), False, False, 8) for q in range(8)], pcs(vg) + ["sel1"], [k("key")], px)
+            for i in range(GP):
+                for par in range(2):
+                    tt(ap(mm_, i * ep + par, (i + 1) * ep, 2), ap(vg, i * ep + par, (i + 1) * ep, 2),
+                       ap(b, i * ep // 2, (i + 1) * ep // 2), A.max, [vg + "_%d" % i, b], [mm_ + "_%d_%d" % (par, i)], ep // 2, b)
+            for par in range(2):
+                mms([(kk(q), ap(mm_, q, EL, 8), ap("sel", 0, 8), False, q == 7, 8) for q in range(par, 8, 2)],
+                    pcs(mm_ + "_%d" % par) + ["sel0"], [k("key")], px)
+            scan(FF, ap("zero"), KEY, 4194304.0, A.add, A.min, [k("key"), "zero"], [k("ff")], C, px)
+            mms([(ap(pz, 5 * C + 7, 6 * C, 8), ap("swp"), ap(sf, 7, C, 8), False, True, 8)], [k("ff"), "swp"], [k("m2")], pz, 4)
+            scan(rev(MB), rev(M2), rev(FF), 0.0, A.max, A.min, [k("ff"), k("m2")], [k("mb")], C, pz)
+            tt(oh(2, 18, 2), KEY, MB, A.is_equal, [k("key"), k("mb")], [k("oh4")], C, px)
+            mms([(OHT, oh(2, 18), ap("ib", 0, 128, 2), True, False, C), (OHT, oh(1, 17), ap("ib", 1, 128, 2), False, True, C)],
+                [k("oh4"), "ib"], [k("oht")], px)
+            tt(XX, OHT, PC, A.mult, [k("oht"), ph], [k("xx")], C, px)
+            mms([(OM, ap("nib"), ap("offd"), True, False, C), (OM, ap("boh"), XX, False, True, C)],
+                [k("xx"), "boh", "nib", "offd"], [k("om")], pz)
+            mms([(O3, ap("boh"), XX, True, True, C)], [k("xx"), "boh"], [k("o3")], px)
+            tt(EQO, O3, PC, A.is_equal, [k("o3"), ph], [k("eqo")], C, px)
+            act(HH, OHT, [k("oht")], [k("hh")], 60 + C, px, bias=-2048.0, scale=16384.0)
+            for i in range(GP):
+                act(pc_(kg, i), ind("kw", K0, KW, off(i)), [pu] + KWK, [kg + "_%d" % i], 80 + GAM * ep)
+            for i in range(GP):
+                scan(pc_(js, i), ap("rmax"), pc_(kg, i), 0.0, A.add, A.max, [kg + "_%d" % i, "rmax"], [js + "_%d" % i], ep // 2)
+            cm = lambda q: (CNT, ap("zz", 15 - q, 143 - q), ap(ge, q, EL, 16), q == 0, False, C)
+            scan(S0, ap("rmax", 0, C), OM, 0.0, A.add, A.max, [k("om"), "rmax"], [k("s0")], C, pz)
+            ts(ap(su, 0, NB), last(6), M_, None, A.add, None, [k("s0")], [k("ob")])
+            cp(KO, ind("kw", K0, KW, ap(su, 0, NB)), [k("ob")] + KWK, [k("ko")], 60 + GAM * C)
+            b = "psy0"
+            mms([(ap(b, q, 8 * C, 8), ap("ih"), KO, q == 0, q == 7, C) for q in range(8)], [k("ko"), "ih"], [b], b)
+            for par in range(2):
+                tt(ap(ge, par, EL, 2), ap(kg, par, EL, 2), ap(b, 0, 8 * C), A.is_ge, pcs(kg) + [b], [ge + "_%d" % par], EL // 2, b)
+            mms([cm(q) for q in range(0, 16, 2)], [ge + "_0", "zz"], [k("cnt")], pz)
+            mms([cm(q) for q in range(1, 16, 2)] + [(CNT, ap("i16n"), EQO, False, True, C)],
+                [ge + "_1", "zz", "i16n", k("eqo")], [k("cnt")], pz)
+            ts(OVER, CNT, 12.5, None, A.is_ge, None, [k("cnt")], [k("over")], C, pz)
+            ov = k("over")
+            mms([(GG, ap("ih"), PC, True, False, C), (GG, ap("tri"), OVER, False, True, C)], [ov, ph, "ih", "tri"], [k("gg")], pz)
+            mms([(UA, ap("la"), HH, True, False, C), (UA, ap("nb"), OVER, False, True, C)], [ov, k("hh"), "la", "nb"], [k("ua")], px)
+            mms([(UJ, ap("ih"), ap(js, 15, EL, 16), True, False, C), (UJ, ap("nb"), OVER, False, True, C)],
+                [ov, "ih", "nb"] + pcs(js), [k("uj")], px)
+            own = lambda o, sp: [(o, ap("ib"), ap("offd"), True, False, C), (o, ap("boh"), XX, False, False, C),
+                                 (o, ap("pb"), OVER, False, sp, C)]
+            ownk = [ov, k("xx"), "ib", "offd", "boh", "pb"]
+            mms(own(BB, True), ownk, [k("bb")], px)
+            ts(YY, GG, -BIG, -2048.0, A.add, A.max, [k("gg")], [k("yy_")], C, pz)
+            mms([(B1, ap("ib"), ap("dmask"), True, False, C), (B1, ap("boh"), YY, False, True, C)],
+                [k("yy_"), "ib", "dmask", "boh"], [k("b1")], pz)
+            scan(S1, ap("rmax", 0, C), B1, 0.0, A.add, A.max, [k("b1"), "rmax"], [k("s1")], C, pz)
+            ts(ap(su, C, C + NB), last(7), M_ + K0, None, A.add, None, [k("s1")], [k("pfo")])
+            mms([(U2, ap("l2"), HH, True, False, C), (U2, ap("boh"), YY, False, True, C)], [k("yy_"), k("hh"), "l2", "boh"], [k("u2")], pz)
+            tt(U1, UA, PC, A.min, [k("ua"), ph], [k("u1")], C, px)
+            tt(U2s, UJ, U1, A.max, [k("uj"), k("u1")], [k("u2s")], C, px)
+            tt(T3, ind("kw", 0, KW, ap(su, C, C + NB)), HH, A.min, [k("pfo"), k("hh")] + KWK, [k("t3")], 60 + GAM * C)
+            tt(U3, U2, U2s, A.max, [k("u2"), k("u2s")], [k("u3")], C, pz)
+            so = ap("po", c0, c0 + C); de = ap("ph", c0 + R, c0 + R + C)
+            tt(so, T3, U3, A.max, [k("t3"), k("u3")], ["po%d_%d" % (t, j)], 2 * C)
+            hop = HOP if t < RO - 1 else -HOP * t
+            land = "ph%d_%d" % (t + 1, j)
+            sem = "a_p%d_%d" % (t + 1, j)
+
+            def send_p(g, T, X, so=so, de=de, hop=hop, sem=sem):
+                rid, pid, msk = X["dst"](hop, 0)
+                return g.remote_dma(de(T), so(T), T.sem[sem], T.sem.sent, pid, rid, msk)
+            s = op("pool", 600, send_p, ["po%d_%d" % (t, j)], [], sem="sent")
+            op("net", 0, None, [], [land], sem=sem, val=16, after=s, lat=LAT - 600)
+            scan(FD, ap("rdum", n0, n0 + C), BB, -4096.0, A.max, A.min, [k("bb"), "rdum"], [k("fd")], C, px)
+            tt(EQ, O3, FS, A.is_equal, [k("o3"), k("fd"), k("fpad")], [k("eq")], C, px)
+            late = own(CC, False) + [(CC, ap("pb"), EQ, False, False, C)]
+            for a in range(NB - 1):
+                e0 = (4 + a) * C; d0 = 16 * (a + 1)
+                ts(ap(sb, e0 + d0, e0 + C), ap(px, 3 * C + d0, 4 * C), ap(sf, f0 + d0 - 1, f0 + d0), None, A.is_equal, None,
+                   [k("o3"), k("fd")], [k("eq") + "_%d" % a], C, px)
+                late.append((ap(px, C + d0, 2 * C), ap("pb"), ap(sb, e0 + d0, e0 + C), False, a == NB - 2, C))
+            mms(late, ownk + [k("eq")] + [k("eq") + "_%d" % a for a in range(NB - 1)], [k("cc")], px)
+            scan(S2, ap("rdum", n0, n0 + C), CC, -4096.0, A.max, A.min, [k("cc"), "rdum"], [k("s2")], C, px)
+            ts(ap(su, C + 16, C + 16 + NB), last(8), M_, None, A.add, None, [k("s2")], [k("tg")])
+            if t == RO - 1:
+                cur[0] = RO
+                ts(ap("pl", n0, n0 + C), de, M_, None, A.add, None, [land], [k("pl")])
+                dma("sp", ap("yp", n0, n0 + C), ap("pl", n0, n0 + C), [k("pl")], [], k("d_yp"), 2400)
+        cur[0], cur[1] = t, NCH
+        for j in range(NCH):
+            cp(ind("kw", K0, KW, ap("su%d" % j, C + 16, C + 16 + NB)), ap("js%d" % j, 15, EL, 16),
+               ["tg%d" % j] + ["js%d_%d" % (j, i) for i in range(GP)], ["kw"], 60 + SCA * C)
+
+    cur[0], cur[1] = RO, 0
+    blk = lambda b: ap("kw", K0 + b * E, K0 + (b + 1) * E)
+    ps = ap("psy0", 0, E)
+    mms([(ps, ap("one", p=1), ap("crow", p=1), True, False, E)], ["one", "crow"], ["psy0"], "psy0")
+    for b in range(5):
+        dst = ap("k16", b * E, (b + 1) * E)
+        if b > 0:
+            act(dst, blk(b), KWK, ["k16_%d" % b], 60 + E)
+        else:
+            cp(dst, blk(b), KWK, ["k16_%d" % b], E)
+        mms([(ps, ap("ih"), dst, False, b == 4, E)], ["k16_%d" % b, "ih"], ["psy0"], "psy0")
+    tt(ap("fs", 0, E), blk(5), blk(6), A.add, KWK, ["fs0"], 2 * E)
+    tt(ap("fs", E, 2 * E), ap("fs", 0, E), blk(7), A.add, KWK + ["fs0"], ["fs1"], 2 * E)
+    tt(ap("fold"), ps, ap("fs", E, 2 * E), A.add, ["psy0", "fs1"], ["fold"], E, "psy0")
+    dma("sp", ap("yk"), ap("fold"), ["fold"], [], "d_yk", 2400)
+    return ops
+
+
+def search(ops, justify, span, pred):
+    n = len(ops)
+    rng = np.random.default_rng(SEED)
+    es = [0.0] * n
+    slot, seen = [0] * n, {}
+    for x in range(n):
+        es[x] = max([es[d] + ops[d]["cost"] + g for d, g in pred[x] if ops[d]["tag"] == ops[x]["tag"]] + [0.0])
+        t = ops[x]["tag"][0]
+        slot[x] = seen.get(t, 0)
+        seen[t] = slot[x] + 1
+    off = np.zeros(seen[1])
+    for x in range(n):
+        t, j = ops[x]["tag"]
+        if t == 1:
+            off[slot[x]] = es[x] + (j * STAG if j < NCH else NCH * STAG + 8000)
+        if t == 0:
+            slot[x] += min(j + 1, NCH)
+
+    def keys(off):
+        return [(-1e6 + x if o["tag"][0] < 0 else 1e6 + x if o["tag"][0] >= RO else o["tag"][0] * PERIOD + float(off[slot[x]]))
+                for x, o in enumerate(ops)]
+    best = justify(keys(off))
+    bs = cs = span(best)
+    for it in range(TRIES):
+        o2 = off.copy()
+        m = rng.integers(3)
+        if m == 0:
+            o2 += rng.normal(0, 300, len(o2))
+        elif m == 1:
+            o2[rng.integers(0, len(o2), 6)] += rng.normal(0, 2500, 6)
+        else:
+            a = rng.integers(0, len(o2))
+            o2[a:a + rng.integers(1, 30)] += rng.normal(0, 2000)
+        st = justify(keys(o2))
+        s = span(st)
+        if s <= cs + 150 * rng.random():
+            off, cs = o2, s
+        if s < bs:
+            best, bs = st, s
+    for it in range(POLISH):
+        v = rng.random(n) * (100.0, 300.0, 1000.0)[it % 3]
+        st = justify([best[x] + float(v[x]) for x in range(n)])
+        if span(st) <= bs:
+            best, bs = st, span(st)
+    return best
+
+
+def plan_program():
+    ops = build_ops()
+    n = len(ops)
+    lastw, readers, runs, lastb = {}, {}, {}, {}
+    for x, o in enumerate(ops):
+        deps = set(lastw[r] for r in o["rd"] + o["wr"] if r in lastw)
+        for w in o["wr"]:
+            deps.update(readers.get(w, []))
+        b = o["bank"]
+        if b is not None:
+            rn = runs.setdefault(b, {})
+            for e, lst in rn.items():
+                if e != o["eng"]:
+                    deps.update(lst)
+                elif e == "pe":
+                    deps.add(lst[-1])
+            if lastb.get(b) == o["eng"]:
+                rn[o["eng"]].append(x)
+            else:
+                rn[o["eng"]] = [x]
+            lastb[b] = o["eng"]
+        for r in o["rd"]:
+            readers.setdefault(r, []).append(x)
+        for w in o["wr"]:
+            lastw[w] = x
+            readers[w] = []
+        deps.discard(x)
+        o["wait"] = set(d for d in deps if not (o["eng"] == "pe" and ops[d]["eng"] == "pe"))
+        o["sd"] = set(deps)
+        if o["after"] is not None:
+            o["sd"].add(o["after"])
+    cost = [o["cost"] for o in ops]
+    eng = [o["eng"] for o in ops]
+    tail = [ops[x]["lat"] if eng[x] != "net" else 0 for x in range(n)]
+
+    def gap(d, x):
+        if eng[x] == "net":
+            return ops[x]["lat"]
+        return tail[d] + (0 if d not in ops[x]["wait"] else HOPS if eng[d] == eng[x] else HOPX)
+    pred = [[(d, gap(d, x)) for d in sorted(ops[x]["sd"])] for x in range(n)]
+    nxt = [[] for x in range(n)]
+    for x in range(n):
+        for d, gp in pred[x]:
+            nxt[d].append((x, gp))
+
+    def place(key, before, after, head):
+        left = [len(p) for p in before]
+        start = [0.0] * n
+        busy = {}
+        cand = [x for x in range(n) if left[x] == 0]
+        while cand:
+            x = min(cand, key=lambda y: key[y])
+            cand.remove(x)
+            t = head[x]
+            for d, gp in before[x]:
+                t = max(t, start[d] + cost[d] + gp)
+            if eng[x] != "net":
+                lst = busy.setdefault(eng[x], [])
+                i = len(lst)
+                while i > 0 and lst[i - 1][1] > t:
+                    i -= 1
+                while i < len(lst) and lst[i][0] < t + cost[x]:
+                    t = max(t, lst[i][1])
+                    i += 1
+                lst.insert(i, (t, t + cost[x]))
+            start[x] = t
+            for s, gp in after[x]:
+                left[s] -= 1
+                if left[s] == 0:
+                    cand.append(s)
+        return start
+    zero = [0.0] * n
+
+    def span(st):
+        return max(st[x] + cost[x] + tail[x] for x in range(n))
+
+    def justify(key):
+        st = place(key, pred, nxt, zero)
+        bk = place([-(st[x] + cost[x]) for x in range(n)], nxt, pred, tail)
+        st2 = place([-(bk[x] + cost[x]) for x in range(n)], pred, nxt, zero)
+        return st2 if span(st2) <= span(st) else st
+    best = search(ops, justify, span, pred)
+    order, pos = {}, {}
+    seq = sorted(range(n), key=lambda y: (best[y], y))
+    for x in seq:
+        ops[x]["t"] = best[x]
+        pos[x] = len(order.setdefault(eng[x], []))
+        order[eng[x]].append(x)
+    known = {e: {} for e in order}
+    for x in seq:
+        o = ops[x]
+        kn = known[o["eng"]]
+        need = {}
+        for d in sorted(o["wait"]):
+            if ops[d]["sem"] is not None:
+                need[("s", d)] = (0, d)
+            elif pos[d] > need.get(eng[d], (-1, 0))[0]:
+                need[eng[d]] = (pos[d], d)
+        o["waits"] = []
+        for key, (p, d) in sorted(need.items(), key=lambda kv: -best[kv[1][1]]):
+            if kn.get(key, -1) >= p:
+                continue
+            o["waits"].append(d)
+            ops[d]["inc"] = True
+            kn[key] = p
+            for k2, v2 in ops[d].get("kn", {}).items():
+                if kn.get(k2, -1) < v2:
+                    kn[k2] = v2
+        o["kn"] = dict(kn) if o["eng"] != "net" else {}
+    for e, lst in order.items():
+        c = 0
+        for x in lst:
+            if ops[x]["sem"] is None and ops[x].get("inc"):
+                c += 1
+                ops[x]["cnt"] = c
+    return ops, order, None, span(best)
+
+
+_PLAN = []
+
+
+def rank_program(g, core, T, topo):
+    rank = T.rank_of(core)
+    if rank is None:
+        return
+    if not _PLAN:
+        _PLAN.append(plan_program())
+    ops, order = _PLAN[0][:2]
+    cores = T.cores
+
+    def dst(hop, part):
+        to = cores[(rank + hop) % len(cores)]
+        rid, pid, se = topo.addr(to)
+        en = topo.engines(core, to)
+        q = len(en) // 4
+        use = {0: en, 1: en[0:q], 2: en[q:2 * q], 3: en[2 * q:]}[part]
+        return rid, pid, sum(1 << e for e in use)
+    X = {"dst": dst}
+    queues = {"dve": g.vector, "act": g.scalar, "pe": g.tensor, "pool": g, "sp": g.sync}
+    sent = 0
+    for e in ("sp", "pool", "act", "pe", "dve"):
+        q = queues[e]
+        for x in order[e]:
+            o = ops[x]
+            for d in o["waits"]:
+                p = ops[d]
+                if p["sem"] is not None:
+                    q.wait_ge(T.sem[p["sem"]], p["val"])
+                else:
+                    q.wait_ge(T.sem["e_" + p["eng"]], p["cnt"])
+            ins = o["fn"](g, T, X)
+            if o["sem"] == "sent":
+                sent += 16
+            elif o["sem"] is not None:
+                ins.then_inc(T.sem[o["sem"]], 16)
+            elif o.get("inc"):
+                ins.then_inc(T.sem["e_" + e], 1)
+    g.wait_ge(T.sem.sent, sent)
+    for j in range(NCH):
+        g.wait_ge(T.sem["d_yp%d" % j], 16)
+    g.wait_ge(T.sem.d_yk, 16)

@@ -13,42 +13,52 @@ KW = K0 + W + R
 BIG = 8192.0
 GP = 2
 NKP = 4
-GAM, SCA, HOPX, HOPS, LAT = 1.56, 3.8, 130, 90, 3000
-PERIOD, STAG, SEED, TRIES, POLISH = 15000, 3500, 0, 2000, 400
+NBC = 4
+NSC = 2
+PAD = 24
+YA = 8
+GAM, SCA, HOPX, HOPS, LAT = 1.56, 3.8, 260, 220, 3000
+PERIOD, STAG, SEED, TRIES, POLISH = 16000, 3500, 0, 2000, 400
 
 SCRATCH = {}
 for _d, _l in (
-        ("float32", dict(kw=KW, pl=R, fs=2 * E, fold=E, ccol=144, gcol=128, kcol=128, ncol=16, qcol=64, ocol=64, bcol=128,
-                         pc=16, tma=128, tmb=128, tmc=128, tmd=128, tme=128, swp=128, rdum=R)),
-        ("bfloat16", dict(vw=W, yy=RO * R, ib=128, nib=128, i16n=128, nb=128, pb=128, tri=128, la=128, l2=128, zz=144, sel=16,
-                          kl=128, kr=128, one=128, crow=E, zero=C, rmax=EL // GP, dmask=C, offd=C)),
+        ("float32", dict(kw=KW, pl=R, fs=2 * E, fold=E, pc=16, swp=128, rdum=R)),
+        ("bfloat16", dict(vw=W, yy=R, ib=128, nb=128, pb=128, tri=128, la=128, l2=128, zz=144, sel=16,
+                          ccol=144, gcol=128, kcol=128, ncol=16, qcol=64, ocol=64, bcol=128,
+                          tma=128, tmb=128, tmc=128, tmd=128, tme=128, tmf=128, tmg=128,
+                          kl=128, kr=64, one=128, crow=E, zero=C, rmax=EL // GP, dmask=C, offd=C, dgm=C)),
         ("float16", dict(po=RO * R, ph=(RO + 1) * R, k16=5 * E, ih=128, boh=128)),
         ("int32", dict(kraw=W, nraw=R, pi=8)), ("uint16", dict(pu=RO * R))):
     for _n, _w in _l.items():
         SCRATCH[_n] = ("sbuf", [128, _w], _d)
+for _t in range(RO):
+    SCRATCH["yx%d" % _t] = ("sbuf", [128, 16 * R], "bfloat16")
 for _j in range(NCH):
-    for _n, _w, _d in (("vg", EL, "bfloat16"), ("mm", EL, "bfloat16"), ("kg", EL, "float16"), ("js", EL, "float16"),
-                       ("ge", EL, "bfloat16"), ("sf", 10 * C + 8, "float32"), ("sh", 3 * C, "float16"),
-                       ("sb", 7 * C, "bfloat16"), ("su", C + 32, "uint16")):
+    for _n, _w, _d in (("kg", EL, "float16"), ("js", EL, "float16"), ("ge", EL, "bfloat16"), ("sf", 7 * C, "float32"),
+                       ("sh", 6 * C + PAD, "float16"), ("sb", 5 * C, "bfloat16"), ("su", 48, "uint16")):
         SCRATCH["%s%d" % (_n, _j)] = ("sbuf", [128, _w], _d)
+    SCRATCH["vg%d" % _j] = ("sbuf", [128, EL], "bfloat16")
+    SCRATCH["mm%d" % _j] = ("sbuf", [128, EL], "bfloat16")
     SCRATCH["oh%d" % _j] = ("sbuf", [128, 18, 8], "bfloat16")
 for _n in ["psy0", "psy1"] + ["ps%s%d" % (_a, _j) for _a in "xz" for _j in range(NCH)]:
     SCRATCH[_n] = ("psum", [128, 512], "float32")
 SEMAPHORES = (["e_dve", "e_act", "e_pe", "e_pool", "sent", "d_val0", "d_val1", "d_nam", "d_seen", "d_yk"]
               + ["d_clk%d" % i for i in range(NKP)] + ["d_yp%d" % j for j in range(NCH)]
-              + ["a_y%d" % t for t in range(1, RO)]
-              + ["a_p%d_%d" % (t, j) for t in range(1, RO + 1) for j in range(NCH)])
+              + ["a_%s%d_%d" % (a, t, j) for a, n in (("y", RO), ("p", RO + 1)) for t in range(1, n) for j in range(NCH)])
 A = AluOpType
 F = ActivationFunctionType
 
 
 def build_ops():
     ops = []
-    cur = [-1, -1]
+    cur = [-1, -1, 0]
 
-    def op(eng, cost, fn, rd=(), wr=(), bank=None, sem=None, val=16, lat=0, after=None):
-        ops.append({"eng": eng, "cost": cost, "fn": fn, "rd": list(rd), "wr": list(wr), "bank": bank,
-                    "sem": sem, "val": val, "lat": lat, "after": after, "tag": (cur[0], cur[1])})
+    def op(eng, cost, fn, rd=(), wr=(), bank=None, sem=None, val=16, lat=0, after=None, slot=None):
+        if slot is None:
+            slot = cur[2]
+            cur[2] += 1
+        ops.append({"eng": eng, "cost": cost, "fn": fn, "rd": list(rd), "wr": list(wr), "bank": bank, "sem": sem,
+                    "val": val, "lat": lat, "after": after, "tag": (cur[0], cur[1]), "slot": (cur[1], slot)})
         return len(ops) - 1
 
     def dve(cost, fn, rd, wr, bank=None):
@@ -71,22 +81,26 @@ def build_ops():
     def scan(out, d0, d1, init, o0, o1, rd, wr, cost, bank=None):
         return dve(cost, lambda g, T, X: g.vector.tensor_tensor_scan(out(T), d0(T), d1(T), init, o0, o1), rd, wr, bank)
 
-    def act(out, a, rd, wr, cost, bank=None, bias=0.0, scale=1.0):
-        return op("act", cost, lambda g, T, X: g.scalar.activation(out(T), a(T), F.Identity, bias=bias, scale=scale), rd, wr, bank)
+    def act(out, a, rd, wr, cost, bank=None, bias=0.0, scale=1.0, slot=None):
+        return op("act", cost, lambda g, T, X: g.scalar.activation(out(T), a(T), F.Identity, bias=bias, scale=scale), rd, wr, bank,
+                  slot=slot)
 
-    def mms(lst, rd, wr, bank, mul=1):
+    def mms(lst, rd, wr, bank, start=True, stop=True, mul=1):
         def fn(g, T, X):
             ins = None
-            for (o, l, r, st, sp, n) in lst:
-                ins = g.tensor.matmul(o(T), l(T), r(T), st, sp)
+            for i, (o, l, r, n) in enumerate(lst):
+                ins = g.tensor.matmul(o(T), l(T), r(T), start and i == 0, stop and i == len(lst) - 1)
             return ins
-        return op("pe", mul * sum(max(64, m[5]) for m in lst), fn, rd, wr, bank)
+        return op("pe", mul * sum(max(64, m[3]) for m in lst), fn, rd, wr, bank)
 
-    def mset(a, v, wr, cost=64):
-        dve(cost, lambda g, T, X: g.vector.memset(a(T), v), [], wr)
+    def mset(a, v, wr, cost=64, bank=None):
+        dve(cost, lambda g, T, X: g.vector.memset(a(T), v), [], wr, bank)
 
     def ap(name, a=None, b=None, s=None, p=128):
         return lambda T: T[name][0:p, a:b:s]
+
+    def ap3(name, a, b, last):
+        return lambda T: T[name][:, a:b, last]
 
     def rev(a):
         return lambda T: a(T)[:, ::-1]
@@ -97,10 +111,18 @@ def build_ops():
     def dma(q, out, in_, rd, wr, sem, lat):
         op(q, 60, lambda g, T, X: (g.sync if q == "sp" else g.scalar).dma_start(out(T), in_(T)), rd, wr, sem=sem, lat=lat)
 
+    def send(de, so, hop, sem, rd, land, lat, after=None, slot=None):
+        def fn(g, T, X):
+            rid, pid, msk = X["dst"](hop, 0)
+            return g.remote_dma(de(T), so(T), T.sem[sem], T.sem.sent, pid, rid, msk)
+        s = op("pool", 600, fn, rd, [], sem="sent", after=after, slot=slot)
+        op("net", 0, None, [], [land], sem=sem, val=16, after=s, lat=lat, slot=slot and slot + "n")
+        return s
+
     dma("sp", ap("nraw"), ap("nam"), [], ["nraw"], "d_nam", 2400)
+    dma("act", ap("yy"), ap("seen"), [], ["yy"], "d_seen", 2400)
     dma("sp", ap("vw", 0, W // 2), ap("val", 0, W // 2), [], ["vwa"], "d_val0", 4500)
     dma("act", ap("vw", W // 2, W), ap("val", W // 2, W), [], ["vwb"], "d_val1", 4500)
-    dma("act", ap("yy", 0, R), ap("seen"), [], ["y0"], "d_seen", 4600)
     kp = W // NKP
     for i in range(NKP):
         dma("sp", ap("kraw", i * kp, (i + 1) * kp), ap("clk", i * kp, (i + 1) * kp), [], ["kraw%d" % i], "d_clk%d" % i, 6000 + 1500 * i)
@@ -109,90 +131,95 @@ def build_ops():
         op("pool", 160 + 2 * n, lambda g, T, X: g.iota(T[name][:, 0:n], pat, base, 0, allow_small_or_imprecise_dtypes=True), [], [name])
     op("pool", 162, lambda g, T, X: g.iota(T.pi[:, 0:1], [[0, 1]], 0, 1), [], ["pi"])
     iota("ccol", 144, [[1, 144]])
-    iota("gcol", 128, [[1, 8], [0, 16]])
-    iota("kcol", 128, [[0, 8], [1, 16]])
     iota("qcol", 64, [[0, 8], [1, 8]])
     iota("ocol", 64, [[-1, 8], [0, 8]], 7)
     iota("bcol", 128, [[0, 64], [8, 2]])
+    iota("gcol", 128, [[1, 8], [0, 16]])
+    iota("kcol", 128, [[0, 8], [1, 16]])
     iota("ncol", 16, [[16, 16]])
     M_ = float(MID)
+    mset(ap("zero"), 0.0, ["zero"])
+    mset(ap("rmax"), 0.0, ["rmax"], EL // GP // 2)
+    mset(ap("rmax", 0, EL // GP, 16), -BIG, ["rmax"])
+    mset(ap("kw", 0, K0), -M_, ["kwlo"])
+    mset(ap("kw", K0 + W, KW), 0.0, ["kwhi"], R)
+    mset(ap("rdum"), -4096.0, ["rdum"], R)
+    mset(ap("one", p=1), 1.0, ["one"])
+    mset(ap("crow", p=1), 8 * M_, ["crow"], E // 2)
+    for j in range(NCH):
+        mset(ap("sh%d" % j, 5 * C, 5 * C + PAD), -4096.0, ["fpad%d" % j])
+        mset(lambda T, j=j: T["oh%d" % j][:], 0.0, ["oh4%d" % j], 72)
+        mset(ap("psz%d" % j, 0, C), 0.0, ["m2%d" % j], C, "psz%d" % j)
     cp(ap("pu", 0, R), ap("nraw"), ["nraw"], ["pu0_%d" % j for j in range(NCH)], R)
     ts(ap("ph", 0, R), ap("nraw"), -M_, None, A.add, None, ["nraw"], ["ph0_%d" % j for j in range(NCH)], R)
+    for q in range(16):
+        dst = ap("yx0", q, 16 * R, 16)
+        if q < YA:
+            act(dst, ap("yy"), ["yy"], ["yx_%d" % q], 60 + R)
+        else:
+            cp(dst, ap("yy"), ["yy"], ["yx_%d" % q], R // 2)
+    YX0 = ["yx_%d" % q for q in range(16)]
     pi = lambda i: ap("pi", i, i + 1)
     pc = lambda i: ap("pc", i, i + 1)
     ts(pi(1), pi(0), 4, None, A.arith_shift_right, None, ["pi"], ["pi1"])
     ts(pi(2), pi(0), 15, None, A.bitwise_and, None, ["pi"], ["pi2"])
     ts(pi(5), pi(0), 1.0, None, A.add, None, ["pi"], ["pi5"])
-    ts(pi(3), pi(5), 15, None, A.bitwise_and, None, ["pi5"], ["pi3"])
     ts(pi(4), pi(0), 1, None, A.bitwise_and, None, ["pi"], ["pi4"])
+    ts(pi(3), pi(5), 15, None, A.bitwise_and, None, ["pi5"], ["pi3"])
     cp(ap("pc", 0, 6), ap("pi", 0, 6), ["pi", "pi1", "pi2", "pi3", "pi4", "pi5"], ["pc"], 64)
     P_, G_, K_, S_ = pc(0), pc(1), pc(2), pc(3)
     EQm = (A.is_equal, A.mult)
-    ts(pc(6), G_, 16.0, 15.0, A.mult, A.add, ["pc"], ["pc6"])
-    ts(pc(7), pc(4), -2.0, pc(5), A.mult, A.add, ["pc"], ["pc7"])
     ts(ap("pc", 8, 11), ap("ccol", 0, 3), P_, None, A.is_equal, None, ["pc", "ccol"], ["pc8"])
     ts(pc(11), P_, 1.0, None, A.not_equal, None, ["pc"], ["pc11"])
-    c128 = ap("ccol", 0, 128)
-    for name, v in (("ib", 1.0), ("nib", -1.0), ("i16n", -16.0), ("ih", 1.0)):
-        ts(ap(name), c128, P_, v, *EQm, ["ccol", "pc"], [name], 128)
-    ts(ap("swp"), c128, pc(7), None, A.is_equal, None, ["ccol", "pc7"], ["swp"], 128)
+    ts(pc(6), G_, 16.0, 15.0, A.mult, A.add, ["pc"], ["pc6"])
+    ts(pc(7), pc(4), -2.0, pc(5), A.mult, A.add, ["pc"], ["pc7"])
     for i, v in enumerate((32.0, -16.0)):
         ts(ap("sel", 8 * i, 8 * i + 8), ap("ccol", 0, 8), G_, v, *EQm, ["ccol", "pc"], ["sel%d" % i])
-    ts(ap("kl"), ap("bcol"), pc(9), pc(11), A.mult, A.add, ["bcol", "pc8", "pc11"], ["kl"], 128)
+    ts(ap("kl"), ap("bcol"), pc(9), pc(11), A.mult, A.add, ["bcol", "pc8", "pc11"], ["kl"])
     ts(ap("tmd", 0, 64), ap("qcol"), pc(8), pc(9), A.mult, A.add, ["qcol", "pc8"], ["tmd0"])
     ts(ap("tmd", 64, 128), ap("ocol"), pc(10), 131072.0, A.mult, A.mult, ["ocol", "pc8"], ["tmd1"])
-    tt(ap("kr", 0, 64), ap("tmd", 0, 64), ap("tmd", 64, 128), A.add, ["tmd0", "tmd1"], ["kr0"], 128)
-    mset(ap("kr", 64, 128), 0.0, ["kr1"])
-    mset(ap("one", p=1), 1.0, ["one"])
-    mset(ap("crow", p=1), 8 * M_, ["crow"], E // 2)
-    mset(ap("zero"), 0.0, ["zero"])
-    for name, v in (("boh", 1.0), ("nb", -BIG), ("pb", BIG), ("tma", 1.0)):
-        ts(ap(name), ap("gcol"), G_, v, *EQm, ["gcol", "pc"], [name], 128)
-    ts(ap("zz"), ap("ccol"), pc(6), None, A.is_equal, None, ["ccol", "pc6"], ["zz"], 144)
-    mset(ap("rmax"), 0.0, ["rmax"], EL // GP // 2)
-    mset(ap("rmax", 0, EL // GP, 16), -BIG, ["rmax"])
-    mset(ap("kw", 0, K0), -M_, ["kwlo"])
-    mset(ap("kw", K0 + W, KW), 0.0, ["kwhi"], R)
+    tt(ap("kr"), ap("tmd", 0, 64), ap("tmd", 64, 128), A.add, ["tmd0", "tmd1"], ["kr"], 128)
+    c128 = ap("ccol", 0, 128)
+    ts(ap("swp"), c128, pc(7), None, A.is_equal, None, ["ccol", "pc7"], ["swp"], 128)
+    for name in ("ib", "ih"):
+        ts(ap(name), c128, P_, None, A.is_equal, None, ["ccol", "pc"], [name])
+    for name, v in (("boh", 1.0), ("tma", 1.0), ("nb", -BIG), ("pb", BIG)):
+        ts(ap(name), ap("gcol"), G_, v, *EQm, ["gcol", "pc"], [name])
     kc = ["kcol", "pc"]
-    ts(ap("dmask"), ap("kcol", 0, C), K_, 30720.0, *EQm, kc, ["dmask"])
     ts(ap("offd"), ap("kcol", 0, C), K_, BIG, A.not_equal, A.mult, kc, ["offd"])
-    ts(ap("tmb"), ap("kcol"), K_, -BIG, A.is_gt, A.mult, kc, ["tmb"], 128)
-    ts(ap("tmc"), ap("kcol"), K_, BIG, *EQm, kc, ["tmc"], 128)
-    tt(ap("tmb"), ap("tmb"), ap("tmc"), A.add, ["tmb", "tmc"], ["tmb"], 256)
-    tt(ap("tri"), ap("tmb"), ap("tma"), A.mult, ["tmb", "tma"], ["tri"], 256)
-    ts(ap("tme"), ap("kcol"), S_, 0.5, *EQm, kc, ["tme"], 128)
-    ts(ap("tmb"), ap("tme"), -1.4375, None, A.add, None, ["tme"], ["tmb"], 128)
-    tt(ap("l2"), ap("tmb"), ap("tma"), A.mult, ["tmb", "tma"], ["l2"], 256)
-    ts(ap("tmc"), ap("tmc"), -8.0 / BIG, -6.25, A.mult, A.add, ["tmc"], ["tmc"], 128)
-    ts(ap("tme"), ap("tme"), -16.0, None, A.mult, None, ["tme"], ["tme"], 128)
-    tt(ap("tme"), ap("tme"), ap("tmc"), A.add, ["tme", "tmc"], ["tme"], 256)
-    tt(ap("la"), ap("tme"), ap("tma"), A.mult, ["tme", "tma"], ["la"], 256)
-    mset(ap("rdum"), -4096.0, ["rdum"], R)
     ts(ap("rdum", 0, R, 16), ap("ncol", 0, R // 16), K_, float(W - MID), A.add, A.add, ["ncol", "pc"], ["rdum"])
-    for j in range(NCH):
-        mset(ap("sf%d" % j, 9 * C, 9 * C + 8), -4096.0, ["fpad%d" % j])
-        mset(lambda T, j=j: T["oh%d" % j][:], 0.0, ["oh4%d" % j], 72)
+    ts(ap("zz"), ap("ccol"), pc(6), 0.25, *EQm, ["ccol", "pc6"], ["zz"], 72)
+    ts(ap("dmask"), ap("kcol", 0, C), K_, 30720.0, *EQm, kc, ["dmask"])
+    ts(ap("dgm"), ap("offd"), -1.0, 4096.0, A.mult, A.add, ["offd"], ["dgm"])
+    ts(ap("tmb"), ap("kcol"), K_, -BIG, A.is_gt, A.mult, kc, ["tmb"])
+    ts(ap("tmc"), ap("kcol"), K_, BIG, *EQm, kc, ["tmc"])
+    ts(ap("tme"), ap("kcol"), S_, 0.5, *EQm, kc, ["tme"])
+    tt(ap("tmb"), ap("tmb"), ap("tmc"), A.add, ["tmb", "tmc"], ["tmb"], 256)
+    ts(ap("tmf"), ap("tme"), -1.4375, None, A.add, None, ["tme"], ["tmf"])
+    ts(ap("tmc"), ap("tmc"), -8.0 / BIG, -6.25, A.mult, A.add, ["tmc"], ["tmc"])
+    ts(ap("tmg"), ap("tme"), -16.0, None, A.mult, None, ["tme"], ["tmg"])
+    tt(ap("tri"), ap("tmb"), ap("tma"), A.mult, ["tmb", "tma"], ["tri"], 256)
+    tt(ap("l2"), ap("tmf"), ap("tma"), A.mult, ["tmf", "tma"], ["l2"], 256)
+    tt(ap("tmg"), ap("tmg"), ap("tmc"), A.add, ["tmg", "tmc"], ["tmg"], 256)
+    tt(ap("la"), ap("tmg"), ap("tma"), A.mult, ["tmg", "tma"], ["la"], 256)
     for i in range(NKP):
         ts(ap("kw", K0 + i * kp, K0 + (i + 1) * kp), ap("kraw", i * kp, (i + 1) * kp), -M_, None, A.add, None,
            ["kraw%d" % i], ["kwi%d" % i], kp)
     KWK = ["kw", "kwlo", "kwhi"] + ["kwi%d" % i for i in range(NKP)]
 
-    def send_y(g, T, X):
-        trs = []
-        for t in range(1, RO):
-            rid, pid, msk = X["dst"](HOP * t, t)
-            trs.append(RemoteDMATransfer(dst_ids=[DstId(rid=rid, pnc=pid)], dma_engine_mask=msk,
-                                         remote_sem=T.sem["a_y%d" % t], src=T.yy[:, 0:R], dst=T.yy[:, t * R:(t + 1) * R]))
-        return g.remote_dma_fused(trs, local_sem=T.sem.sent)
-    s = op("pool", 1200, send_y, ["y0"], [], sem="sent")
-    for t in range(1, RO):
-        op("net", 0, None, [], ["y%d" % t], sem="a_y%d" % t, val=(4, 4, 8)[t - 1], after=s, lat=4000)
+    def send_y(t, j, rd, after):
+        n0 = R - C * (j + 1)
+        part = lambda s: ap(s, 16 * n0, 16 * (n0 + C))
+        send(part("yx%d" % t), part("yx0"), HOP * t, "a_y%d_%d" % (t, j),
+             YX0 + rd, "y%d_%d" % (t, j), 3500, after, "y")
+    for j in range(NCH):
+        send_y(1, j, ["kraw%d" % (NKP - 1)], None)
 
     cq = C // GP
     ep = EL // GP
     for t in range(RO):
         for j in range(NCH):
-            cur[0], cur[1] = t, j
+            cur[0], cur[1], cur[2] = t, j, 0
             n0 = R - C * (j + 1)
             c0 = t * R + n0
             k = lambda s, j=j: "%s%d" % (s, j)
@@ -200,128 +227,121 @@ def build_ops():
             vg, mm_, kg, js, ge = k("vg"), k("mm"), k("kg"), k("js"), k("ge")
             sf, sh, sb, su, px, pz = k("sf"), k("sh"), k("sb"), k("su"), k("psx"), k("psz")
             oh = lambda a, b, s=1, j=j: (lambda T: T["oh%d" % j][:, a:b:s, :])
-            pu, ph, yk = "pu%d_%d" % (t, j), "ph%d_%d" % (t, j), "y%d" % t
+            pu, ph = "pu%d_%d" % (t, j), "ph%d_%d" % (t, j)
+            yk = ["y%d_%d" % (t, j)] if t else YX0
             PC = ap("ph", c0, c0 + C)
-            FF, MB, U1, U2s, U3, T3, S0, S1, S2 = (ap(sf, i * C, (i + 1) * C) for i in range(9))
+            FF, MB, S0, S1, S2, U1, U2s = (ap(sf, i * C, (i + 1) * C) for i in range(7))
             last = lambda i, sf=sf: ap(sf, i * C + 15, (i + 1) * C, 16)
-            f0 = 9 * C + 8
-            FD = ap(sf, f0, f0 + C); FS = ap(sf, f0 - 1, f0 + C - 1)
             XX, YY, KO = (ap(sh, i * C, (i + 1) * C) for i in range(3))
-            EQO, OVER, HH, EQ = (ap(sb, i * C, (i + 1) * C) for i in range(4))
-            KEY, CC, OHT, O3, UA, UJ, BB = (ap(px, i * C, (i + 1) * C) for i in range(7))
-            CNT, GG, B1, U2, OM, M2 = (ap(pz, i * C, (i + 1) * C) for i in range(6))
+            held = lambda d, sh=sh: ap(sh, 5 * C + PAD - d, 6 * C + PAD - d)
+            NE, OVER, HH, EQ1, EQ2 = (ap(sb, i * C, (i + 1) * C) for i in range(5))
+            KEY, OHT, CNT, BB, CC = (ap(px, i * C, (i + 1) * C) for i in range(5))
+            M2, O3, RR, GG = (ap(pz, i * C, (i + 1) * C) for i in range(4))
             pc_ = lambda s, i: ap(s, i * ep, (i + 1) * ep)
             off = lambda i: ap("pu", c0 + i * cq, c0 + (i + 1) * cq)
+            JJ = ap(js, 15, EL, 16)
 
             if t > 0:
-                ts(ap("pu", c0, c0 + C), PC, M_, None, A.add, None, [ph], [pu])
+                act(ap("pu", c0, c0 + C), PC, [ph], [pu], 60 + C, bias=M_, slot="cvt")
             for i in range(GP):
-                act(pc_(vg, i), ind("vw", 0, W, off(i)), [pu, "vwa", "vwb"], [vg + "_%d" % i], 80 + GAM * ep)
+                act(pc_(vg, i), ind("vw", 0, W, off(i)), [pu, "vwa", "vwb"], [vg + "_%d" % i, vg + "f%d" % i], 80 + GAM * ep)
             kk = lambda q: ap(px, q, C, 8)
-            mms([(KEY, ap("kl", p=3), ap("kr", 0, C, p=3), True, False, C)], ["kl", "kr0"], [k("key")], px)
-            mms([(M2, ap("kl", p=3), ap("kr", C, 2 * C, p=3), True, False, C)], ["kl", "kr1"], [k("m2")], pz)
-            b = "psy1"
-            mms([(ap(b, q, 8 * C, 8), ap("ib"), ap("yy", c0, c0 + C), q == 0, q == 7, C) for q in range(8)], [yk, "ib"], [b], b)
-            mms([(kk(q), ap(vg, q, EL, 8), ap("sel", 8, 16), False, False, 8) for q in range(8)], pcs(vg) + ["sel1"], [k("key")], px)
+            col = lambda s, q: ap(s, q, EL, 8)
+            mms([(KEY, ap("kl", p=3), ap("kr", p=3), C)], ["kl", "kr"], [k("key")], px, True, False)
+            yx = lambda a, b, s=1: ap("yx%d" % t, 16 * n0 + a, 16 * n0 + b, s)
+            pp = 128 // GP
             for i in range(GP):
-                for par in range(2):
-                    tt(ap(mm_, i * ep + par, (i + 1) * ep, 2), ap(vg, i * ep + par, (i + 1) * ep, 2),
-                       ap(b, i * ep // 2, (i + 1) * ep // 2), A.max, [vg + "_%d" % i, b], [mm_ + "_%d_%d" % (par, i)], ep // 2, b)
-            for par in range(2):
-                mms([(kk(q), ap(mm_, q, EL, 8), ap("sel", 0, 8), False, q == 7, 8) for q in range(par, 8, 2)],
-                    pcs(mm_ + "_%d" % par) + ["sel0"], [k("key")], px)
+                a, b = i * ep, (i + 1) * ep
+                mms([(lambda T, i=i, px=px: T[px][i * pp:(i + 1) * pp, 0:C:8], ap(vg, a, b, 8), ap("sel", 8, 16), 8)],
+                    [vg + "_%d" % i, vg + "f%d" % i, "sel1"], [k("key")], px, False, False)
+                tt(ap(vg, a, b, 16), ap(vg, a, b, 16), yx(a, b, 16), A.max, [vg + "f%d" % i] + yk, [vg + "f%d" % i], 2 * cq)
+                scan(pc_(mm_, i), yx(a, b), pc_(vg, i), 0.0, A.min, A.max, [vg + "_%d" % i, vg + "f%d" % i] + yk, [mm_ + "_%d" % i], ep // 2)
+            mms([(kk(q), col(vg, q), ap("sel", 8, 16), 8) for q in range(1, 8)], pcs(vg) + ["sel1"], [k("key")], px, False, False)
+            mms([(kk(q), col(mm_, q), ap("sel", 0, 8), 8) for q in range(8)], pcs(mm_) + ["sel0"], [k("key")], px, False)
             scan(FF, ap("zero"), KEY, 4194304.0, A.add, A.min, [k("key"), "zero"], [k("ff")], C, px)
-            mms([(ap(pz, 5 * C + 7, 6 * C, 8), ap("swp"), ap(sf, 7, C, 8), False, True, 8)], [k("ff"), "swp"], [k("m2")], pz, 4)
+            mms([(ap(pz, 7, C, 8), ap("swp"), ap(sf, 7, C, 8), 8)], [k("ff"), "swp"], [k("m2")], pz, True, mul=4)
             scan(rev(MB), rev(M2), rev(FF), 0.0, A.max, A.min, [k("ff"), k("m2")], [k("mb")], C, pz)
             tt(oh(2, 18, 2), KEY, MB, A.is_equal, [k("key"), k("mb")], [k("oh4")], C, px)
-            mms([(OHT, oh(2, 18), ap("ib", 0, 128, 2), True, False, C), (OHT, oh(1, 17), ap("ib", 1, 128, 2), False, True, C)],
-                [k("oh4"), "ib"], [k("oht")], px)
+            mms([(RR, ap("ib"), ap("offd"), C)], ["ib", "offd"], [k("rr")], pz, True, False)
+            mms([(OHT, oh(2, 18), ap("ib", 0, 128, 2), C), (OHT, oh(1, 17), ap("ib", 1, 128, 2), C)], [k("oh4"), "ib"], [k("oht")], px)
             tt(XX, OHT, PC, A.mult, [k("oht"), ph], [k("xx")], C, px)
-            mms([(OM, ap("nib"), ap("offd"), True, False, C), (OM, ap("boh"), XX, False, True, C)],
-                [k("xx"), "boh", "nib", "offd"], [k("om")], pz)
-            mms([(O3, ap("boh"), XX, True, True, C)], [k("xx"), "boh"], [k("o3")], px)
-            tt(EQO, O3, PC, A.is_equal, [k("o3"), ph], [k("eqo")], C, px)
             act(HH, OHT, [k("oht")], [k("hh")], 60 + C, px, bias=-2048.0, scale=16384.0)
+            mms([(RR, ap("boh"), XX, C)], [k("xx"), "boh"], [k("rr")], pz, False)
+            rd_ = ap("rdum", n0, n0 + C)
+            scan(S0, rd_, RR, -4096.0, A.max, A.min, [k("rr"), "rdum"], [k("s0")], C, pz)
+            ts(ap(su, 0, NB), last(2), M_, None, A.add, None, [k("s0")], [k("ob")])
+            mms([(O3, ap("boh"), XX, C)], [k("xx"), "boh"], [k("o3")], pz)
+            tt(NE, O3, PC, A.not_equal, [k("o3"), ph], [k("ne")], C, pz)
+            mms([(GG, ap("ih"), PC, C)], [ph, "ih"], [k("gg")], pz, True, False)
             for i in range(GP):
                 act(pc_(kg, i), ind("kw", K0, KW, off(i)), [pu] + KWK, [kg + "_%d" % i], 80 + GAM * ep)
+            cp(KO, ind("kw", K0, KW, ap(su, 0, NB)), [k("ob")] + KWK, [k("ko")], 60 + GAM * C)
             for i in range(GP):
                 scan(pc_(js, i), ap("rmax"), pc_(kg, i), 0.0, A.add, A.max, [kg + "_%d" % i, "rmax"], [js + "_%d" % i], ep // 2)
-            cm = lambda q: (CNT, ap("zz", 15 - q, 143 - q), ap(ge, q, EL, 16), q == 0, False, C)
-            scan(S0, ap("rmax", 0, C), OM, 0.0, A.add, A.max, [k("om"), "rmax"], [k("s0")], C, pz)
-            ts(ap(su, 0, NB), last(6), M_, None, A.add, None, [k("s0")], [k("ob")])
-            cp(KO, ind("kw", K0, KW, ap(su, 0, NB)), [k("ob")] + KWK, [k("ko")], 60 + GAM * C)
-            b = "psy0"
-            mms([(ap(b, q, 8 * C, 8), ap("ih"), KO, q == 0, q == 7, C) for q in range(8)], [k("ko"), "ih"], [b], b)
-            for par in range(2):
-                tt(ap(ge, par, EL, 2), ap(kg, par, EL, 2), ap(b, 0, 8 * C), A.is_ge, pcs(kg) + [b], [ge + "_%d" % par], EL // 2, b)
-            mms([cm(q) for q in range(0, 16, 2)], [ge + "_0", "zz"], [k("cnt")], pz)
-            mms([cm(q) for q in range(1, 16, 2)] + [(CNT, ap("i16n"), EQO, False, True, C)],
-                [ge + "_1", "zz", "i16n", k("eqo")], [k("cnt")], pz)
-            ts(OVER, CNT, 12.5, None, A.is_ge, None, [k("cnt")], [k("over")], C, pz)
+            b = "psy%d" % ((t * NCH + j) % 2)
+            B1, U2, UA, UJ, U3 = (ap(b, i * C, (i + 1) * C) for i in range(5))
+            mms([(ap(b, q, NBC * C, NBC), ap("ih"), KO, C) for q in range(NBC)], [k("ko"), "ih"], [b], b)
+            NP = 16 // NBC
+            for r in range(NP):
+                tt(ap(ge, r, EL, NP), ap(kg, r, EL, NP), ap(b, 0, NBC * C), A.is_lt, pcs(kg) + [b], [ge + "_%d" % r], NBC * C, b)
+            for r in range(NP):
+                mms([(CNT, ap("zz", 15 - q, 143 - q), ap(ge, q, EL, 16), C) for q in range(r, 16, NP)],
+                    [ge + "_%d" % r, "zz"], [k("cnt")], px, r == 0, r == NP - 1)
+            mms([(B1, ap("ib"), ap("dmask"), C), (U2, ap("l2"), HH, C)], ["ib", "dmask", k("hh"), "l2"], [b], b, True, False)
+            mms([(UA, ap("la"), HH, C), (UJ, ap("ih"), JJ, C)], pcs(js) + ["ih", k("hh"), "la"], [b], b, False, False)
+            tt(OVER, CNT, NE, A.is_lt, [k("cnt"), k("ne")], [k("over")], C, px)
             ov = k("over")
-            mms([(GG, ap("ih"), PC, True, False, C), (GG, ap("tri"), OVER, False, True, C)], [ov, ph, "ih", "tri"], [k("gg")], pz)
-            mms([(UA, ap("la"), HH, True, False, C), (UA, ap("nb"), OVER, False, True, C)], [ov, k("hh"), "la", "nb"], [k("ua")], px)
-            mms([(UJ, ap("ih"), ap(js, 15, EL, 16), True, False, C), (UJ, ap("nb"), OVER, False, True, C)],
-                [ov, "ih", "nb"] + pcs(js), [k("uj")], px)
-            own = lambda o, sp: [(o, ap("ib"), ap("offd"), True, False, C), (o, ap("boh"), XX, False, False, C),
-                                 (o, ap("pb"), OVER, False, sp, C)]
+            own = lambda o: [(o, ap("ib"), ap("offd"), C), (o, ap("boh"), XX, C), (o, ap("pb"), OVER, C)]
             ownk = [ov, k("xx"), "ib", "offd", "boh", "pb"]
-            mms(own(BB, True), ownk, [k("bb")], px)
+            mms([(GG, ap("tri"), OVER, C)], [ov, "tri"], [k("gg")], pz, False)
+            mms(own(BB), ownk, [k("bb")], px)
+            mms([(UA, ap("nb"), OVER, C), (UJ, ap("nb"), OVER, C)], [ov, "nb"], [b], b, False, False)
             ts(YY, GG, -BIG, -2048.0, A.add, A.max, [k("gg")], [k("yy_")], C, pz)
-            mms([(B1, ap("ib"), ap("dmask"), True, False, C), (B1, ap("boh"), YY, False, True, C)],
-                [k("yy_"), "ib", "dmask", "boh"], [k("b1")], pz)
-            scan(S1, ap("rmax", 0, C), B1, 0.0, A.add, A.max, [k("b1"), "rmax"], [k("s1")], C, pz)
-            ts(ap(su, C, C + NB), last(7), M_ + K0, None, A.add, None, [k("s1")], [k("pfo")])
-            mms([(U2, ap("l2"), HH, True, False, C), (U2, ap("boh"), YY, False, True, C)], [k("yy_"), k("hh"), "l2", "boh"], [k("u2")], pz)
-            tt(U1, UA, PC, A.min, [k("ua"), ph], [k("u1")], C, px)
-            tt(U2s, UJ, U1, A.max, [k("uj"), k("u1")], [k("u2s")], C, px)
-            tt(T3, ind("kw", 0, KW, ap(su, C, C + NB)), HH, A.min, [k("pfo"), k("hh")] + KWK, [k("t3")], 60 + GAM * C)
-            tt(U3, U2, U2s, A.max, [k("u2"), k("u2s")], [k("u3")], C, pz)
+            mms([(B1, ap("boh"), YY, C), (U2, ap("boh"), YY, C)], [k("yy_"), "boh"], [b], b, False)
+            scan(held(0), ap("dgm"), BB, -4096.0, A.max, A.min, [k("bb"), "dgm"], [k("fd")], C, px)
+            mms(own(CC), ownk, [k("cc")], px, True, False)
+            tt(EQ1, O3, held(1), A.is_equal, [k("o3"), k("fd"), k("fpad")], [k("eq1")], C, pz)
+            tt(EQ2, O3, held(17), A.is_equal, [k("o3"), k("fd"), k("fpad")], [k("eq2")], C, pz)
+            scan(S1, ap("rmax", 0, C), B1, 0.0, A.add, A.max, [b, "rmax"], [k("s1")], C, b)
+            tt(U1, UA, PC, A.min, [b, ph], [k("u1")], C, b)
+            ts(ap(su, 16, 16 + NB), last(3), M_ + K0, None, A.add, None, [k("s1")], [k("pfo")])
+            tt(U2s, UJ, U1, A.max, [b, k("u1")], [k("u2s")], C, b)
+            tt(U3, U2, U2s, A.max, [b, k("u2s")], [k("u3")], C, b)
+            tt(YY, ind("kw", 0, KW, ap(su, 16, 16 + NB)), HH, A.min, [k("pfo"), k("hh")] + KWK, [k("yy_")], 60 + GAM * C)
             so = ap("po", c0, c0 + C); de = ap("ph", c0 + R, c0 + R + C)
-            tt(so, T3, U3, A.max, [k("t3"), k("u3")], ["po%d_%d" % (t, j)], 2 * C)
-            hop = HOP if t < RO - 1 else -HOP * t
+            tt(so, U3, YY, A.max, [k("yy_"), k("u3")], ["po%d_%d" % (t, j)], C, b)
             land = "ph%d_%d" % (t + 1, j)
-            sem = "a_p%d_%d" % (t + 1, j)
-
-            def send_p(g, T, X, so=so, de=de, hop=hop, sem=sem):
-                rid, pid, msk = X["dst"](hop, 0)
-                return g.remote_dma(de(T), so(T), T.sem[sem], T.sem.sent, pid, rid, msk)
-            s = op("pool", 600, send_p, ["po%d_%d" % (t, j)], [], sem="sent")
-            op("net", 0, None, [], [land], sem=sem, val=16, after=s, lat=LAT - 600)
-            scan(FD, ap("rdum", n0, n0 + C), BB, -4096.0, A.max, A.min, [k("bb"), "rdum"], [k("fd")], C, px)
-            tt(EQ, O3, FS, A.is_equal, [k("o3"), k("fd"), k("fpad")], [k("eq")], C, px)
-            late = own(CC, False) + [(CC, ap("pb"), EQ, False, False, C)]
-            for a in range(NB - 1):
-                e0 = (4 + a) * C; d0 = 16 * (a + 1)
-                ts(ap(sb, e0 + d0, e0 + C), ap(px, 3 * C + d0, 4 * C), ap(sf, f0 + d0 - 1, f0 + d0), None, A.is_equal, None,
-                   [k("o3"), k("fd")], [k("eq") + "_%d" % a], C, px)
-                late.append((ap(px, C + d0, 2 * C), ap("pb"), ap(sb, e0 + d0, e0 + C), False, a == NB - 2, C))
-            mms(late, ownk + [k("eq")] + [k("eq") + "_%d" % a for a in range(NB - 1)], [k("cc")], px)
-            scan(S2, ap("rdum", n0, n0 + C), CC, -4096.0, A.max, A.min, [k("cc"), "rdum"], [k("s2")], C, px)
-            ts(ap(su, C + 16, C + 16 + NB), last(8), M_, None, A.add, None, [k("s2")], [k("tg")])
+            s = send(de, so, HOP if t < RO - 1 else -HOP * t, "a_p%d_%d" % (t + 1, j), ["po%d_%d" % (t, j)], land, LAT - 600)
+            if t + 2 < RO:
+                send_y(t + 2, j, [], s)
+            mms([(CC, ap("pb"), EQ1, C), (CC, ap("pb"), EQ2, C)], [k("eq1"), k("eq2"), "pb"], [k("cc")], px, False)
+            scan(S2, rd_, CC, -4096.0, A.max, A.min, [k("cc"), "rdum"], [k("s2")], C, px)
+            ts(ap(su, 32, 32 + NB), last(4), M_, None, A.add, None, [k("s2")], [k("tg")])
             if t == RO - 1:
                 cur[0] = RO
-                ts(ap("pl", n0, n0 + C), de, M_, None, A.add, None, [land], [k("pl")])
+                act(ap("pl", n0, n0 + C), de, [land], [k("pl")], 60 + C, bias=M_)
                 dma("sp", ap("yp", n0, n0 + C), ap("pl", n0, n0 + C), [k("pl")], [], k("d_yp"), 2400)
-        cur[0], cur[1] = t, NCH
+        cur[0], cur[1], cur[2] = t, NCH, 0
+        nb_, ne = NB // NSC, EL // NSC
         for j in range(NCH):
-            cp(ind("kw", K0, KW, ap("su%d" % j, C + 16, C + 16 + NB)), ap("js%d" % j, 15, EL, 16),
-               ["tg%d" % j] + ["js%d_%d" % (j, i) for i in range(GP)], ["kw"], 60 + SCA * C)
+            for h in reversed(range(NSC)):
+                cp(ind("kw", K0, KW, ap("su%d" % j, 32 + h * nb_, 32 + (h + 1) * nb_)), ap("js%d" % j, h * ne + 15, (h + 1) * ne, 16),
+                   ["tg%d" % j] + ["js%d_%d" % (j, i) for i in range(GP)], ["kw"], 60 + SCA * C / NSC)
 
     cur[0], cur[1] = RO, 0
     blk = lambda b: ap("kw", K0 + b * E, K0 + (b + 1) * E)
     ps = ap("psy0", 0, E)
-    mms([(ps, ap("one", p=1), ap("crow", p=1), True, False, E)], ["one", "crow"], ["psy0"], "psy0")
+    mms([(ps, ap("one", p=1), ap("crow", p=1), E)], ["one", "crow"], ["psy0"], "psy0", True, False)
     for b in range(5):
         dst = ap("k16", b * E, (b + 1) * E)
         if b > 0:
             act(dst, blk(b), KWK, ["k16_%d" % b], 60 + E)
         else:
             cp(dst, blk(b), KWK, ["k16_%d" % b], E)
-        mms([(ps, ap("ih"), dst, False, b == 4, E)], ["k16_%d" % b, "ih"], ["psy0"], "psy0")
-    tt(ap("fs", 0, E), blk(5), blk(6), A.add, KWK, ["fs0"], 2 * E)
-    tt(ap("fs", E, 2 * E), ap("fs", 0, E), blk(7), A.add, KWK + ["fs0"], ["fs1"], 2 * E)
-    tt(ap("fold"), ps, ap("fs", E, 2 * E), A.add, ["psy0", "fs1"], ["fold"], E, "psy0")
+        mms([(ps, ap("ih"), dst, E)], ["k16_%d" % b, "ih"], ["psy0"], "psy0", False, b == 4)
+    tt(ap("psy1", 0, E), blk(5), blk(6), A.add, KWK, ["psy1"], 2 * E, "psy1")
+    tt(ap("fs", 0, E), ap("psy1", 0, E), blk(7), A.add, KWK + ["psy1"], ["fs1"], E, "psy1")
+    tt(ap("fold"), ps, ap("fs", 0, E), A.add, ["psy0", "fs1"], ["fold"], E, "psy0")
     dma("sp", ap("yk"), ap("fold"), ["fold"], [], "d_yk", 2400)
     return ops
 
@@ -330,22 +350,19 @@ def search(ops, justify, span, pred):
     n = len(ops)
     rng = np.random.default_rng(SEED)
     es = [0.0] * n
-    slot, seen = [0] * n, {}
+    slots = {}
     for x in range(n):
         es[x] = max([es[d] + ops[d]["cost"] + g for d, g in pred[x] if ops[d]["tag"] == ops[x]["tag"]] + [0.0])
-        t = ops[x]["tag"][0]
-        slot[x] = seen.get(t, 0)
-        seen[t] = slot[x] + 1
-    off = np.zeros(seen[1])
+        if ops[x]["tag"][0] == 1:
+            slots[ops[x]["slot"]] = len(slots)
+    off = np.zeros(len(slots))
     for x in range(n):
         t, j = ops[x]["tag"]
         if t == 1:
-            off[slot[x]] = es[x] + (j * STAG if j < NCH else NCH * STAG + 8000)
-        if t == 0:
-            slot[x] += min(j + 1, NCH)
+            off[slots[ops[x]["slot"]]] = es[x] + (j * STAG if j < NCH else NCH * STAG + 8000)
 
     def keys(off):
-        return [(-1e6 + x if o["tag"][0] < 0 else 1e6 + x if o["tag"][0] >= RO else o["tag"][0] * PERIOD + float(off[slot[x]]))
+        return [(-1e6 + x if o["tag"][0] < 0 else 1e6 + x if o["tag"][0] >= RO else o["tag"][0] * PERIOD + float(off[slots[o["slot"]]]))
                 for x, o in enumerate(ops)]
     best = justify(keys(off))
     bs = cs = span(best)
@@ -488,7 +505,7 @@ def plan_program():
             if ops[x]["sem"] is None and ops[x].get("inc"):
                 c += 1
                 ops[x]["cnt"] = c
-    return ops, order, None, span(best)
+    return ops, order, seq, span(best)
 
 
 _PLAN = []
@@ -506,10 +523,7 @@ def rank_program(g, core, T, topo):
     def dst(hop, part):
         to = cores[(rank + hop) % len(cores)]
         rid, pid, se = topo.addr(to)
-        en = topo.engines(core, to)
-        q = len(en) // 4
-        use = {0: en, 1: en[0:q], 2: en[q:2 * q], 3: en[2 * q:]}[part]
-        return rid, pid, sum(1 << e for e in use)
+        return rid, pid, topo.mask(core, to)
     X = {"dst": dst}
     queues = {"dve": g.vector, "act": g.scalar, "pe": g.tensor, "pool": g, "sp": g.sync}
     sent = 0

@@ -1,6 +1,6 @@
 import numpy as np
 from concourse.bass import DstId, RemoteDMATransfer
-from concourse.mybir import AluOpType, ActivationFunctionType
+from concourse.mybir import AluOpType, ActivationFunctionType, AxisListType
 
 W, R, RO, HOP, E = 3072, 192, 4, 3, 384
 C = 64
@@ -8,42 +8,42 @@ NCH = R // C
 EL = 16 * C
 NB = C // 16
 MID = 1536
-K0 = 8
+K0 = 128
 KW = K0 + W + R
 BIG = 8192.0
 GP = 2
 NKP = 4
+NVP = 4
 NBC = 4
-NSC = 2
-PAD = 24
+NSC = 1
+GH = 2
+RED = True
+PAD = 56
 YA = 8
-GAM, SCA, HOPX, HOPS, LAT = 1.56, 3.8, 260, 220, 3000
-PERIOD, STAG, SEED, TRIES, POLISH = 16000, 3500, 0, 2000, 400
+GAM, SCA, PEF, HOPX, HOPS, LAT = 1.65, 3.8, 0.5, 285, 220, 2800
+PERIOD, STAG, SEED, TRIES, SWAPS, PASSES = 15500, 2500, 0, 3000, 2000, 3
 
 SCRATCH = {}
 for _d, _l in (
-        ("float32", dict(kw=KW, pl=R, fs=2 * E, fold=E, pc=16, swp=128, rdum=R)),
-        ("bfloat16", dict(vw=W, yy=R, ib=128, nb=128, pb=128, tri=128, la=128, l2=128, zz=144, sel=16,
-                          ccol=144, gcol=128, kcol=128, ncol=16, qcol=64, ocol=64, bcol=128,
-                          tma=128, tmb=128, tmc=128, tmd=128, tme=128, tmf=128, tmg=128,
-                          kl=128, kr=64, one=128, crow=E, zero=C, rmax=EL // GP, dmask=C, offd=C, dgm=C)),
-        ("float16", dict(po=RO * R, ph=(RO + 1) * R, k16=5 * E, ih=128, boh=128)),
-        ("int32", dict(kraw=W, nraw=R, pi=8)), ("uint16", dict(pu=RO * R))):
+        ("float32", dict(kw=KW, pl=R, fs=E, fold=E, pc=16, rdum=R)),
+        ("bfloat16", dict(vw=2 * W, yy=R, ib=128, nb=128, pb=128, tri=128, la=128, l2=128, zz=144, sel=16,
+                          ccol=144, gcol=128, kcol=128, ncol=16, tma=128, tmb=128, tmc=128, tme=128, tmf=128, tmg=128,
+                          kr=128, one=128, crow=E, rmin=128, rmax=EL // GP, dmask=C, offd=C, offm=C, dgm=C)),
+        ("float16", dict(po=RO * R, pq=RO * R, ph=(RO + 1) * R, k16=5 * E, ih=128, boh=128)),
+        ("int32", dict(kraw=W, nraw=R, pi=8)), ("uint16", dict(pu=RO * R, pv=RO * R))):
     for _n, _w in _l.items():
         SCRATCH[_n] = ("sbuf", [128, _w], _d)
 for _t in range(RO):
     SCRATCH["yx%d" % _t] = ("sbuf", [128, 16 * R], "bfloat16")
 for _j in range(NCH):
-    for _n, _w, _d in (("kg", EL, "float16"), ("js", EL, "float16"), ("ge", EL, "bfloat16"), ("sf", 7 * C, "float32"),
-                       ("sh", 6 * C + PAD, "float16"), ("sb", 5 * C, "bfloat16"), ("su", 48, "uint16")):
+    for _n, _w, _d in (("vg", EL, "bfloat16"), ("mm", EL, "bfloat16"), ("kg", EL, "float16"), ("js", EL, "float16"),
+                       ("ge", EL, "bfloat16"), ("sf", 7 * C, "float32"), ("m0", C, "bfloat16"), ("oh", 128, "bfloat16"),
+                       ("sh", 4 * C + PAD, "float16"), ("sb", 7 * C, "bfloat16"), ("su", 48, "uint16")):
         SCRATCH["%s%d" % (_n, _j)] = ("sbuf", [128, _w], _d)
-    SCRATCH["vg%d" % _j] = ("sbuf", [128, EL], "bfloat16")
-    SCRATCH["mm%d" % _j] = ("sbuf", [128, EL], "bfloat16")
-    SCRATCH["oh%d" % _j] = ("sbuf", [128, 18, 8], "bfloat16")
 for _n in ["psy0", "psy1"] + ["ps%s%d" % (_a, _j) for _a in "xz" for _j in range(NCH)]:
-    SCRATCH[_n] = ("psum", [128, 512], "float32")
-SEMAPHORES = (["e_dve", "e_act", "e_pe", "e_pool", "sent", "d_val0", "d_val1", "d_nam", "d_seen", "d_yk"]
-              + ["d_clk%d" % i for i in range(NKP)] + ["d_yp%d" % j for j in range(NCH)]
+    SCRATCH[_n] = ("psum", [128, 32, 16] if RED and _n[2] == "z" else [128, 512], "float32")
+SEMAPHORES = (["e_dve", "e_act", "e_pe", "e_pool", "sent", "d_nam", "d_seen", "d_yk"]
+              + ["d_clk%d" % i for i in range(NKP)] + ["d_val%d" % i for i in range(NVP)] + ["d_yp%d" % j for j in range(NCH)]
               + ["a_%s%d_%d" % (a, t, j) for a, n in (("y", RO), ("p", RO + 1)) for t in range(1, n) for j in range(NCH)])
 A = AluOpType
 F = ActivationFunctionType
@@ -81,26 +81,26 @@ def build_ops():
     def scan(out, d0, d1, init, o0, o1, rd, wr, cost, bank=None):
         return dve(cost, lambda g, T, X: g.vector.tensor_tensor_scan(out(T), d0(T), d1(T), init, o0, o1), rd, wr, bank)
 
-    def act(out, a, rd, wr, cost, bank=None, bias=0.0, scale=1.0, slot=None):
-        return op("act", cost, lambda g, T, X: g.scalar.activation(out(T), a(T), F.Identity, bias=bias, scale=scale), rd, wr, bank,
-                  slot=slot)
+    def red(out, a, o, rd, wr, bank):
+        return dve(C, lambda g, T, X: g.vector.tensor_reduce(out(T), a(T), AxisListType.X, o), rd, wr, bank)
 
-    def mms(lst, rd, wr, bank, start=True, stop=True, mul=1):
+    def act(out, a, rd, wr, cost, bank=None, bias=0.0, scale=1.0, slot=None):
+        return op("act", cost, lambda g, T, X: g.scalar.activation(out(T), a(T), F.Identity, bias=val(bias, T), scale=scale),
+                  rd, wr, bank, slot=slot)
+
+    def mms(lst, rd, wr, bank, start=True, stop=True, solo=False):
         def fn(g, T, X):
             ins = None
             for i, (o, l, r, n) in enumerate(lst):
-                ins = g.tensor.matmul(o(T), l(T), r(T), start and i == 0, stop and i == len(lst) - 1)
+                ins = g.tensor.matmul(o(T), l(T), r(T), solo or (start and i == 0), solo or (stop and i == len(lst) - 1))
             return ins
-        return op("pe", mul * sum(max(64, m[3]) for m in lst), fn, rd, wr, bank)
+        return op("pe", PEF * sum(m[3] for m in lst), fn, rd, wr, bank)
 
     def mset(a, v, wr, cost=64, bank=None):
         dve(cost, lambda g, T, X: g.vector.memset(a(T), v), [], wr, bank)
 
-    def ap(name, a=None, b=None, s=None, p=128):
-        return lambda T: T[name][0:p, a:b:s]
-
-    def ap3(name, a, b, last):
-        return lambda T: T[name][:, a:b, last]
+    def ap(name, a=None, b=None, s=None, p=128, p0=0):
+        return lambda T: T[name][p0:p0 + p, a:b:s]
 
     def rev(a):
         return lambda T: a(T)[:, ::-1]
@@ -114,16 +114,20 @@ def build_ops():
     def send(de, so, hop, sem, rd, land, lat, after=None, slot=None):
         def fn(g, T, X):
             rid, pid, msk = X["dst"](hop, 0)
-            return g.remote_dma(de(T), so(T), T.sem[sem], T.sem.sent, pid, rid, msk)
+            if len(so) == 1:
+                return g.remote_dma(de(T), so[0](T), T.sem[sem], T.sem.sent, pid, rid, msk)
+            return g.remote_dma_fused([RemoteDMATransfer(dst_ids=[DstId(rid=rid, pnc=pid)], dma_engine_mask=msk, remote_sem=T.sem[sem],
+                                                         srcs=[s(T) for s in so], dsts=[de(T)], alu_op=2)], local_sem=T.sem.sent)
         s = op("pool", 600, fn, rd, [], sem="sent", after=after, slot=slot)
         op("net", 0, None, [], [land], sem=sem, val=16, after=s, lat=lat, slot=slot and slot + "n")
         return s
 
     dma("sp", ap("nraw"), ap("nam"), [], ["nraw"], "d_nam", 2400)
     dma("act", ap("yy"), ap("seen"), [], ["yy"], "d_seen", 2400)
-    dma("sp", ap("vw", 0, W // 2), ap("val", 0, W // 2), [], ["vwa"], "d_val0", 4500)
-    dma("act", ap("vw", W // 2, W), ap("val", W // 2, W), [], ["vwb"], "d_val1", 4500)
-    kp = W // NKP
+    vp, kp = W // NVP, W // NKP
+    for i in range(NVP):
+        dma(("sp", "act")[i % 2], ap("vw", i * vp, (i + 1) * vp), ap("val", i * vp, (i + 1) * vp), [], ["vw%d" % i], "d_val%d" % i,
+            3000 + 500 * i)
     for i in range(NKP):
         dma("sp", ap("kraw", i * kp, (i + 1) * kp), ap("clk", i * kp, (i + 1) * kp), [], ["kraw%d" % i], "d_clk%d" % i, 6000 + 1500 * i)
 
@@ -131,65 +135,60 @@ def build_ops():
         op("pool", 160 + 2 * n, lambda g, T, X: g.iota(T[name][:, 0:n], pat, base, 0, allow_small_or_imprecise_dtypes=True), [], [name])
     op("pool", 162, lambda g, T, X: g.iota(T.pi[:, 0:1], [[0, 1]], 0, 1), [], ["pi"])
     iota("ccol", 144, [[1, 144]])
-    iota("qcol", 64, [[0, 8], [1, 8]])
-    iota("ocol", 64, [[-1, 8], [0, 8]], 7)
-    iota("bcol", 128, [[0, 64], [8, 2]])
-    iota("gcol", 128, [[1, 8], [0, 16]])
     iota("kcol", 128, [[0, 8], [1, 16]])
+    iota("gcol", 128, [[1, 8], [0, 16]])
     iota("ncol", 16, [[16, 16]])
     M_ = float(MID)
-    mset(ap("zero"), 0.0, ["zero"])
+    mset(ap("rmin"), 0.0, ["rmin"])
     mset(ap("rmax"), 0.0, ["rmax"], EL // GP // 2)
-    mset(ap("rmax", 0, EL // GP, 16), -BIG, ["rmax"])
-    mset(ap("kw", 0, K0), -M_, ["kwlo"])
-    mset(ap("kw", K0 + W, KW), 0.0, ["kwhi"], R)
     mset(ap("rdum"), -4096.0, ["rdum"], R)
+    mset(ap("kw", 0, K0), -M_, ["kwlo"], K0)
+    mset(ap("kw", K0 + W, KW), 0.0, ["kwhi"], R)
     mset(ap("one", p=1), 1.0, ["one"])
     mset(ap("crow", p=1), 8 * M_, ["crow"], E // 2)
+    mset(ap("rmin", 0, 128, 16), 262144.0, ["rmin"])
+    mset(ap("rmax", 0, EL // GP, 16), -BIG, ["rmax"])
     for j in range(NCH):
-        mset(ap("sh%d" % j, 5 * C, 5 * C + PAD), -4096.0, ["fpad%d" % j])
-        mset(lambda T, j=j: T["oh%d" % j][:], 0.0, ["oh4%d" % j], 72)
-        mset(ap("psz%d" % j, 0, C), 0.0, ["m2%d" % j], C, "psz%d" % j)
-    cp(ap("pu", 0, R), ap("nraw"), ["nraw"], ["pu0_%d" % j for j in range(NCH)], R)
-    ts(ap("ph", 0, R), ap("nraw"), -M_, None, A.add, None, ["nraw"], ["ph0_%d" % j for j in range(NCH)], R)
-    for q in range(16):
-        dst = ap("yx0", q, 16 * R, 16)
-        if q < YA:
-            act(dst, ap("yy"), ["yy"], ["yx_%d" % q], 60 + R)
-        else:
-            cp(dst, ap("yy"), ["yy"], ["yx_%d" % q], R // 2)
-    YX0 = ["yx_%d" % q for q in range(16)]
+        mset(ap("sh%d" % j, 3 * C, 3 * C + PAD), -4096.0, ["fpad%d" % j])
     pi = lambda i: ap("pi", i, i + 1)
     pc = lambda i: ap("pc", i, i + 1)
     ts(pi(1), pi(0), 4, None, A.arith_shift_right, None, ["pi"], ["pi1"])
     ts(pi(2), pi(0), 15, None, A.bitwise_and, None, ["pi"], ["pi2"])
     ts(pi(5), pi(0), 1.0, None, A.add, None, ["pi"], ["pi5"])
-    ts(pi(4), pi(0), 1, None, A.bitwise_and, None, ["pi"], ["pi4"])
     ts(pi(3), pi(5), 15, None, A.bitwise_and, None, ["pi5"], ["pi3"])
-    cp(ap("pc", 0, 6), ap("pi", 0, 6), ["pi", "pi1", "pi2", "pi3", "pi4", "pi5"], ["pc"], 64)
+    cp(ap("pc", 0, 4), ap("pi", 0, 4), ["pi", "pi1", "pi2", "pi3"], ["pc"], 64)
     P_, G_, K_, S_ = pc(0), pc(1), pc(2), pc(3)
     EQm = (A.is_equal, A.mult)
-    ts(ap("pc", 8, 11), ap("ccol", 0, 3), P_, None, A.is_equal, None, ["pc", "ccol"], ["pc8"])
-    ts(pc(11), P_, 1.0, None, A.not_equal, None, ["pc"], ["pc11"])
+    ts(pc(8), K_, 0.0, float(W), *EQm, ["pc"], ["pc8"])
+    ts(ap("pv", 0, R), ap("nraw"), pc(8), None, A.add, None, ["nraw", "pc8"], ["pv0_%d" % j for j in range(NCH)], R)
+    for i in range(NVP):
+        ts(ap("vw", W + i * vp, W + (i + 1) * vp), ap("vw", i * vp, (i + 1) * vp), -256.0, None, A.add, None,
+           ["vw%d" % i], ["vx%d" % i], vp // 2)
+    VWK = ["v%s%d" % (a, i) for a in "wx" for i in range(NVP)]
+    for q in range(16):
+        dst = ap("yx0", q, 16 * R, 16)
+        if q < YA:
+            act(dst, ap("yy"), ["yy"], ["yx_%d" % q], 60 + R, bias=0.0 if q else -256.0)
+        else:
+            cp(dst, ap("yy"), ["yy"], ["yx_%d" % q], R // 2)
+    YX0 = ["yx_%d" % q for q in range(16)]
+    cp(ap("pu", 0, R), ap("nraw"), ["nraw"], ["pu0_%d" % j for j in range(NCH)], R)
+    ts(ap("ph", 0, R), ap("nraw"), -M_, None, A.add, None, ["nraw"], ["ph0_%d" % j for j in range(NCH)], R)
+    ts(pc(9), pc(8), M_, None, A.add, None, ["pc8"], ["pc9"])
     ts(pc(6), G_, 16.0, 15.0, A.mult, A.add, ["pc"], ["pc6"])
-    ts(pc(7), pc(4), -2.0, pc(5), A.mult, A.add, ["pc"], ["pc7"])
-    for i, v in enumerate((32.0, -16.0)):
+    for i, v in enumerate((16.0, -32.0)):
         ts(ap("sel", 8 * i, 8 * i + 8), ap("ccol", 0, 8), G_, v, *EQm, ["ccol", "pc"], ["sel%d" % i])
-    ts(ap("kl"), ap("bcol"), pc(9), pc(11), A.mult, A.add, ["bcol", "pc8", "pc11"], ["kl"])
-    ts(ap("tmd", 0, 64), ap("qcol"), pc(8), pc(9), A.mult, A.add, ["qcol", "pc8"], ["tmd0"])
-    ts(ap("tmd", 64, 128), ap("ocol"), pc(10), 131072.0, A.mult, A.mult, ["ocol", "pc8"], ["tmd1"])
-    tt(ap("kr"), ap("tmd", 0, 64), ap("tmd", 64, 128), A.add, ["tmd0", "tmd1"], ["kr"], 128)
-    c128 = ap("ccol", 0, 128)
-    ts(ap("swp"), c128, pc(7), None, A.is_equal, None, ["ccol", "pc7"], ["swp"], 128)
+    ts(ap("kr", p=1), ap("kcol", p=1), 0.0, 65536.0, A.not_equal, A.mult, ["kcol"], ["kr"])
     for name in ("ib", "ih"):
-        ts(ap(name), c128, P_, None, A.is_equal, None, ["ccol", "pc"], [name])
+        ts(ap(name), ap("ccol", 0, 128), P_, None, A.is_equal, None, ["ccol", "pc"], [name])
     for name, v in (("boh", 1.0), ("tma", 1.0), ("nb", -BIG), ("pb", BIG)):
         ts(ap(name), ap("gcol"), G_, v, *EQm, ["gcol", "pc"], [name])
     kc = ["kcol", "pc"]
     ts(ap("offd"), ap("kcol", 0, C), K_, BIG, A.not_equal, A.mult, kc, ["offd"])
     ts(ap("rdum", 0, R, 16), ap("ncol", 0, R // 16), K_, float(W - MID), A.add, A.add, ["ncol", "pc"], ["rdum"])
     ts(ap("zz"), ap("ccol"), pc(6), 0.25, *EQm, ["ccol", "pc6"], ["zz"], 72)
-    ts(ap("dmask"), ap("kcol", 0, C), K_, 30720.0, *EQm, kc, ["dmask"])
+    ts(ap("offm"), ap("offd"), M_ if RED else 0.0, None, A.max, None, ["offd"], ["offm"])
+    ts(ap("dmask"), ap("kcol", 0, C), K_, 30720.0 + (M_ + K0 if RED else 0.0), *EQm, kc, ["dmask"])
     ts(ap("dgm"), ap("offd"), -1.0, 4096.0, A.mult, A.add, ["offd"], ["dgm"])
     ts(ap("tmb"), ap("kcol"), K_, -BIG, A.is_gt, A.mult, kc, ["tmb"])
     ts(ap("tmc"), ap("kcol"), K_, BIG, *EQm, kc, ["tmc"])
@@ -210,8 +209,7 @@ def build_ops():
     def send_y(t, j, rd, after):
         n0 = R - C * (j + 1)
         part = lambda s: ap(s, 16 * n0, 16 * (n0 + C))
-        send(part("yx%d" % t), part("yx0"), HOP * t, "a_y%d_%d" % (t, j),
-             YX0 + rd, "y%d_%d" % (t, j), 3500, after, "y")
+        send(part("yx%d" % t), [part("yx0")], HOP * t, "a_y%d_%d" % (t, j), YX0 + rd, "y%d_%d" % (t, j), 3500, after, "y")
     for j in range(NCH):
         send_y(1, j, ["kraw%d" % (NKP - 1)], None)
 
@@ -226,60 +224,70 @@ def build_ops():
             pcs = lambda s: [s + "_%d" % i for i in range(GP)]
             vg, mm_, kg, js, ge = k("vg"), k("mm"), k("kg"), k("js"), k("ge")
             sf, sh, sb, su, px, pz = k("sf"), k("sh"), k("sb"), k("su"), k("psx"), k("psz")
-            oh = lambda a, b, s=1, j=j: (lambda T: T["oh%d" % j][:, a:b:s, :])
-            pu, ph = "pu%d_%d" % (t, j), "ph%d_%d" % (t, j)
+            pu, pv, ph = ("p%s%d_%d" % (a, t, j) for a in "uvh")
             yk = ["y%d_%d" % (t, j)] if t else YX0
             PC = ap("ph", c0, c0 + C)
-            FF, MB, S0, S1, S2, U1, U2s = (ap(sf, i * C, (i + 1) * C) for i in range(7))
+            S0, S1, S2, U1, U2s = (ap(sf, i * C, (i + 1) * C) for i in range(2, 7))
             last = lambda i, sf=sf: ap(sf, i * C + 15, (i + 1) * C, 16)
             XX, YY, KO = (ap(sh, i * C, (i + 1) * C) for i in range(3))
-            held = lambda d, sh=sh: ap(sh, 5 * C + PAD - d, 6 * C + PAD - d)
-            NE, OVER, HH, EQ1, EQ2 = (ap(sb, i * C, (i + 1) * C) for i in range(5))
-            KEY, OHT, CNT, BB, CC = (ap(px, i * C, (i + 1) * C) for i in range(5))
-            M2, O3, RR, GG = (ap(pz, i * C, (i + 1) * C) for i in range(4))
+            held = lambda d, sh=sh: ap(sh, 3 * C + PAD - d, 4 * C + PAD - d)
+            NE, OVER, HH = (ap(sb, i * C, (i + 1) * C) for i in range(3))
+            EQ = [ap(sb, i * C, (i + 1) * C) for i in range(3, 3 + NB // NSC)]
+            UA, UJ, OHT, CNT, BB, CC = (ap(px, i * C, (i + 1) * C) for i in range(2, 8))
+            O3, RR, B1, U2, U3 = (((lambda T, i=i, pz=pz: T[pz][:, 4 * i:4 * i + 4, :]) if RED else ap(pz, i * C, (i + 1) * C))
+                                  for i in range(5))
+            kp_, kw_ = C * GH, 128 // GH
+            KEY, RF, FF, OH = (ap(s, a, a + kw_, p=kp_) for s, a in ((px, 0), (px, 128), (sf, 0), (k("oh"), 0)))
             pc_ = lambda s, i: ap(s, i * ep, (i + 1) * ep)
-            off = lambda i: ap("pu", c0 + i * cq, c0 + (i + 1) * cq)
+            off = lambda i, s="pu": ap(s, c0 + i * cq, c0 + (i + 1) * cq)
             JJ = ap(js, 15, EL, 16)
 
             if t > 0:
-                act(ap("pu", c0, c0 + C), PC, [ph], [pu], 60 + C, bias=M_, slot="cvt")
+                act(ap("pv", c0, c0 + C), PC, [ph, "pc9"], [pv], 60 + C, bias=pc(9), slot="cvt")
+                ops[ts(ap("pu", c0, c0 + C), ap("pv", c0, c0 + C), pc(8), None, A.subtract, None, [pv, "pc8"], [pu])]["slot"] = (j, "cvu")
+                cur[2] = 0
             for i in range(GP):
-                act(pc_(vg, i), ind("vw", 0, W, off(i)), [pu, "vwa", "vwb"], [vg + "_%d" % i, vg + "f%d" % i], 80 + GAM * ep)
-            kk = lambda q: ap(px, q, C, 8)
-            col = lambda s, q: ap(s, q, EL, 8)
-            mms([(KEY, ap("kl", p=3), ap("kr", p=3), C)], ["kl", "kr"], [k("key")], px, True, False)
+                act(pc_(vg, i), ind("vw", 0, 2 * W, off(i, "pv")), [pv] + VWK, [vg + "_%d" % i], 80 + GAM * ep)
+            row = lambda s: [(KEY, ap("one", 0, kp_, p=1), ap(s, 0, kw_, p=1), kw_)]
+            mms(row("kcol"), ["one", "kcol"], [k("key")], px, True, False)
             yx = lambda a, b, s=1: ap("yx%d" % t, 16 * n0 + a, 16 * n0 + b, s)
-            pp = 128 // GP
+            ng = 8 // GH
             for i in range(GP):
                 a, b = i * ep, (i + 1) * ep
-                mms([(lambda T, i=i, px=px: T[px][i * pp:(i + 1) * pp, 0:C:8], ap(vg, a, b, 8), ap("sel", 8, 16), 8)],
-                    [vg + "_%d" % i, vg + "f%d" % i, "sel1"], [k("key")], px, False, False)
-                tt(ap(vg, a, b, 16), ap(vg, a, b, 16), yx(a, b, 16), A.max, [vg + "f%d" % i] + yk, [vg + "f%d" % i], 2 * cq)
-                scan(pc_(mm_, i), yx(a, b), pc_(vg, i), 0.0, A.min, A.max, [vg + "_%d" % i, vg + "f%d" % i] + yk, [mm_ + "_%d" % i], ep // 2)
-            mms([(kk(q), col(vg, q), ap("sel", 8, 16), 8) for q in range(1, 8)], pcs(vg) + ["sel1"], [k("key")], px, False, False)
-            mms([(kk(q), col(mm_, q), ap("sel", 0, 8), 8) for q in range(8)], pcs(mm_) + ["sel0"], [k("key")], px, False)
-            scan(FF, ap("zero"), KEY, 4194304.0, A.add, A.min, [k("key"), "zero"], [k("ff")], C, px)
-            mms([(ap(pz, 7, C, 8), ap("swp"), ap(sf, 7, C, 8), 8)], [k("ff"), "swp"], [k("m2")], pz, True, mul=4)
-            scan(rev(MB), rev(M2), rev(FF), 0.0, A.max, A.min, [k("ff"), k("m2")], [k("mb")], C, pz)
-            tt(oh(2, 18, 2), KEY, MB, A.is_equal, [k("key"), k("mb")], [k("oh4")], C, px)
-            mms([(RR, ap("ib"), ap("offd"), C)], ["ib", "offd"], [k("rr")], pz, True, False)
-            mms([(OHT, oh(2, 18), ap("ib", 0, 128, 2), C), (OHT, oh(1, 17), ap("ib", 1, 128, 2), C)], [k("oh4"), "ib"], [k("oht")], px)
+                m0 = ap(k("m0"), i * cq, (i + 1) * cq)
+                sums = lambda src, s0: [(ap(px, q, kw_, 16, cq, C * h + cq * i), src(q), ap("sel", s0 + ng * h, s0 + ng * (h + 1)), cq)
+                                        for h in range(GH) for q in range(16)]
+                mms(sums(lambda q: ap(vg, a + q, b, 16), 0), [vg + "_%d" % i, "sel0"], [k("key")], px, False, False)
+                tt(m0, ap(vg, a, b, 16), yx(a, b, 16), A.min, [vg + "_%d" % i] + yk, [k("m0") + "_%d" % i], 2 * cq)
+                scan(pc_(mm_, i), yx(a, b), pc_(vg, i), 0.0, A.max, A.min, [vg + "_%d" % i] + yk, [mm_ + "_%d" % i], ep // 2)
+                mms(sums(lambda q: ap(mm_, a + q, b, 16) if q else m0, 8) + (row("kr") if i == GP - 1 else []),
+                    [mm_ + "_%d" % i, k("m0") + "_%d" % i, "sel1", "kr"], [k("key")], px, False, i == GP - 1)
+            rst = ap("rmin", 0, kw_, p=kp_)
+            scan(FF, rst, KEY, 0.0, A.add, A.min, [k("key"), "rmin"], [k("ff")], kw_, px)
+            scan(rev(RF), rst, rev(KEY), 0.0, A.add, A.min, [k("key"), "rmin"], [k("rf")], kw_, px)
+            tt(OH, RF, FF, A.is_equal, [k("ff"), k("rf")], [k("oh")], kw_, px)
+            mms([(RR, ap("ib"), ap("offm"), C)], ["ib", "offm"], [k("rr")], pz, True, False)
+            mms([(ap(px, 4 * C, 5 * C, 1, kw_, kw_ * h), OH, ap("ib", C * h, C * (h + 1), p=kp_), C) for h in range(GH)],
+                [k("oh"), "ib"], [k("oht")], px, solo=True)
             tt(XX, OHT, PC, A.mult, [k("oht"), ph], [k("xx")], C, px)
             act(HH, OHT, [k("oht")], [k("hh")], 60 + C, px, bias=-2048.0, scale=16384.0)
             mms([(RR, ap("boh"), XX, C)], [k("xx"), "boh"], [k("rr")], pz, False)
             rd_ = ap("rdum", n0, n0 + C)
-            scan(S0, rd_, RR, -4096.0, A.max, A.min, [k("rr"), "rdum"], [k("s0")], C, pz)
-            ts(ap(su, 0, NB), last(2), M_, None, A.add, None, [k("s0")], [k("ob")])
+            if RED:
+                red(ap(su, 0, NB), RR, A.min, [k("rr")], [k("ob")], pz)
+            else:
+                scan(S0, rd_, RR, -4096.0, A.max, A.min, [k("rr"), "rdum"], [k("s0")], C, pz)
+                ts(ap(su, 0, NB), last(2), M_, None, A.add, None, [k("s0")], [k("ob")])
             mms([(O3, ap("boh"), XX, C)], [k("xx"), "boh"], [k("o3")], pz)
             tt(NE, O3, PC, A.not_equal, [k("o3"), ph], [k("ne")], C, pz)
-            mms([(GG, ap("ih"), PC, C)], [ph, "ih"], [k("gg")], pz, True, False)
+            mms([(B1, ap("ib"), ap("dmask"), C), (U2, ap("l2"), HH, C)], ["ib", "dmask", k("hh"), "l2"], [k("b1")], pz, True, False)
             for i in range(GP):
                 act(pc_(kg, i), ind("kw", K0, KW, off(i)), [pu] + KWK, [kg + "_%d" % i], 80 + GAM * ep)
             cp(KO, ind("kw", K0, KW, ap(su, 0, NB)), [k("ob")] + KWK, [k("ko")], 60 + GAM * C)
             for i in range(GP):
                 scan(pc_(js, i), ap("rmax"), pc_(kg, i), 0.0, A.add, A.max, [kg + "_%d" % i, "rmax"], [js + "_%d" % i], ep // 2)
             b = "psy%d" % ((t * NCH + j) % 2)
-            B1, U2, UA, UJ, U3 = (ap(b, i * C, (i + 1) * C) for i in range(5))
+            GG = ap(b, 0, C)
             mms([(ap(b, q, NBC * C, NBC), ap("ih"), KO, C) for q in range(NBC)], [k("ko"), "ih"], [b], b)
             NP = 16 // NBC
             for r in range(NP):
@@ -287,34 +295,37 @@ def build_ops():
             for r in range(NP):
                 mms([(CNT, ap("zz", 15 - q, 143 - q), ap(ge, q, EL, 16), C) for q in range(r, 16, NP)],
                     [ge + "_%d" % r, "zz"], [k("cnt")], px, r == 0, r == NP - 1)
-            mms([(B1, ap("ib"), ap("dmask"), C), (U2, ap("l2"), HH, C)], ["ib", "dmask", k("hh"), "l2"], [b], b, True, False)
-            mms([(UA, ap("la"), HH, C), (UJ, ap("ih"), JJ, C)], pcs(js) + ["ih", k("hh"), "la"], [b], b, False, False)
+            mms([(GG, ap("ih"), PC, C)], [ph, "ih"], [b], b, True, False)
             tt(OVER, CNT, NE, A.is_lt, [k("cnt"), k("ne")], [k("over")], C, px)
             ov = k("over")
             own = lambda o: [(o, ap("ib"), ap("offd"), C), (o, ap("boh"), XX, C), (o, ap("pb"), OVER, C)]
             ownk = [ov, k("xx"), "ib", "offd", "boh", "pb"]
-            mms([(GG, ap("tri"), OVER, C)], [ov, "tri"], [k("gg")], pz, False)
-            mms(own(BB), ownk, [k("bb")], px)
-            mms([(UA, ap("nb"), OVER, C), (UJ, ap("nb"), OVER, C)], [ov, "nb"], [b], b, False, False)
-            ts(YY, GG, -BIG, -2048.0, A.add, A.max, [k("gg")], [k("yy_")], C, pz)
-            mms([(B1, ap("boh"), YY, C), (U2, ap("boh"), YY, C)], [k("yy_"), "boh"], [b], b, False)
+            mms([(GG, ap("tri"), OVER, C)], [ov, "tri"], [b], b, False)
+            mms(own(BB) + [(UA, ap("la"), HH, C), (UJ, ap("ih"), JJ, C), (UA, ap("nb"), OVER, C), (UJ, ap("nb"), OVER, C)],
+                ownk + pcs(js) + ["ih", k("hh"), "la", "nb"], [k("bb")], px)
+            ts(YY, GG, -BIG, -2048.0, A.add, A.max, [b], [k("yy_")], C, b)
+            mms([(B1, ap("boh"), YY, C), (U2, ap("boh"), YY, C)], [k("yy_"), "boh"], [k("b1")], pz, False)
             scan(held(0), ap("dgm"), BB, -4096.0, A.max, A.min, [k("bb"), "dgm"], [k("fd")], C, px)
+            tt(U1, UA, PC, A.min, [k("bb"), ph], [k("u1")], C, px)
+            tt(U2s, UJ, U1, A.max, [k("bb"), k("u1")], [k("u2s")], C, px)
             mms(own(CC), ownk, [k("cc")], px, True, False)
-            tt(EQ1, O3, held(1), A.is_equal, [k("o3"), k("fd"), k("fpad")], [k("eq1")], C, pz)
-            tt(EQ2, O3, held(17), A.is_equal, [k("o3"), k("fd"), k("fpad")], [k("eq2")], C, pz)
-            scan(S1, ap("rmax", 0, C), B1, 0.0, A.add, A.max, [b, "rmax"], [k("s1")], C, b)
-            tt(U1, UA, PC, A.min, [b, ph], [k("u1")], C, b)
-            ts(ap(su, 16, 16 + NB), last(3), M_ + K0, None, A.add, None, [k("s1")], [k("pfo")])
-            tt(U2s, UJ, U1, A.max, [b, k("u1")], [k("u2s")], C, b)
-            tt(U3, U2, U2s, A.max, [b, k("u2s")], [k("u3")], C, b)
-            tt(YY, ind("kw", 0, KW, ap(su, 16, 16 + NB)), HH, A.min, [k("pfo"), k("hh")] + KWK, [k("yy_")], 60 + GAM * C)
-            so = ap("po", c0, c0 + C); de = ap("ph", c0 + R, c0 + R + C)
-            tt(so, U3, YY, A.max, [k("yy_"), k("u3")], ["po%d_%d" % (t, j)], C, b)
+            if RED:
+                red(ap(su, 16, 16 + NB), B1, A.max, [k("b1")], [k("pfo")], pz)
+            else:
+                scan(S1, ap("rmax", 0, C), B1, 0.0, A.add, A.max, [k("b1"), "rmax"], [k("s1")], C, pz)
+                ts(ap(su, 16, 16 + NB), last(3), M_ + K0, None, A.add, None, [k("s1")], [k("pfo")])
+            for i, e in enumerate(EQ):
+                tt(e, O3, held(16 * i + 1), A.is_equal, [k("o3"), k("fd"), k("fpad")], [k("eq") + "_%d" % i], C, pz)
+            so = [ap(s, c0, c0 + C) for s in ("po", "pq")]
+            sk = ["p%s%d_%d" % (s, t, j) for s in "oq"]
+            de = ap("ph", c0 + R, c0 + R + C)
+            tt(so[0], U2, U2s, A.max, [k("b1"), k("u2s")], sk[:1], C, pz)
+            tt(so[1], ind("kw", 0, KW, ap(su, 16, 16 + NB)), HH, A.min, [k("pfo"), k("hh")] + KWK, sk[1:], 60 + GAM * C)
             land = "ph%d_%d" % (t + 1, j)
-            s = send(de, so, HOP if t < RO - 1 else -HOP * t, "a_p%d_%d" % (t + 1, j), ["po%d_%d" % (t, j)], land, LAT - 600)
+            s = send(de, so, HOP if t < RO - 1 else -HOP * t, "a_p%d_%d" % (t + 1, j), sk, land, LAT - 600)
             if t + 2 < RO:
                 send_y(t + 2, j, [], s)
-            mms([(CC, ap("pb"), EQ1, C), (CC, ap("pb"), EQ2, C)], [k("eq1"), k("eq2"), "pb"], [k("cc")], px, False)
+            mms([(CC, ap("pb"), e, C) for e in EQ], [k("eq") + "_%d" % i for i in range(len(EQ))] + ["pb"], [k("cc")], px, False)
             scan(S2, rd_, CC, -4096.0, A.max, A.min, [k("cc"), "rdum"], [k("s2")], C, px)
             ts(ap(su, 32, 32 + NB), last(4), M_, None, A.add, None, [k("s2")], [k("tg")])
             if t == RO - 1:
@@ -340,8 +351,8 @@ def build_ops():
             cp(dst, blk(b), KWK, ["k16_%d" % b], E)
         mms([(ps, ap("ih"), dst, E)], ["k16_%d" % b, "ih"], ["psy0"], "psy0", False, b == 4)
     tt(ap("psy1", 0, E), blk(5), blk(6), A.add, KWK, ["psy1"], 2 * E, "psy1")
-    tt(ap("fs", 0, E), ap("psy1", 0, E), blk(7), A.add, KWK + ["psy1"], ["fs1"], E, "psy1")
-    tt(ap("fold"), ps, ap("fs", 0, E), A.add, ["psy0", "fs1"], ["fold"], E, "psy0")
+    tt(ap("fs"), ap("psy1", 0, E), blk(7), A.add, KWK + ["psy1"], ["fs"], E, "psy1")
+    tt(ap("fold"), ps, ap("fs"), A.add, ["psy0", "fs"], ["fold"], E, "psy0")
     dma("sp", ap("yk"), ap("fold"), ["fold"], [], "d_yk", 2400)
     return ops
 
@@ -368,25 +379,88 @@ def search(ops, justify, span, pred):
     bs = cs = span(best)
     for it in range(TRIES):
         o2 = off.copy()
-        m = rng.integers(3)
+        m = rng.integers(4)
+        a = rng.integers(0, len(o2))
         if m == 0:
-            o2 += rng.normal(0, 300, len(o2))
+            o2 += rng.normal(0, 150, len(o2))
         elif m == 1:
-            o2[rng.integers(0, len(o2), 6)] += rng.normal(0, 2500, 6)
+            o2[rng.integers(0, len(o2), 3)] += rng.normal(0, 1500, 3)
         else:
-            a = rng.integers(0, len(o2))
-            o2[a:a + rng.integers(1, 30)] += rng.normal(0, 2000)
+            o2[a:a + rng.integers(1, 30 * (m - 1))] += rng.normal(0, 1500 if m == 2 else 400)
         st = justify(keys(o2))
         s = span(st)
-        if s <= cs + 150 * rng.random():
+        if s <= cs + 150 * (1 - it / TRIES) * rng.exponential():
             off, cs = o2, s
         if s < bs:
             best, bs = st, s
-    for it in range(POLISH):
-        v = rng.random(n) * (100.0, 300.0, 1000.0)[it % 3]
-        st = justify([best[x] + float(v[x]) for x in range(n)])
-        if span(st) <= bs:
-            best, bs = st, span(st)
+    return best
+
+
+def improve(start, eng, cost, tail, pred, nxt, seed):
+    n = len(start)
+    rng = np.random.default_rng(seed)
+    seq = sorted(range(n), key=lambda y: (start[y], y))
+    before, after, lastq = [-1] * n, [-1] * n, {}
+    for x in seq:
+        if eng[x] != "net":
+            before[x] = lastq.get(eng[x], -1)
+            if before[x] >= 0:
+                after[before[x]] = x
+            lastq[eng[x]] = x
+    direct = [set(d for d, g in pred[x]) for x in range(n)]
+    head, rdy, rest, dep = [0.0] * n, [0.0] * n, [0.0] * n, [0.0] * n
+    tabu, best, bs = {}, None, 1e18
+    for it in range(SWAPS):
+        for x in seq:
+            t = 0.0
+            for d, g in pred[x]:
+                if head[d] + cost[d] + g > t:
+                    t = head[d] + cost[d] + g
+            rdy[x] = t
+            p = before[x]
+            head[x] = head[p] + cost[p] if p >= 0 and head[p] + cost[p] > t else t
+        for x in reversed(seq):
+            t = tail[x]
+            for s, g in nxt[x]:
+                if rest[s] + g > t:
+                    t = rest[s] + g
+            dep[x] = t
+            s = after[x]
+            rest[x] = cost[x] + (rest[s] if s >= 0 and rest[s] > t else t)
+        span = max(head[x] + rest[x] for x in seq) - 1e-6
+        if span < bs:
+            best, bs = list(head), span
+        pick, pv = None, 1e18
+        for u in seq:
+            v = after[u]
+            if (v < 0 or head[u] + rest[u] < span or head[v] + rest[v] < span or head[v] > head[u] + cost[u] + 1e-6
+                    or u in direct[v]):
+                continue
+            p, s = before[u], after[v]
+            hv = max(rdy[v], head[p] + cost[p] if p >= 0 else 0.0)
+            ru = cost[u] + max(dep[u], rest[s] if s >= 0 else 0.0)
+            est = max(hv + cost[v] + max(dep[v], ru), max(rdy[u], hv + cost[v]) + ru) + 40.0 * rng.random()
+            if tabu.get((v, u), -1) > it and est >= bs:
+                est += 1e6
+            if est < pv:
+                pick, pv = (u, v), est
+        if pick is None:
+            break
+        u, v = pick
+        tabu[(u, v)] = it + 8 + int(rng.integers(12))
+        p, s = before[u], after[v]
+        before[v], after[v], before[u], after[u] = p, u, v, s
+        if p >= 0:
+            after[p] = v
+        if s >= 0:
+            before[s] = u
+        a, b = seq.index(u), seq.index(v)
+        late = {u}
+        for x in seq[a + 1:b]:
+            if before[x] in late or not late.isdisjoint(direct[x]):
+                late.add(x)
+        mid = seq[a:b + 1]
+        seq[a:b + 1] = [x for x in mid if x not in late] + [x for x in mid if x in late]
     return best
 
 
@@ -435,19 +509,21 @@ def plan_program():
         for d, gp in pred[x]:
             nxt[d].append((x, gp))
 
-    def place(key, before, after, head):
-        left = [len(p) for p in before]
+    def place(key, before, head, serial):
+        key = list(key)
+        for x in serial:
+            for d, gp in before[x]:
+                if key[d] >= key[x]:
+                    key[x] = key[d] + 1e-3
         start = [0.0] * n
-        busy = {}
-        cand = [x for x in range(n) if left[x] == 0]
-        while cand:
-            x = min(cand, key=lambda y: key[y])
-            cand.remove(x)
+        busy = {e: [] for e in eng}
+        for x in sorted(serial, key=lambda y: key[y]):
             t = head[x]
             for d, gp in before[x]:
-                t = max(t, start[d] + cost[d] + gp)
+                if start[d] + cost[d] + gp > t:
+                    t = start[d] + cost[d] + gp
             if eng[x] != "net":
-                lst = busy.setdefault(eng[x], [])
+                lst = busy[eng[x]]
                 i = len(lst)
                 while i > 0 and lst[i - 1][1] > t:
                     i -= 1
@@ -456,22 +532,20 @@ def plan_program():
                     i += 1
                 lst.insert(i, (t, t + cost[x]))
             start[x] = t
-            for s, gp in after[x]:
-                left[s] -= 1
-                if left[s] == 0:
-                    cand.append(s)
         return start
-    zero = [0.0] * n
+    zero, fw = [0.0] * n, list(range(n))
 
     def span(st):
-        return max(st[x] + cost[x] + tail[x] for x in range(n))
+        return max(st[x] + cost[x] + tail[x] for x in fw)
 
     def justify(key):
-        st = place(key, pred, nxt, zero)
-        bk = place([-(st[x] + cost[x]) for x in range(n)], nxt, pred, tail)
-        st2 = place([-(bk[x] + cost[x]) for x in range(n)], pred, nxt, zero)
+        st = place(key, pred, zero, fw)
+        bk = place([-(st[x] + cost[x]) for x in fw], nxt, tail, fw[::-1])
+        st2 = place([-(bk[x] + cost[x]) for x in fw], pred, zero, fw)
         return st2 if span(st2) <= span(st) else st
     best = search(ops, justify, span, pred)
+    for i in range(PASSES):
+        best = justify(improve(best, eng, cost, tail, pred, nxt, i))
     order, pos = {}, {}
     seq = sorted(range(n), key=lambda y: (best[y], y))
     for x in seq:

@@ -15,22 +15,24 @@ GP = 2
 NKP = 4
 NVP = 4
 NBC = 4
+JP = 4
+GEP = 2
+KCUT = (0, 1024, 2048, 2816, W)
 NSC = 1
-GH = 2
-RED = True
+GH = 1
 PAD = 56
 YA = 8
 GAM, SCA, PEF, HOPX, HOPS, LAT = 1.65, 3.8, 0.5, 285, 220, 2800
-PERIOD, STAG, SEED, TRIES, SWAPS, PASSES = 15500, 2500, 0, 3000, 2000, 3
+PERIOD, STAG, SEED, TRIES, SHAKES, SWAPS, PASSES = 15000, 2500, 0, 1800, 700, 800, 4
 
 SCRATCH = {}
 for _d, _l in (
-        ("float32", dict(kw=KW, pl=R, fs=E, fold=E, pc=16, rdum=R)),
+        ("float32", dict(kw=KW, pl=R, pof=R, pqf=R, fs=E, fold=E, pc=16, rdum=R, i32=128)),
         ("bfloat16", dict(vw=2 * W, yy=R, ib=128, nb=128, pb=128, tri=128, la=128, l2=128, zz=144, sel=16,
-                          ccol=144, gcol=128, kcol=128, ncol=16, tma=128, tmb=128, tmc=128, tme=128, tmf=128, tmg=128,
+                          ccol=144, gcol=128, kcol=128, ncol=16, tma=128, tmb=128, rows=1024,
                           kr=128, one=128, crow=E, rmin=128, rmax=EL // GP, dmask=C, offd=C, offm=C, dgm=C)),
-        ("float16", dict(po=RO * R, pq=RO * R, ph=(RO + 1) * R, k16=5 * E, ih=128, boh=128)),
-        ("int32", dict(kraw=W, nraw=R, pi=8)), ("uint16", dict(pu=RO * R, pv=RO * R))):
+        ("float16", dict(ph=RO * R, k16=5 * E, ih=128, boh=128)),
+        ("int32", dict(kraw=K0 + W, nraw=R, pi=8)), ("uint16", dict(pu=RO * R, pv=RO * R, po=RO * R, pq=RO * R))):
     for _n, _w in _l.items():
         SCRATCH[_n] = ("sbuf", [128, _w], _d)
 for _t in range(RO):
@@ -41,7 +43,7 @@ for _j in range(NCH):
                        ("sh", 4 * C + PAD, "float16"), ("sb", 7 * C, "bfloat16"), ("su", 48, "uint16")):
         SCRATCH["%s%d" % (_n, _j)] = ("sbuf", [128, _w], _d)
 for _n in ["psy0", "psy1"] + ["ps%s%d" % (_a, _j) for _a in "xz" for _j in range(NCH)]:
-    SCRATCH[_n] = ("psum", [128, 32, 16] if RED and _n[2] == "z" else [128, 512], "float32")
+    SCRATCH[_n] = ("psum", [128, 32, 16] if _n[2] == "z" else [128, 512], "float32")
 SEMAPHORES = (["e_dve", "e_act", "e_pe", "e_pool", "sent", "d_nam", "d_seen", "d_yk"]
               + ["d_clk%d" % i for i in range(NKP)] + ["d_val%d" % i for i in range(NVP)] + ["d_yp%d" % j for j in range(NCH)]
               + ["a_%s%d_%d" % (a, t, j) for a, n in (("y", RO), ("p", RO + 1)) for t in range(1, n) for j in range(NCH)])
@@ -124,12 +126,12 @@ def build_ops():
 
     dma("sp", ap("nraw"), ap("nam"), [], ["nraw"], "d_nam", 2400)
     dma("act", ap("yy"), ap("seen"), [], ["yy"], "d_seen", 2400)
-    vp, kp = W // NVP, W // NKP
+    vp = W // NVP
     for i in range(NVP):
         dma(("sp", "act")[i % 2], ap("vw", i * vp, (i + 1) * vp), ap("val", i * vp, (i + 1) * vp), [], ["vw%d" % i], "d_val%d" % i,
             3000 + 500 * i)
     for i in range(NKP):
-        dma("sp", ap("kraw", i * kp, (i + 1) * kp), ap("clk", i * kp, (i + 1) * kp), [], ["kraw%d" % i], "d_clk%d" % i, 6000 + 1500 * i)
+        dma("sp", ap("kraw", K0 + KCUT[i], K0 + KCUT[i + 1]), ap("clk", *KCUT[i:i + 2]), [], ["kraw%d" % i], "d_clk%d" % i, 4500 + 2 * KCUT[i + 1])
 
     def iota(name, n, pat, base=0):
         op("pool", 160 + 2 * n, lambda g, T, X: g.iota(T[name][:, 0:n], pat, base, 0, allow_small_or_imprecise_dtypes=True), [], [name])
@@ -148,8 +150,16 @@ def build_ops():
     mset(ap("crow", p=1), 8 * M_, ["crow"], E // 2)
     mset(ap("rmin", 0, 128, 16), 262144.0, ["rmin"])
     mset(ap("rmax", 0, EL // GP, 16), -BIG, ["rmax"])
+    mset(ap("kraw", 0, K0), 0, ["kpad"], K0)
     for j in range(NCH):
         mset(ap("sh%d" % j, 3 * C, 3 * C + PAD), -4096.0, ["fpad%d" % j])
+    rows = lambda i, s=1, a=0: ap("rows", 128 * i + a, 128 * (i + 1), s, p=1)
+    for i, v in enumerate((-99328.0, M_, 30720.0, -99328.0, M_, 30720.0, -123904.0, 32256.0)):
+        mset(rows(i), v, ["rows%d" % i])
+    for i, a, v in ((0, 0, -74752.0), (0, 1, -74752.0), (1, 0, M_ + W), (2, 0, 30720.0 + W), (2, 1, 30720.0 - W),
+                    (6, 0, -99328.0), (6, 1, -99328.0), (7, 0, 32256.0 + W), (7, 1, 32256.0 - W)):
+        mset(rows(i, 16, a), v, ["rows%d" % i])
+    ROWS = ["rows%d" % i for i in range(8)]
     pi = lambda i: ap("pi", i, i + 1)
     pc = lambda i: ap("pc", i, i + 1)
     ts(pi(1), pi(0), 4, None, A.arith_shift_right, None, ["pi"], ["pi1"])
@@ -174,36 +184,36 @@ def build_ops():
     YX0 = ["yx_%d" % q for q in range(16)]
     cp(ap("pu", 0, R), ap("nraw"), ["nraw"], ["pu0_%d" % j for j in range(NCH)], R)
     ts(ap("ph", 0, R), ap("nraw"), -M_, None, A.add, None, ["nraw"], ["ph0_%d" % j for j in range(NCH)], R)
-    ts(pc(9), pc(8), M_, None, A.add, None, ["pc8"], ["pc9"])
+    ts(pc(9), pc(8), -1.0, -M_, A.mult, A.add, ["pc8"], ["pc9"])
+    ts(pc(11), pc(8), -16384.0, None, A.add, None, ["pc8"], ["pc11"])
+    ts(pc(10), pc(11), M_, None, A.add, None, ["pc11"], ["pc10"])
     ts(pc(6), G_, 16.0, 15.0, A.mult, A.add, ["pc"], ["pc6"])
     for i, v in enumerate((16.0, -32.0)):
         ts(ap("sel", 8 * i, 8 * i + 8), ap("ccol", 0, 8), G_, v, *EQm, ["ccol", "pc"], ["sel%d" % i])
     ts(ap("kr", p=1), ap("kcol", p=1), 0.0, 65536.0, A.not_equal, A.mult, ["kcol"], ["kr"])
-    for name in ("ib", "ih"):
-        ts(ap(name), ap("ccol", 0, 128), P_, None, A.is_equal, None, ["ccol", "pc"], [name])
-    for name, v in (("boh", 1.0), ("tma", 1.0), ("nb", -BIG), ("pb", BIG)):
+    for name in ("ib", "ih", "i32"):
+        ts(ap(name), ap("ccol", 0, 128), P_, None, A.is_equal, None, ["ccol", "pc"], [name], 128 if name == "i32" else 64)
+    for name, v in (("boh", 1.0), ("nb", -BIG), ("pb", BIG)):
         ts(ap(name), ap("gcol"), G_, v, *EQm, ["gcol", "pc"], [name])
     kc = ["kcol", "pc"]
     ts(ap("offd"), ap("kcol", 0, C), K_, BIG, A.not_equal, A.mult, kc, ["offd"])
     ts(ap("rdum", 0, R, 16), ap("ncol", 0, R // 16), K_, float(W - MID), A.add, A.add, ["ncol", "pc"], ["rdum"])
     ts(ap("zz"), ap("ccol"), pc(6), 0.25, *EQm, ["ccol", "pc6"], ["zz"], 72)
-    ts(ap("offm"), ap("offd"), M_ if RED else 0.0, None, A.max, None, ["offd"], ["offm"])
-    ts(ap("dmask"), ap("kcol", 0, C), K_, 30720.0 + (M_ + K0 if RED else 0.0), *EQm, kc, ["dmask"])
+    ts(ap("offm"), ap("offd"), M_, None, A.max, None, ["offd"], ["offm"])
+    ts(ap("dmask"), ap("kcol", 0, C), K_, 30720.0 + M_ + K0, *EQm, kc, ["dmask"])
     ts(ap("dgm"), ap("offd"), -1.0, 4096.0, A.mult, A.add, ["offd"], ["dgm"])
-    ts(ap("tmb"), ap("kcol"), K_, -BIG, A.is_gt, A.mult, kc, ["tmb"])
-    ts(ap("tmc"), ap("kcol"), K_, BIG, *EQm, kc, ["tmc"])
-    ts(ap("tme"), ap("kcol"), S_, 0.5, *EQm, kc, ["tme"])
-    tt(ap("tmb"), ap("tmb"), ap("tmc"), A.add, ["tmb", "tmc"], ["tmb"], 256)
-    ts(ap("tmf"), ap("tme"), -1.4375, None, A.add, None, ["tme"], ["tmf"])
-    ts(ap("tmc"), ap("tmc"), -8.0 / BIG, -6.25, A.mult, A.add, ["tmc"], ["tmc"])
-    ts(ap("tmg"), ap("tme"), -16.0, None, A.mult, None, ["tme"], ["tmg"])
-    tt(ap("tri"), ap("tmb"), ap("tma"), A.mult, ["tmb", "tma"], ["tri"], 256)
-    tt(ap("l2"), ap("tmf"), ap("tma"), A.mult, ["tmf", "tma"], ["l2"], 256)
-    tt(ap("tmg"), ap("tmg"), ap("tmc"), A.add, ["tmg", "tmc"], ["tmg"], 256)
-    tt(ap("la"), ap("tmg"), ap("tma"), A.mult, ["tmg", "tma"], ["la"], 256)
+    def select(out, in_, how, fill):
+        op("pool", 460, lambda g, T, X: g.affine_select(T[out][:], T[in_][:], [[1, 128]], how, fill, 0, -1), [in_], [out])
+    ts(pc(7), G_, 16.0, S_, A.mult, A.add, ["pc"], ["pc7"])
+    ts(ap("l2"), ap("ccol", 0, 128), pc(7), None, A.is_equal, None, ["ccol", "pc7"], ["l2"])
+    ts(ap("tmb"), ap("ccol", 0, 128), pc(7), -8.0, *EQm, ["ccol", "pc7"], ["tmb"])
+    select("la", "tmb", A.not_equal, -8.0)
+    select("tma", "nb", A.is_gt, 0.0)
+    select("tri", "tma", A.not_equal, BIG)
     for i in range(NKP):
-        ts(ap("kw", K0 + i * kp, K0 + (i + 1) * kp), ap("kraw", i * kp, (i + 1) * kp), -M_, None, A.add, None,
-           ["kraw%d" % i], ["kwi%d" % i], kp)
+        part = lambda s: ap(s, K0 + KCUT[i], K0 + KCUT[i + 1])
+        ops[act(part("kw"), part("kraw"), ["kraw%d" % i], ["kwi%d" % i], 60 + KCUT[i + 1] - KCUT[i], bias=-M_)]["key"] = PERIOD + i
+    KRAW = ["kraw%d" % i for i in range(NKP)] + ["kpad"]
     KWK = ["kw", "kwlo", "kwhi"] + ["kwi%d" % i for i in range(NKP)]
 
     def send_y(t, j, rd, after):
@@ -233,9 +243,9 @@ def build_ops():
             held = lambda d, sh=sh: ap(sh, 3 * C + PAD - d, 4 * C + PAD - d)
             NE, OVER, HH = (ap(sb, i * C, (i + 1) * C) for i in range(3))
             EQ = [ap(sb, i * C, (i + 1) * C) for i in range(3, 3 + NB // NSC)]
-            UA, UJ, OHT, CNT, BB, CC = (ap(px, i * C, (i + 1) * C) for i in range(2, 8))
-            O3, RR, B1, U2, U3 = (((lambda T, i=i, pz=pz: T[pz][:, 4 * i:4 * i + 4, :]) if RED else ap(pz, i * C, (i + 1) * C))
-                                  for i in range(5))
+            OHT, CNT, BB, CC = (ap(px, i * C, (i + 1) * C) for i in range(4, 8))
+            O3, RR, B1, U2 = ((lambda T, i=i, pz=pz: T[pz][:, NB * i:NB * (i + 1), :]) for i in range(4))
+            end = t == RO - 1
             kp_, kw_ = C * GH, 128 // GH
             KEY, RF, FF, OH = (ap(s, a, a + kw_, p=kp_) for s, a in ((px, 0), (px, 128), (sf, 0), (k("oh"), 0)))
             pc_ = lambda s, i: ap(s, i * ep, (i + 1) * ep)
@@ -243,7 +253,7 @@ def build_ops():
             JJ = ap(js, 15, EL, 16)
 
             if t > 0:
-                act(ap("pv", c0, c0 + C), PC, [ph, "pc9"], [pv], 60 + C, bias=pc(9), slot="cvt")
+                act(PC, ap("pv", c0, c0 + C), [pv, "pc9"], [ph], 60 + C, bias=pc(9), slot="cvt")
                 ops[ts(ap("pu", c0, c0 + C), ap("pv", c0, c0 + C), pc(8), None, A.subtract, None, [pv, "pc8"], [pu])]["slot"] = (j, "cvu")
                 cur[2] = 0
             for i in range(GP):
@@ -270,59 +280,68 @@ def build_ops():
             mms([(ap(px, 4 * C, 5 * C, 1, kw_, kw_ * h), OH, ap("ib", C * h, C * (h + 1), p=kp_), C) for h in range(GH)],
                 [k("oh"), "ib"], [k("oht")], px, solo=True)
             tt(XX, OHT, PC, A.mult, [k("oht"), ph], [k("xx")], C, px)
-            act(HH, OHT, [k("oht")], [k("hh")], 60 + C, px, bias=-2048.0, scale=16384.0)
+            act(HH, OHT, [k("oht"), "pc10"], [k("hh")], 60 + C, px, bias=M_ - 16384.0 if end else pc(10 if t else 11), scale=16384.0)
             mms([(RR, ap("boh"), XX, C)], [k("xx"), "boh"], [k("rr")], pz, False)
             rd_ = ap("rdum", n0, n0 + C)
-            if RED:
-                red(ap(su, 0, NB), RR, A.min, [k("rr")], [k("ob")], pz)
-            else:
-                scan(S0, rd_, RR, -4096.0, A.max, A.min, [k("rr"), "rdum"], [k("s0")], C, pz)
-                ts(ap(su, 0, NB), last(2), M_, None, A.add, None, [k("s0")], [k("ob")])
+            red(ap(su, 0, NB), RR, A.min, [k("rr")], [k("ob")], pz)
             mms([(O3, ap("boh"), XX, C)], [k("xx"), "boh"], [k("o3")], pz)
             tt(NE, O3, PC, A.not_equal, [k("o3"), ph], [k("ne")], C, pz)
-            mms([(B1, ap("ib"), ap("dmask"), C), (U2, ap("l2"), HH, C)], ["ib", "dmask", k("hh"), "l2"], [k("b1")], pz, True, False)
-            for i in range(GP):
-                act(pc_(kg, i), ind("kw", K0, KW, off(i)), [pu] + KWK, [kg + "_%d" % i], 80 + GAM * ep)
-            cp(KO, ind("kw", K0, KW, ap(su, 0, NB)), [k("ob")] + KWK, [k("ko")], 60 + GAM * C)
-            for i in range(GP):
-                scan(pc_(js, i), ap("rmax"), pc_(kg, i), 0.0, A.add, A.max, [kg + "_%d" % i, "rmax"], [js + "_%d" % i], ep // 2)
+            lift = lambda o, i: (o, rows(((6, 1, 7), (0, 1, 2), (0, 1, 2), (3, 4, 5))[t][i]), ap("one", 0, C, p=1), C)
+            mms([(B1, ap("ib"), ap("dmask"), C), (U2, ap("l2"), HH, C), lift(U2, 2)], ["ib", "dmask", k("hh"), "l2", "one"] + ROWS,
+                [k("b1")], pz, True, False)
+            if t > 0:
+                for i in range(GP):
+                    act(pc_(kg, i), ind("kw", K0, KW, off(i)), [pu] + KWK, [kg + "_%d" % i], 80 + GAM * ep)
+                cp(KO, ind("kw", K0, KW, ap(su, 0, NB)), [k("ob")] + KWK, [k("ko")], 60 + GAM * C)
+            else:
+                for i in range(GP):
+                    if j == 0 and i == GP - 1:
+                        ts(pc_(kg, i), ind("kraw", K0, K0 + W, off(i)), -M_, None, A.add, None, [pu] + KRAW, [kg + "_%d" % i], 60 + GAM * ep)
+                    else:
+                        act(pc_(kg, i), ind("kraw", K0, K0 + W, off(i)), [pu] + KRAW, [kg + "_%d" % i], 80 + GAM * ep, bias=-M_)
+                ts(KO, ind("kraw", K0, K0 + W, ap(su, 0, NB)), -M_, None, A.add, None, [k("ob")] + KRAW, [k("ko")], 60 + GAM * C)
+            ej = EL // JP
+            for i in range(JP):
+                scan(ap(js, i * ej, (i + 1) * ej), ap("rmax", 0, ej), ap(kg, i * ej, (i + 1) * ej), 0.0, A.add, A.max,
+                     [kg + "_%d" % (i * GP // JP), "rmax"], [js + "_%d" % i], ej // 2)
             b = "psy%d" % ((t * NCH + j) % 2)
-            GG = ap(b, 0, C)
+            GG, UA, UJ = (ap(b, i * C, (i + 1) * C) for i in range(3))
             mms([(ap(b, q, NBC * C, NBC), ap("ih"), KO, C) for q in range(NBC)], [k("ko"), "ih"], [b], b)
             NP = 16 // NBC
-            for r in range(NP):
-                tt(ap(ge, r, EL, NP), ap(kg, r, EL, NP), ap(b, 0, NBC * C), A.is_lt, pcs(kg) + [b], [ge + "_%d" % r], NBC * C, b)
-            for r in range(NP):
-                mms([(CNT, ap("zz", 15 - q, 143 - q), ap(ge, q, EL, 16), C) for q in range(r, 16, NP)],
-                    [ge + "_%d" % r, "zz"], [k("cnt")], px, r == 0, r == NP - 1)
-            mms([(GG, ap("ih"), PC, C)], [ph, "ih"], [b], b, True, False)
+            cg = C // GEP
+            passes = [(i, r) for i in range(GEP) for r in range(NP)]
+            for i, r in passes:
+                cols = lambda s: ap(s, 16 * cg * i + r, 16 * cg * (i + 1), NP)
+                tt(cols(ge), cols(kg), ap(b, NBC * cg * i, NBC * cg * (i + 1)), A.is_lt, (pcs(kg) if GEP == 1 else [kg + "_%d" % i]) + [b],
+                   [ge + "_%d_%d" % (i, r)], NBC * cg, b)
+            for i, r in passes:
+                mms([(ap(px, 5 * C + cg * i, 5 * C + cg * (i + 1)), ap("zz", 15 - q, 143 - q), ap(ge, 16 * cg * i + q, 16 * cg * (i + 1), 16), C)
+                     for q in range(r, 16, NP)], [ge + "_%d_%d" % (i, r), "zz"], [k("cnt")], px, (i, r) == passes[0], (i, r) == passes[-1])
+            mms([(GG, ap("ih"), PC, C), (UA, ap("la"), HH, C), lift(UA, 0), lift(UJ, 1), (UJ, ap("ih"), JJ, C)],
+                [ph, "ih", k("hh"), "la", "one"] + [js + "_%d" % i for i in range(JP)] + ROWS, [b], b, True, False)
             tt(OVER, CNT, NE, A.is_lt, [k("cnt"), k("ne")], [k("over")], C, px)
             ov = k("over")
             own = lambda o: [(o, ap("ib"), ap("offd"), C), (o, ap("boh"), XX, C), (o, ap("pb"), OVER, C)]
             ownk = [ov, k("xx"), "ib", "offd", "boh", "pb"]
-            mms([(GG, ap("tri"), OVER, C)], [ov, "tri"], [b], b, False)
-            mms(own(BB) + [(UA, ap("la"), HH, C), (UJ, ap("ih"), JJ, C), (UA, ap("nb"), OVER, C), (UJ, ap("nb"), OVER, C)],
-                ownk + pcs(js) + ["ih", k("hh"), "la", "nb"], [k("bb")], px)
+            mms([(GG, ap("tri"), OVER, C), (UA, ap("nb"), OVER, C), (UJ, ap("nb"), OVER, C)], [ov, "tri", "nb"], [b], b, False)
+            mms(own(BB), ownk, [k("bb")], px)
             ts(YY, GG, -BIG, -2048.0, A.add, A.max, [b], [k("yy_")], C, b)
             mms([(B1, ap("boh"), YY, C), (U2, ap("boh"), YY, C)], [k("yy_"), "boh"], [k("b1")], pz, False)
             scan(held(0), ap("dgm"), BB, -4096.0, A.max, A.min, [k("bb"), "dgm"], [k("fd")], C, px)
-            tt(U1, UA, PC, A.min, [k("bb"), ph], [k("u1")], C, px)
-            tt(U2s, UJ, U1, A.max, [k("bb"), k("u1")], [k("u2s")], C, px)
+            tt(U1, UA, ap("pu" if end else "pv", c0, c0 + C), A.min, [b, pu, pv], [k("u1")], C, b)
+            tt(U2s, UJ, U1, A.max, [b, k("u1")], [k("u2s")], C, b)
             mms(own(CC), ownk, [k("cc")], px, True, False)
-            if RED:
-                red(ap(su, 16, 16 + NB), B1, A.max, [k("b1")], [k("pfo")], pz)
-            else:
-                scan(S1, ap("rmax", 0, C), B1, 0.0, A.add, A.max, [k("b1"), "rmax"], [k("s1")], C, pz)
-                ts(ap(su, 16, 16 + NB), last(3), M_ + K0, None, A.add, None, [k("s1")], [k("pfo")])
+            red(ap(su, 16, 16 + NB), B1, A.max, [k("b1")], [k("pfo")], pz)
             for i, e in enumerate(EQ):
                 tt(e, O3, held(16 * i + 1), A.is_equal, [k("o3"), k("fd"), k("fpad")], [k("eq") + "_%d" % i], C, pz)
-            so = [ap(s, c0, c0 + C) for s in ("po", "pq")]
+            so = [ap(s + "f", n0, n0 + C) if end else ap(s, c0, c0 + C) for s in ("po", "pq")]
             sk = ["p%s%d_%d" % (s, t, j) for s in "oq"]
-            de = ap("ph", c0 + R, c0 + R + C)
+            de = ap("pl", n0, n0 + C) if end else ap("pv", c0 + R, c0 + R + C)
             tt(so[0], U2, U2s, A.max, [k("b1"), k("u2s")], sk[:1], C, pz)
-            tt(so[1], ind("kw", 0, KW, ap(su, 16, 16 + NB)), HH, A.min, [k("pfo"), k("hh")] + KWK, sk[1:], 60 + GAM * C)
-            land = "ph%d_%d" % (t + 1, j)
-            s = send(de, so, HOP if t < RO - 1 else -HOP * t, "a_p%d_%d" % (t + 1, j), sk, land, LAT - 600)
+            tt(so[1], ind("kw" if t else "kraw", 0, K0 + W, ap(su, 16, 16 + NB)), HH, A.add, [k("pfo"), k("hh")] + (KWK if t else KRAW),
+               sk[1:], 60 + GAM * C)
+            land = "pv%d_%d" % (t + 1, j)
+            s = send(de, so, -HOP * t if end else HOP, "a_p%d_%d" % (t + 1, j), sk, land, LAT - 600)
             if t + 2 < RO:
                 send_y(t + 2, j, [], s)
             mms([(CC, ap("pb"), e, C) for e in EQ], [k("eq") + "_%d" % i for i in range(len(EQ))] + ["pb"], [k("cc")], px, False)
@@ -330,26 +349,26 @@ def build_ops():
             ts(ap(su, 32, 32 + NB), last(4), M_, None, A.add, None, [k("s2")], [k("tg")])
             if t == RO - 1:
                 cur[0] = RO
-                act(ap("pl", n0, n0 + C), de, [land], [k("pl")], 60 + C, bias=M_)
-                dma("sp", ap("yp", n0, n0 + C), ap("pl", n0, n0 + C), [k("pl")], [], k("d_yp"), 2400)
+                dma("sp", ap("yp", n0, n0 + C), de, [land], [], k("d_yp"), 2400)
         cur[0], cur[1], cur[2] = t, NCH, 0
         nb_, ne = NB // NSC, EL // NSC
         for j in range(NCH):
             for h in reversed(range(NSC)):
                 cp(ind("kw", K0, KW, ap("su%d" % j, 32 + h * nb_, 32 + (h + 1) * nb_)), ap("js%d" % j, h * ne + 15, (h + 1) * ne, 16),
-                   ["tg%d" % j] + ["js%d_%d" % (j, i) for i in range(GP)], ["kw"], 60 + SCA * C / NSC)
+                   ["tg%d" % j] + ["js%d_%d" % (j, i) for i in range(JP)] + KWK[1:], ["kw"], 60 + SCA * C / NSC)
 
     cur[0], cur[1] = RO, 0
     blk = lambda b: ap("kw", K0 + b * E, K0 + (b + 1) * E)
     ps = ap("psy0", 0, E)
     mms([(ps, ap("one", p=1), ap("crow", p=1), E)], ["one", "crow"], ["psy0"], "psy0", True, False)
-    for b in range(5):
+    mms([(ps, ap("i32"), blk(4), 4 * E)], KWK + ["i32"], ["psy0"], "psy0", False, False)
+    for b in range(4):
         dst = ap("k16", b * E, (b + 1) * E)
         if b > 0:
             act(dst, blk(b), KWK, ["k16_%d" % b], 60 + E)
         else:
             cp(dst, blk(b), KWK, ["k16_%d" % b], E)
-        mms([(ps, ap("ih"), dst, E)], ["k16_%d" % b, "ih"], ["psy0"], "psy0", False, b == 4)
+        mms([(ps, ap("ih"), dst, E)], ["k16_%d" % b, "ih"], ["psy0"], "psy0", False, b == 3)
     tt(ap("psy1", 0, E), blk(5), blk(6), A.add, KWK, ["psy1"], 2 * E, "psy1")
     tt(ap("fs"), ap("psy1", 0, E), blk(7), A.add, KWK + ["psy1"], ["fs"], E, "psy1")
     tt(ap("fold"), ps, ap("fs"), A.add, ["psy0", "fs"], ["fold"], E, "psy0")
@@ -373,7 +392,7 @@ def search(ops, justify, span, pred):
             off[slots[ops[x]["slot"]]] = es[x] + (j * STAG if j < NCH else NCH * STAG + 8000)
 
     def keys(off):
-        return [(-1e6 + x if o["tag"][0] < 0 else 1e6 + x if o["tag"][0] >= RO else o["tag"][0] * PERIOD + float(off[slots[o["slot"]]]))
+        return [(o.get("key", -1e6 + x) if o["tag"][0] < 0 else 1e6 + x if o["tag"][0] >= RO else o["tag"][0] * PERIOD + float(off[slots[o["slot"]]]))
                 for x, o in enumerate(ops)]
     best = justify(keys(off))
     bs = cs = span(best)
@@ -391,6 +410,24 @@ def search(ops, justify, span, pred):
         s = span(st)
         if s <= cs + 150 * (1 - it / TRIES) * rng.exponential():
             off, cs = o2, s
+        if s < bs:
+            best, bs = st, s
+    return best
+
+
+def shake(start, justify, span, seed):
+    rng = np.random.default_rng(seed)
+    cur = best = start
+    cs = bs = span(start)
+    for it in range(SHAKES):
+        a = rng.random() * cs
+        b = a + (1500, 4000, 16000)[rng.integers(3)]
+        now = np.array(cur)
+        move = rng.normal(0, (150, 500, 1500)[rng.integers(3)], len(cur)) * ((now >= a) & (now < b) & (rng.random(len(cur)) < 0.3))
+        st = justify((now + move).tolist())
+        s = span(st)
+        if s <= cs + 60 * rng.exponential():
+            cur, cs = st, s
         if s < bs:
             best, bs = st, s
     return best
@@ -545,7 +582,7 @@ def plan_program():
         return st2 if span(st2) <= span(st) else st
     best = search(ops, justify, span, pred)
     for i in range(PASSES):
-        best = justify(improve(best, eng, cost, tail, pred, nxt, i))
+        best = justify(improve(shake(best, justify, span, i), eng, cost, tail, pred, nxt, i))
     order, pos = {}, {}
     seq = sorted(range(n), key=lambda y: (best[y], y))
     for x in seq:

import numpy as np
from concourse.bass import DstId, RemoteDMATransfer
from concourse.mybir import AluOpType, ActivationFunctionType, AxisListType

W, R, RO, HOP, E = 3072, 192, 4, 3, 384
C = 64
NCH = R // C
EL = 16 * C
NB = C // 16
MID = 1536
K0 = 128
KW = K0 + W + R
BIG = 8192.0
GP = 2
NKP = 4
NVP = 4
NBC = 4
JP = 4
GEP = 2
KCUT = (0, 1024, 2048, 2816, W)
NSC = 1
GH = 1
PAD = 56
YA = 8
GAM, SCA, PEF, HOPX, HOPS, LAT = 1.65, 3.8, 0.5, 285, 220, 2800
PERIOD, STAG, SEED, TRIES, SHAKES, SWAPS, PASSES = 15000, 2500, 0, 1800, 700, 800, 4

SCRATCH = {}
for _d, _l in (
        ("float32", dict(kw=KW, pl=R, pof=R, pqf=R, fs=E, fold=E, pc=16, rdum=R, i32=128)),
        ("bfloat16", dict(vw=2 * W, yy=R, ib=128, nb=128, pb=128, tri=128, la=128, l2=128, zz=144, sel=16,
                          ccol=144, gcol=128, kcol=128, ncol=16, tma=128, tmb=128, rows=1024,
                          kr=128, one=128, crow=E, rmin=128, rmax=EL // GP, dmask=C, offd=C, offm=C, dgm=C)),
        ("float16", dict(ph=RO * R, k16=5 * E, ih=128, boh=128)),
        ("int32", dict(kraw=K0 + W, nraw=R, pi=8)), ("uint16", dict(pu=RO * R, pv=RO * R, po=RO * R, pq=RO * R))):
    for _n, _w in _l.items():
        SCRATCH[_n] = ("sbuf", [128, _w], _d)
for _t in range(RO):
    SCRATCH["yx%d" % _t] = ("sbuf", [128, 16 * R], "bfloat16")
for _j in range(NCH):
    for _n, _w, _d in (("vg", EL, "bfloat16"), ("mm", EL, "bfloat16"), ("kg", EL, "float16"), ("js", EL, "float16"),
                       ("ge", EL, "bfloat16"), ("sf", 7 * C, "float32"), ("m0", C, "bfloat16"), ("oh", 128, "bfloat16"),
                       ("sh", 4 * C + PAD, "float16"), ("sb", 7 * C, "bfloat16"), ("su", 48, "uint16")):
        SCRATCH["%s%d" % (_n, _j)] = ("sbuf", [128, _w], _d)
for _n in ["psy0", "psy1"] + ["ps%s%d" % (_a, _j) for _a in "xz" for _j in range(NCH)]:
    SCRATCH[_n] = ("psum", [128, 32, 16] if _n[2] == "z" else [128, 512], "float32")
SEMAPHORES = (["e_dve", "e_act", "e_pe", "e_pool", "sent", "d_nam", "d_seen", "d_yk"]
              + ["d_clk%d" % i for i in range(NKP)] + ["d_val%d" % i for i in range(NVP)] + ["d_yp%d" % j for j in range(NCH)]
              + ["a_%s%d_%d" % (a, t, j) for a, n in (("y", RO), ("p", RO + 1)) for t in range(1, n) for j in range(NCH)])
A = AluOpType
F = ActivationFunctionType


def build_ops():
    ops = []
    cur = [-1, -1, 0]

    def op(eng, cost, fn, rd=(), wr=(), bank=None, sem=None, val=16, lat=0, after=None, slot=None):
        if slot is None:
            slot = cur[2]
            cur[2] += 1
        ops.append({"eng": eng, "cost": cost, "fn": fn, "rd": list(rd), "wr": list(wr), "bank": bank, "sem": sem,
                    "val": val, "lat": lat, "after": after, "tag": (cur[0], cur[1]), "slot": (cur[1], slot)})
        return len(ops) - 1

    def dve(cost, fn, rd, wr, bank=None):
        return op("dve", max(64, cost), fn, rd, wr, bank)

    def val(s, T):
        return s if isinstance(s, (int, float)) else s(T)

    def ts(out, in0, s1, s2, o0, o1, rd, wr, cost=64, bank=None):
        if o1 is None:
            return dve(cost, lambda g, T, X: g.vector.tensor_scalar(out(T), in0(T), val(s1, T), None, o0), rd, wr, bank)
        return dve(cost, lambda g, T, X: g.vector.tensor_scalar(out(T), in0(T), val(s1, T), val(s2, T), o0, o1), rd, wr, bank)

    def tt(out, a, b, o, rd, wr, cost, bank=None):
        return dve(cost, lambda g, T, X: g.vector.tensor_tensor(out(T), a(T), b(T), o), rd, wr, bank)

    def cp(out, a, rd, wr, cost):
        return dve(cost, lambda g, T, X: g.vector.tensor_copy(out(T), a(T)), rd, wr)

    def scan(out, d0, d1, init, o0, o1, rd, wr, cost, bank=None):
        return dve(cost, lambda g, T, X: g.vector.tensor_tensor_scan(out(T), d0(T), d1(T), init, o0, o1), rd, wr, bank)

    def red(out, a, o, rd, wr, bank):
        return dve(C, lambda g, T, X: g.vector.tensor_reduce(out(T), a(T), AxisListType.X, o), rd, wr, bank)

    def act(out, a, rd, wr, cost, bank=None, bias=0.0, scale=1.0, slot=None):
        return op("act", cost, lambda g, T, X: g.scalar.activation(out(T), a(T), F.Identity, bias=val(bias, T), scale=scale),
                  rd, wr, bank, slot=slot)

    def mms(lst, rd, wr, bank, start=True, stop=True, solo=False):
        def fn(g, T, X):
            ins = None
            for i, (o, l, r, n) in enumerate(lst):
                ins = g.tensor.matmul(o(T), l(T), r(T), solo or (start and i == 0), solo or (stop and i == len(lst) - 1))
            return ins
        return op("pe", PEF * sum(m[3] for m in lst), fn, rd, wr, bank)

    def mset(a, v, wr, cost=64, bank=None):
        dve(cost, lambda g, T, X: g.vector.memset(a(T), v), [], wr, bank)

    def ap(name, a=None, b=None, s=None, p=128, p0=0):
        return lambda T: T[name][p0:p0 + p, a:b:s]

    def rev(a):
        return lambda T: a(T)[:, ::-1]

    def ind(win, a, b, off):
        return lambda T: T[win][:, a:b].indirect(off(T))

    def dma(q, out, in_, rd, wr, sem, lat):
        op(q, 60, lambda g, T, X: (g.sync if q == "sp" else g.scalar).dma_start(out(T), in_(T)), rd, wr, sem=sem, lat=lat)

    def send(de, so, hop, sem, rd, land, lat, after=None, slot=None):
        def fn(g, T, X):
            rid, pid, msk = X["dst"](hop, 0)
            if len(so) == 1:
                return g.remote_dma(de(T), so[0](T), T.sem[sem], T.sem.sent, pid, rid, msk)
            return g.remote_dma_fused([RemoteDMATransfer(dst_ids=[DstId(rid=rid, pnc=pid)], dma_engine_mask=msk, remote_sem=T.sem[sem],
                                                         srcs=[s(T) for s in so], dsts=[de(T)], alu_op=2)], local_sem=T.sem.sent)
        s = op("pool", 600, fn, rd, [], sem="sent", after=after, slot=slot)
        op("net", 0, None, [], [land], sem=sem, val=16, after=s, lat=lat, slot=slot and slot + "n")
        return s

    dma("sp", ap("nraw"), ap("nam"), [], ["nraw"], "d_nam", 2400)
    dma("act", ap("yy"), ap("seen"), [], ["yy"], "d_seen", 2400)
    vp = W // NVP
    for i in range(NVP):
        dma(("sp", "act")[i % 2], ap("vw", i * vp, (i + 1) * vp), ap("val", i * vp, (i + 1) * vp), [], ["vw%d" % i], "d_val%d" % i,
            3000 + 500 * i)
    for i in range(NKP):
        dma("sp", ap("kraw", K0 + KCUT[i], K0 + KCUT[i + 1]), ap("clk", *KCUT[i:i + 2]), [], ["kraw%d" % i], "d_clk%d" % i, 4500 + 2 * KCUT[i + 1])

    def iota(name, n, pat, base=0):
        op("pool", 160 + 2 * n, lambda g, T, X: g.iota(T[name][:, 0:n], pat, base, 0, allow_small_or_imprecise_dtypes=True), [], [name])
    op("pool", 162, lambda g, T, X: g.iota(T.pi[:, 0:1], [[0, 1]], 0, 1), [], ["pi"])
    iota("ccol", 144, [[1, 144]])
    iota("kcol", 128, [[0, 8], [1, 16]])
    iota("gcol", 128, [[1, 8], [0, 16]])
    iota("ncol", 16, [[16, 16]])
    M_ = float(MID)
    mset(ap("rmin"), 0.0, ["rmin"])
    mset(ap("rmax"), 0.0, ["rmax"], EL // GP // 2)
    mset(ap("rdum"), -4096.0, ["rdum"], R)
    mset(ap("kw", 0, K0), -M_, ["kwlo"], K0)
    mset(ap("kw", K0 + W, KW), 0.0, ["kwhi"], R)
    mset(ap("one", p=1), 1.0, ["one"])
    mset(ap("crow", p=1), 8 * M_, ["crow"], E // 2)
    mset(ap("rmin", 0, 128, 16), 262144.0, ["rmin"])
    mset(ap("rmax", 0, EL // GP, 16), -BIG, ["rmax"])
    mset(ap("kraw", 0, K0), 0, ["kpad"], K0)
    for j in range(NCH):
        mset(ap("sh%d" % j, 3 * C, 3 * C + PAD), -4096.0, ["fpad%d" % j])
    rows = lambda i, s=1, a=0: ap("rows", 128 * i + a, 128 * (i + 1), s, p=1)
    for i, v in enumerate((-99328.0, M_, 30720.0, -99328.0, M_, 30720.0, -123904.0, 32256.0)):
        mset(rows(i), v, ["rows%d" % i])
    for i, a, v in ((0, 0, -74752.0), (0, 1, -74752.0), (1, 0, M_ + W), (2, 0, 30720.0 + W), (2, 1, 30720.0 - W),
                    (6, 0, -99328.0), (6, 1, -99328.0), (7, 0, 32256.0 + W), (7, 1, 32256.0 - W)):
        mset(rows(i, 16, a), v, ["rows%d" % i])
    ROWS = ["rows%d" % i for i in range(8)]
    pi = lambda i: ap("pi", i, i + 1)
    pc = lambda i: ap("pc", i, i + 1)
    ts(pi(1), pi(0), 4, None, A.arith_shift_right, None, ["pi"], ["pi1"])
    ts(pi(2), pi(0), 15, None, A.bitwise_and, None, ["pi"], ["pi2"])
    ts(pi(5), pi(0), 1.0, None, A.add, None, ["pi"], ["pi5"])
    ts(pi(3), pi(5), 15, None, A.bitwise_and, None, ["pi5"], ["pi3"])
    cp(ap("pc", 0, 4), ap("pi", 0, 4), ["pi", "pi1", "pi2", "pi3"], ["pc"], 64)
    P_, G_, K_, S_ = pc(0), pc(1), pc(2), pc(3)
    EQm = (A.is_equal, A.mult)
    ts(pc(8), K_, 0.0, float(W), *EQm, ["pc"], ["pc8"])
    ts(ap("pv", 0, R), ap("nraw"), pc(8), None, A.add, None, ["nraw", "pc8"], ["pv0_%d" % j for j in range(NCH)], R)
    for i in range(NVP):
        ts(ap("vw", W + i * vp, W + (i + 1) * vp), ap("vw", i * vp, (i + 1) * vp), -256.0, None, A.add, None,
           ["vw%d" % i], ["vx%d" % i], vp // 2)
    VWK = ["v%s%d" % (a, i) for a in "wx" for i in range(NVP)]
    for q in range(16):
        dst = ap("yx0", q, 16 * R, 16)
        if q < YA:
            act(dst, ap("yy"), ["yy"], ["yx_%d" % q], 60 + R, bias=0.0 if q else -256.0)
        else:
            cp(dst, ap("yy"), ["yy"], ["yx_%d" % q], R // 2)
    YX0 = ["yx_%d" % q for q in range(16)]
    cp(ap("pu", 0, R), ap("nraw"), ["nraw"], ["pu0_%d" % j for j in range(NCH)], R)
    ts(ap("ph", 0, R), ap("nraw"), -M_, None, A.add, None, ["nraw"], ["ph0_%d" % j for j in range(NCH)], R)
    ts(pc(9), pc(8), -1.0, -M_, A.mult, A.add, ["pc8"], ["pc9"])
    ts(pc(11), pc(8), -16384.0, None, A.add, None, ["pc8"], ["pc11"])
    ts(pc(10), pc(11), M_, None, A.add, None, ["pc11"], ["pc10"])
    ts(pc(6), G_, 16.0, 15.0, A.mult, A.add, ["pc"], ["pc6"])
    for i, v in enumerate((16.0, -32.0)):
        ts(ap("sel", 8 * i, 8 * i + 8), ap("ccol", 0, 8), G_, v, *EQm, ["ccol", "pc"], ["sel%d" % i])
    ts(ap("kr", p=1), ap("kcol", p=1), 0.0, 65536.0, A.not_equal, A.mult, ["kcol"], ["kr"])
    for name in ("ib", "ih", "i32"):
        ts(ap(name), ap("ccol", 0, 128), P_, None, A.is_equal, None, ["ccol", "pc"], [name], 128 if name == "i32" else 64)
    for name, v in (("boh", 1.0), ("nb", -BIG), ("pb", BIG)):
        ts(ap(name), ap("gcol"), G_, v, *EQm, ["gcol", "pc"], [name])
    kc = ["kcol", "pc"]
    ts(ap("offd"), ap("kcol", 0, C), K_, BIG, A.not_equal, A.mult, kc, ["offd"])
    ts(ap("rdum", 0, R, 16), ap("ncol", 0, R // 16), K_, float(W - MID), A.add, A.add, ["ncol", "pc"], ["rdum"])
    ts(ap("zz"), ap("ccol"), pc(6), 0.25, *EQm, ["ccol", "pc6"], ["zz"], 72)
    ts(ap("offm"), ap("offd"), M_, None, A.max, None, ["offd"], ["offm"])
    ts(ap("dmask"), ap("kcol", 0, C), K_, 30720.0 + M_ + K0, *EQm, kc, ["dmask"])
    ts(ap("dgm"), ap("offd"), -1.0, 4096.0, A.mult, A.add, ["offd"], ["dgm"])
    def select(out, in_, how, fill):
        op("pool", 460, lambda g, T, X: g.affine_select(T[out][:], T[in_][:], [[1, 128]], how, fill, 0, -1), [in_], [out])
    ts(pc(7), G_, 16.0, S_, A.mult, A.add, ["pc"], ["pc7"])
    ts(ap("l2"), ap("ccol", 0, 128), pc(7), None, A.is_equal, None, ["ccol", "pc7"], ["l2"])
    ts(ap("tmb"), ap("ccol", 0, 128), pc(7), -8.0, *EQm, ["ccol", "pc7"], ["tmb"])
    select("la", "tmb", A.not_equal, -8.0)
    select("tma", "nb", A.is_gt, 0.0)
    select("tri", "tma", A.not_equal, BIG)
    for i in range(NKP):
        part = lambda s: ap(s, K0 + KCUT[i], K0 + KCUT[i + 1])
        ops[act(part("kw"), part("kraw"), ["kraw%d" % i], ["kwi%d" % i], 60 + KCUT[i + 1] - KCUT[i], bias=-M_)]["key"] = PERIOD + i
    KRAW = ["kraw%d" % i for i in range(NKP)] + ["kpad"]
    KWK = ["kw", "kwlo", "kwhi"] + ["kwi%d" % i for i in range(NKP)]

    def send_y(t, j, rd, after):
        n0 = R - C * (j + 1)
        part = lambda s: ap(s, 16 * n0, 16 * (n0 + C))
        send(part("yx%d" % t), [part("yx0")], HOP * t, "a_y%d_%d" % (t, j), YX0 + rd, "y%d_%d" % (t, j), 3500, after, "y")
    for j in range(NCH):
        send_y(1, j, ["kraw%d" % (NKP - 1)], None)

    cq = C // GP
    ep = EL // GP
    for t in range(RO):
        for j in range(NCH):
            cur[0], cur[1], cur[2] = t, j, 0
            n0 = R - C * (j + 1)
            c0 = t * R + n0
            k = lambda s, j=j: "%s%d" % (s, j)
            pcs = lambda s: [s + "_%d" % i for i in range(GP)]
            vg, mm_, kg, js, ge = k("vg"), k("mm"), k("kg"), k("js"), k("ge")
            sf, sh, sb, su, px, pz = k("sf"), k("sh"), k("sb"), k("su"), k("psx"), k("psz")
            pu, pv, ph = ("p%s%d_%d" % (a, t, j) for a in "uvh")
            yk = ["y%d_%d" % (t, j)] if t else YX0
            PC = ap("ph", c0, c0 + C)
            S0, S1, S2, U1, U2s = (ap(sf, i * C, (i + 1) * C) for i in range(2, 7))
            last = lambda i, sf=sf: ap(sf, i * C + 15, (i + 1) * C, 16)
            XX, YY, KO = (ap(sh, i * C, (i + 1) * C) for i in range(3))
            held = lambda d, sh=sh: ap(sh, 3 * C + PAD - d, 4 * C + PAD - d)
            NE, OVER, HH = (ap(sb, i * C, (i + 1) * C) for i in range(3))
            EQ = [ap(sb, i * C, (i + 1) * C) for i in range(3, 3 + NB // NSC)]
            OHT, CNT, BB, CC = (ap(px, i * C, (i + 1) * C) for i in range(4, 8))
            O3, RR, B1, U2 = ((lambda T, i=i, pz=pz: T[pz][:, NB * i:NB * (i + 1), :]) for i in range(4))
            end = t == RO - 1
            kp_, kw_ = C * GH, 128 // GH
            KEY, RF, FF, OH = (ap(s, a, a + kw_, p=kp_) for s, a in ((px, 0), (px, 128), (sf, 0), (k("oh"), 0)))
            pc_ = lambda s, i: ap(s, i * ep, (i + 1) * ep)
            off = lambda i, s="pu": ap(s, c0 + i * cq, c0 + (i + 1) * cq)
            JJ = ap(js, 15, EL, 16)

            if t > 0:
                act(PC, ap("pv", c0, c0 + C), [pv, "pc9"], [ph], 60 + C, bias=pc(9), slot="cvt")
                ops[ts(ap("pu", c0, c0 + C), ap("pv", c0, c0 + C), pc(8), None, A.subtract, None, [pv, "pc8"], [pu])]["slot"] = (j, "cvu")
                cur[2] = 0
            for i in range(GP):
                act(pc_(vg, i), ind("vw", 0, 2 * W, off(i, "pv")), [pv] + VWK, [vg + "_%d" % i], 80 + GAM * ep)
            row = lambda s: [(KEY, ap("one", 0, kp_, p=1), ap(s, 0, kw_, p=1), kw_)]
            mms(row("kcol"), ["one", "kcol"], [k("key")], px, True, False)
            yx = lambda a, b, s=1: ap("yx%d" % t, 16 * n0 + a, 16 * n0 + b, s)
            ng = 8 // GH
            for i in range(GP):
                a, b = i * ep, (i + 1) * ep
                m0 = ap(k("m0"), i * cq, (i + 1) * cq)
                sums = lambda src, s0: [(ap(px, q, kw_, 16, cq, C * h + cq * i), src(q), ap("sel", s0 + ng * h, s0 + ng * (h + 1)), cq)
                                        for h in range(GH) for q in range(16)]
                mms(sums(lambda q: ap(vg, a + q, b, 16), 0), [vg + "_%d" % i, "sel0"], [k("key")], px, False, False)
                tt(m0, ap(vg, a, b, 16), yx(a, b, 16), A.min, [vg + "_%d" % i] + yk, [k("m0") + "_%d" % i], 2 * cq)
                scan(pc_(mm_, i), yx(a, b), pc_(vg, i), 0.0, A.max, A.min, [vg + "_%d" % i] + yk, [mm_ + "_%d" % i], ep // 2)
                mms(sums(lambda q: ap(mm_, a + q, b, 16) if q else m0, 8) + (row("kr") if i == GP - 1 else []),
                    [mm_ + "_%d" % i, k("m0") + "_%d" % i, "sel1", "kr"], [k("key")], px, False, i == GP - 1)
            rst = ap("rmin", 0, kw_, p=kp_)
            scan(FF, rst, KEY, 0.0, A.add, A.min, [k("key"), "rmin"], [k("ff")], kw_, px)
            scan(rev(RF), rst, rev(KEY), 0.0, A.add, A.min, [k("key"), "rmin"], [k("rf")], kw_, px)
            tt(OH, RF, FF, A.is_equal, [k("ff"), k("rf")], [k("oh")], kw_, px)
            mms([(RR, ap("ib"), ap("offm"), C)], ["ib", "offm"], [k("rr")], pz, True, False)
            mms([(ap(px, 4 * C, 5 * C, 1, kw_, kw_ * h), OH, ap("ib", C * h, C * (h + 1), p=kp_), C) for h in range(GH)],
                [k("oh"), "ib"], [k("oht")], px, solo=True)
            tt(XX, OHT, PC, A.mult, [k("oht"), ph], [k("xx")], C, px)
            act(HH, OHT, [k("oht"), "pc10"], [k("hh")], 60 + C, px, bias=M_ - 16384.0 if end else pc(10 if t else 11), scale=16384.0)
            mms([(RR, ap("boh"), XX, C)], [k("xx"), "boh"], [k("rr")], pz, False)
            rd_ = ap("rdum", n0, n0 + C)
            red(ap(su, 0, NB), RR, A.min, [k("rr")], [k("ob")], pz)
            mms([(O3, ap("boh"), XX, C)], [k("xx"), "boh"], [k("o3")], pz)
            tt(NE, O3, PC, A.not_equal, [k("o3"), ph], [k("ne")], C, pz)
            lift = lambda o, i: (o, rows(((6, 1, 7), (0, 1, 2), (0, 1, 2), (3, 4, 5))[t][i]), ap("one", 0, C, p=1), C)
            mms([(B1, ap("ib"), ap("dmask"), C), (U2, ap("l2"), HH, C), lift(U2, 2)], ["ib", "dmask", k("hh"), "l2", "one"] + ROWS,
                [k("b1")], pz, True, False)
            if t > 0:
                for i in range(GP):
                    act(pc_(kg, i), ind("kw", K0, KW, off(i)), [pu] + KWK, [kg + "_%d" % i], 80 + GAM * ep)
                cp(KO, ind("kw", K0, KW, ap(su, 0, NB)), [k("ob")] + KWK, [k("ko")], 60 + GAM * C)
            else:
                for i in range(GP):
                    if j == 0 and i == GP - 1:
                        ts(pc_(kg, i), ind("kraw", K0, K0 + W, off(i)), -M_, None, A.add, None, [pu] + KRAW, [kg + "_%d" % i], 60 + GAM * ep)
                    else:
                        act(pc_(kg, i), ind("kraw", K0, K0 + W, off(i)), [pu] + KRAW, [kg + "_%d" % i], 80 + GAM * ep, bias=-M_)
                ts(KO, ind("kraw", K0, K0 + W, ap(su, 0, NB)), -M_, None, A.add, None, [k("ob")] + KRAW, [k("ko")], 60 + GAM * C)
            ej = EL // JP
            for i in range(JP):
                scan(ap(js, i * ej, (i + 1) * ej), ap("rmax", 0, ej), ap(kg, i * ej, (i + 1) * ej), 0.0, A.add, A.max,
                     [kg + "_%d" % (i * GP // JP), "rmax"], [js + "_%d" % i], ej // 2)
            b = "psy%d" % ((t * NCH + j) % 2)
            GG, UA, UJ = (ap(b, i * C, (i + 1) * C) for i in range(3))
            mms([(ap(b, q, NBC * C, NBC), ap("ih"), KO, C) for q in range(NBC)], [k("ko"), "ih"], [b], b)
            NP = 16 // NBC
            cg = C // GEP
            passes = [(i, r) for i in range(GEP) for r in range(NP)]
            for i, r in passes:
                cols = lambda s: ap(s, 16 * cg * i + r, 16 * cg * (i + 1), NP)
                tt(cols(ge), cols(kg), ap(b, NBC * cg * i, NBC * cg * (i + 1)), A.is_lt, (pcs(kg) if GEP == 1 else [kg + "_%d" % i]) + [b],
                   [ge + "_%d_%d" % (i, r)], NBC * cg, b)
            for i, r in passes:
                mms([(ap(px, 5 * C + cg * i, 5 * C + cg * (i + 1)), ap("zz", 15 - q, 143 - q), ap(ge, 16 * cg * i + q, 16 * cg * (i + 1), 16), C)
                     for q in range(r, 16, NP)], [ge + "_%d_%d" % (i, r), "zz"], [k("cnt")], px, (i, r) == passes[0], (i, r) == passes[-1])
            mms([(GG, ap("ih"), PC, C), (UA, ap("la"), HH, C), lift(UA, 0), lift(UJ, 1), (UJ, ap("ih"), JJ, C)],
                [ph, "ih", k("hh"), "la", "one"] + [js + "_%d" % i for i in range(JP)] + ROWS, [b], b, True, False)
            tt(OVER, CNT, NE, A.is_lt, [k("cnt"), k("ne")], [k("over")], C, px)
            ov = k("over")
            own = lambda o: [(o, ap("ib"), ap("offd"), C), (o, ap("boh"), XX, C), (o, ap("pb"), OVER, C)]
            ownk = [ov, k("xx"), "ib", "offd", "boh", "pb"]
            mms([(GG, ap("tri"), OVER, C), (UA, ap("nb"), OVER, C), (UJ, ap("nb"), OVER, C)], [ov, "tri", "nb"], [b], b, False)
            mms(own(BB), ownk, [k("bb")], px)
            ts(YY, GG, -BIG, -2048.0, A.add, A.max, [b], [k("yy_")], C, b)
            mms([(B1, ap("boh"), YY, C), (U2, ap("boh"), YY, C)], [k("yy_"), "boh"], [k("b1")], pz, False)
            scan(held(0), ap("dgm"), BB, -4096.0, A.max, A.min, [k("bb"), "dgm"], [k("fd")], C, px)
            tt(U1, UA, ap("pu" if end else "pv", c0, c0 + C), A.min, [b, pu, pv], [k("u1")], C, b)
            tt(U2s, UJ, U1, A.max, [b, k("u1")], [k("u2s")], C, b)
            mms(own(CC), ownk, [k("cc")], px, True, False)
            red(ap(su, 16, 16 + NB), B1, A.max, [k("b1")], [k("pfo")], pz)
            for i, e in enumerate(EQ):
                tt(e, O3, held(16 * i + 1), A.is_equal, [k("o3"), k("fd"), k("fpad")], [k("eq") + "_%d" % i], C, pz)
            so = [ap(s + "f", n0, n0 + C) if end else ap(s, c0, c0 + C) for s in ("po", "pq")]
            sk = ["p%s%d_%d" % (s, t, j) for s in "oq"]
            de = ap("pl", n0, n0 + C) if end else ap("pv", c0 + R, c0 + R + C)
            tt(so[0], U2, U2s, A.max, [k("b1"), k("u2s")], sk[:1], C, pz)
            tt(so[1], ind("kw" if t else "kraw", 0, K0 + W, ap(su, 16, 16 + NB)), HH, A.add, [k("pfo"), k("hh")] + (KWK if t else KRAW),
               sk[1:], 60 + GAM * C)
            land = "pv%d_%d" % (t + 1, j)
            s = send(de, so, -HOP * t if end else HOP, "a_p%d_%d" % (t + 1, j), sk, land, LAT - 600)
            if t + 2 < RO:
                send_y(t + 2, j, [], s)
            mms([(CC, ap("pb"), e, C) for e in EQ], [k("eq") + "_%d" % i for i in range(len(EQ))] + ["pb"], [k("cc")], px, False)
            scan(S2, rd_, CC, -4096.0, A.max, A.min, [k("cc"), "rdum"], [k("s2")], C, px)
            ts(ap(su, 32, 32 + NB), last(4), M_, None, A.add, None, [k("s2")], [k("tg")])
            if t == RO - 1:
                cur[0] = RO
                dma("sp", ap("yp", n0, n0 + C), de, [land], [], k("d_yp"), 2400)
        cur[0], cur[1], cur[2] = t, NCH, 0
        nb_, ne = NB // NSC, EL // NSC
        for j in range(NCH):
            for h in reversed(range(NSC)):
                cp(ind("kw", K0, KW, ap("su%d" % j, 32 + h * nb_, 32 + (h + 1) * nb_)), ap("js%d" % j, h * ne + 15, (h + 1) * ne, 16),
                   ["tg%d" % j] + ["js%d_%d" % (j, i) for i in range(JP)] + KWK[1:], ["kw"], 60 + SCA * C / NSC)

    cur[0], cur[1] = RO, 0
    blk = lambda b: ap("kw", K0 + b * E, K0 + (b + 1) * E)
    ps = ap("psy0", 0, E)
    mms([(ps, ap("one", p=1), ap("crow", p=1), E)], ["one", "crow"], ["psy0"], "psy0", True, False)
    mms([(ps, ap("i32"), blk(4), 4 * E)], KWK + ["i32"], ["psy0"], "psy0", False, False)
    for b in range(4):
        dst = ap("k16", b * E, (b + 1) * E)
        if b > 0:
            act(dst, blk(b), KWK, ["k16_%d" % b], 60 + E)
        else:
            cp(dst, blk(b), KWK, ["k16_%d" % b], E)
        mms([(ps, ap("ih"), dst, E)], ["k16_%d" % b, "ih"], ["psy0"], "psy0", False, b == 3)
    tt(ap("psy1", 0, E), blk(5), blk(6), A.add, KWK, ["psy1"], 2 * E, "psy1")
    tt(ap("fs"), ap("psy1", 0, E), blk(7), A.add, KWK + ["psy1"], ["fs"], E, "psy1")
    tt(ap("fold"), ps, ap("fs"), A.add, ["psy0", "fs"], ["fold"], E, "psy0")
    dma("sp", ap("yk"), ap("fold"), ["fold"], [], "d_yk", 2400)
    return ops


def search(ops, justify, span, pred):
    n = len(ops)
    rng = np.random.default_rng(SEED)
    es = [0.0] * n
    slots = {}
    for x in range(n):
        es[x] = max([es[d] + ops[d]["cost"] + g for d, g in pred[x] if ops[d]["tag"] == ops[x]["tag"]] + [0.0])
        if ops[x]["tag"][0] == 1:
            slots[ops[x]["slot"]] = len(slots)
    off = np.zeros(len(slots))
    for x in range(n):
        t, j = ops[x]["tag"]
        if t == 1:
            off[slots[ops[x]["slot"]]] = es[x] + (j * STAG if j < NCH else NCH * STAG + 8000)

    def keys(off):
        return [(o.get("key", -1e6 + x) if o["tag"][0] < 0 else 1e6 + x if o["tag"][0] >= RO else o["tag"][0] * PERIOD + float(off[slots[o["slot"]]]))
                for x, o in enumerate(ops)]
    best = justify(keys(off))
    bs = cs = span(best)
    for it in range(TRIES):
        o2 = off.copy()
        m = rng.integers(4)
        a = rng.integers(0, len(o2))
        if m == 0:
            o2 += rng.normal(0, 150, len(o2))
        elif m == 1:
            o2[rng.integers(0, len(o2), 3)] += rng.normal(0, 1500, 3)
        else:
            o2[a:a + rng.integers(1, 30 * (m - 1))] += rng.normal(0, 1500 if m == 2 else 400)
        st = justify(keys(o2))
        s = span(st)
        if s <= cs + 150 * (1 - it / TRIES) * rng.exponential():
            off, cs = o2, s
        if s < bs:
            best, bs = st, s
    return best


def shake(start, justify, span, seed):
    rng = np.random.default_rng(seed)
    cur = best = start
    cs = bs = span(start)
    for it in range(SHAKES):
        a = rng.random() * cs
        b = a + (1500, 4000, 16000)[rng.integers(3)]
        now = np.array(cur)
        move = rng.normal(0, (150, 500, 1500)[rng.integers(3)], len(cur)) * ((now >= a) & (now < b) & (rng.random(len(cur)) < 0.3))
        st = justify((now + move).tolist())
        s = span(st)
        if s <= cs + 60 * rng.exponential():
            cur, cs = st, s
        if s < bs:
            best, bs = st, s
    return best


def improve(start, eng, cost, tail, pred, nxt, seed):
    n = len(start)
    rng = np.random.default_rng(seed)
    seq = sorted(range(n), key=lambda y: (start[y], y))
    before, after, lastq = [-1] * n, [-1] * n, {}
    for x in seq:
        if eng[x] != "net":
            before[x] = lastq.get(eng[x], -1)
            if before[x] >= 0:
                after[before[x]] = x
            lastq[eng[x]] = x
    direct = [set(d for d, g in pred[x]) for x in range(n)]
    head, rdy, rest, dep = [0.0] * n, [0.0] * n, [0.0] * n, [0.0] * n
    tabu, best, bs = {}, None, 1e18
    for it in range(SWAPS):
        for x in seq:
            t = 0.0
            for d, g in pred[x]:
                if head[d] + cost[d] + g > t:
                    t = head[d] + cost[d] + g
            rdy[x] = t
            p = before[x]
            head[x] = head[p] + cost[p] if p >= 0 and head[p] + cost[p] > t else t
        for x in reversed(seq):
            t = tail[x]
            for s, g in nxt[x]:
                if rest[s] + g > t:
                    t = rest[s] + g
            dep[x] = t
            s = after[x]
            rest[x] = cost[x] + (rest[s] if s >= 0 and rest[s] > t else t)
        span = max(head[x] + rest[x] for x in seq) - 1e-6
        if span < bs:
            best, bs = list(head), span
        pick, pv = None, 1e18
        for u in seq:
            v = after[u]
            if (v < 0 or head[u] + rest[u] < span or head[v] + rest[v] < span or head[v] > head[u] + cost[u] + 1e-6
                    or u in direct[v]):
                continue
            p, s = before[u], after[v]
            hv = max(rdy[v], head[p] + cost[p] if p >= 0 else 0.0)
            ru = cost[u] + max(dep[u], rest[s] if s >= 0 else 0.0)
            est = max(hv + cost[v] + max(dep[v], ru), max(rdy[u], hv + cost[v]) + ru) + 40.0 * rng.random()
            if tabu.get((v, u), -1) > it and est >= bs:
                est += 1e6
            if est < pv:
                pick, pv = (u, v), est
        if pick is None:
            break
        u, v = pick
        tabu[(u, v)] = it + 8 + int(rng.integers(12))
        p, s = before[u], after[v]
        before[v], after[v], before[u], after[u] = p, u, v, s
        if p >= 0:
            after[p] = v
        if s >= 0:
            before[s] = u
        a, b = seq.index(u), seq.index(v)
        late = {u}
        for x in seq[a + 1:b]:
            if before[x] in late or not late.isdisjoint(direct[x]):
                late.add(x)
        mid = seq[a:b + 1]
        seq[a:b + 1] = [x for x in mid if x not in late] + [x for x in mid if x in late]
    return best


def plan_program():
    ops = build_ops()
    n = len(ops)
    lastw, readers, runs, lastb = {}, {}, {}, {}
    for x, o in enumerate(ops):
        deps = set(lastw[r] for r in o["rd"] + o["wr"] if r in lastw)
        for w in o["wr"]:
            deps.update(readers.get(w, []))
        b = o["bank"]
        if b is not None:
            rn = runs.setdefault(b, {})
            for e, lst in rn.items():
                if e != o["eng"]:
                    deps.update(lst)
                elif e == "pe":
                    deps.add(lst[-1])
            if lastb.get(b) == o["eng"]:
                rn[o["eng"]].append(x)
            else:
                rn[o["eng"]] = [x]
            lastb[b] = o["eng"]
        for r in o["rd"]:
            readers.setdefault(r, []).append(x)
        for w in o["wr"]:
            lastw[w] = x
            readers[w] = []
        deps.discard(x)
        o["wait"] = set(d for d in deps if not (o["eng"] == "pe" and ops[d]["eng"] == "pe"))
        o["sd"] = set(deps)
        if o["after"] is not None:
            o["sd"].add(o["after"])
    cost = [o["cost"] for o in ops]
    eng = [o["eng"] for o in ops]
    tail = [ops[x]["lat"] if eng[x] != "net" else 0 for x in range(n)]

    def gap(d, x):
        if eng[x] == "net":
            return ops[x]["lat"]
        return tail[d] + (0 if d not in ops[x]["wait"] else HOPS if eng[d] == eng[x] else HOPX)
    pred = [[(d, gap(d, x)) for d in sorted(ops[x]["sd"])] for x in range(n)]
    nxt = [[] for x in range(n)]
    for x in range(n):
        for d, gp in pred[x]:
            nxt[d].append((x, gp))

    def place(key, before, head, serial):
        key = list(key)
        for x in serial:
            for d, gp in before[x]:
                if key[d] >= key[x]:
                    key[x] = key[d] + 1e-3
        start = [0.0] * n
        busy = {e: [] for e in eng}
        for x in sorted(serial, key=lambda y: key[y]):
            t = head[x]
            for d, gp in before[x]:
                if start[d] + cost[d] + gp > t:
                    t = start[d] + cost[d] + gp
            if eng[x] != "net":
                lst = busy[eng[x]]
                i = len(lst)
                while i > 0 and lst[i - 1][1] > t:
                    i -= 1
                while i < len(lst) and lst[i][0] < t + cost[x]:
                    t = max(t, lst[i][1])
                    i += 1
                lst.insert(i, (t, t + cost[x]))
            start[x] = t
        return start
    zero, fw = [0.0] * n, list(range(n))

    def span(st):
        return max(st[x] + cost[x] + tail[x] for x in fw)

    def justify(key):
        st = place(key, pred, zero, fw)
        bk = place([-(st[x] + cost[x]) for x in fw], nxt, tail, fw[::-1])
        st2 = place([-(bk[x] + cost[x]) for x in fw], pred, zero, fw)
        return st2 if span(st2) <= span(st) else st
    best = search(ops, justify, span, pred)
    for i in range(PASSES):
        best = justify(improve(shake(best, justify, span, i), eng, cost, tail, pred, nxt, i))
    order, pos = {}, {}
    seq = sorted(range(n), key=lambda y: (best[y], y))
    for x in seq:
        ops[x]["t"] = best[x]
        pos[x] = len(order.setdefault(eng[x], []))
        order[eng[x]].append(x)
    known = {e: {} for e in order}
    for x in seq:
        o = ops[x]
        kn = known[o["eng"]]
        need = {}
        for d in sorted(o["wait"]):
            if ops[d]["sem"] is not None:
                need[("s", d)] = (0, d)
            elif pos[d] > need.get(eng[d], (-1, 0))[0]:
                need[eng[d]] = (pos[d], d)
        o["waits"] = []
        for key, (p, d) in sorted(need.items(), key=lambda kv: -best[kv[1][1]]):
            if kn.get(key, -1) >= p:
                continue
            o["waits"].append(d)
            ops[d]["inc"] = True
            kn[key] = p
            for k2, v2 in ops[d].get("kn", {}).items():
                if kn.get(k2, -1) < v2:
                    kn[k2] = v2
        o["kn"] = dict(kn) if o["eng"] != "net" else {}
    for e, lst in order.items():
        c = 0
        for x in lst:
            if ops[x]["sem"] is None and ops[x].get("inc"):
                c += 1
                ops[x]["cnt"] = c
    return ops, order, seq, span(best)


_PLAN = []


def rank_program(g, core, T, topo):
    rank = T.rank_of(core)
    if rank is None:
        return
    if not _PLAN:
        _PLAN.append(plan_program())
    ops, order = _PLAN[0][:2]
    cores = T.cores

    def dst(hop, part):
        to = cores[(rank + hop) % len(cores)]
        rid, pid, se = topo.addr(to)
        return rid, pid, topo.mask(core, to)
    X = {"dst": dst}
    queues = {"dve": g.vector, "act": g.scalar, "pe": g.tensor, "pool": g, "sp": g.sync}
    sent = 0
    for e in ("sp", "pool", "act", "pe", "dve"):
        q = queues[e]
        for x in order[e]:
            o = ops[x]
            for d in o["waits"]:
                p = ops[d]
                if p["sem"] is not None:
                    q.wait_ge(T.sem[p["sem"]], p["val"])
                else:
                    q.wait_ge(T.sem["e_" + p["eng"]], p["cnt"])
            ins = o["fn"](g, T, X)
            if o["sem"] == "sent":
                sent += 16
            elif o["sem"] is not None:
                ins.then_inc(T.sem[o["sem"]], 16)
            elif o.get("inc"):
                ins.then_inc(T.sem["e_" + e], 1)
    g.wait_ge(T.sem.sent, sent)
    for j in range(NCH):
        g.wait_ge(T.sem["d_yp%d" % j], 16)
    g.wait_ge(T.sem.d_yk, 16)
